import numpy as np
import ml_dtypes


def mxq(x, axis, fmt="e4m3"):
    dtype, down = {"e4m3": (ml_dtypes.float8_e4m3fn, 7), "e5m2": (ml_dtypes.float8_e5m2, 14)}[fmt]
    v = np.moveaxis(np.asarray(x, np.float32).astype(ml_dtypes.bfloat16).astype(np.float64), axis, -1)
    blocks = v.reshape(v.shape[:-1] + (-1, 32))
    amax = np.abs(blocks).max(-1, keepdims=True)
    byte = np.maximum(np.where(amax > 0, np.frexp(amax)[1] - 1 + 127, 0) - down, 1)
    scale = np.exp2(byte - 127.0)
    codes = (blocks / scale).astype(np.float32).astype(dtype).astype(np.float64)
    return np.moveaxis((codes * scale).reshape(v.shape), -1, axis)


WIDE = False


def mx_kscale(k):
    if not WIDE:
        return np.ones(k)
    levels = np.array([10, -10, 5, -5, 0])
    if k % 512:
        return np.exp2(np.random.permutation(np.resize(levels, k // 32))).repeat(32)
    a = np.empty((k // 512, 16))
    for p in range(k // 512):
        a[p, :8] = np.random.permutation(np.resize(levels, 8))
        for g in range(8):
            far = levels[np.abs(levels - a[p, g]) >= 10]
            a[p, g + 8] = far[np.random.randint(len(far))]
    return np.exp2(a.ravel()).repeat(32)


def f64(x):
    return np.asarray(x).astype(np.float64)


def striped(idx):
    return np.tile(idx.reshape(-1, 16).T, (8, 1)).astype(np.uint16)


def unstriped(offs):
    return offs[:16].T.reshape(-1).astype(np.int64)


E2M1 = np.array([0.0, 0.5, 1.0, 1.5, 2.0, 3.0, 4.0, 6.0, -0.0, -0.5, -1.0, -1.5, -2.0, -3.0, -4.0, -6.0])


def pack_weight(w, fmt):
    k, n = w.shape
    w = f64(np.asarray(w, np.float32).astype(ml_dtypes.bfloat16)).reshape(k // 32, 32, n)
    amax = np.abs(w).max(1)
    if fmt == "e4m3":
        byte = np.frexp(amax)[1] - 1 + 127 - 7
    else:
        mant, ex = np.frexp(amax / 6.0)
        byte = np.where(mant > 0.5, ex, ex - 1) + 127
    byte = np.clip(np.where(amax > 0, byte, 1), 1, 254)
    scaled = (w * np.exp2(127.0 - byte)[:, None, :]).reshape(k, n).astype(np.float32)
    by_word = np.ascontiguousarray(scaled.reshape(k // 512, 128, 4, n).transpose(0, 1, 3, 2))
    if fmt == "e4m3":
        words = by_word.astype(ml_dtypes.float8_e4m3fn).view(np.uint8)
    else:
        c = by_word.astype(ml_dtypes.float4_e2m1fn).view(np.uint8) & 0xF
        words = (c[..., 0::2] | (c[..., 1::2] << 4)).reshape(k // 512, 128, 2 * n)
    return np.ascontiguousarray(words), np.ascontiguousarray(byte.astype(np.uint8).reshape(k // 512, 16, n))


def unpack_weight(words, scales, fmt):
    g, _, n = scales.shape
    words = np.ascontiguousarray(words).reshape(g, 128, n, -1)
    if fmt == "e4m3":
        vals = words.view(ml_dtypes.float8_e4m3fn).astype(np.float64)
    else:
        nib = np.empty((g, 128, n, 4), np.uint8)
        nib[..., 0::2] = words & 0xF
        nib[..., 1::2] = words >> 4
        vals = E2M1[nib]
    vals = vals * np.repeat(np.exp2(scales.astype(np.float64) - 127.0), 8, axis=1)[..., None]
    return vals.transpose(0, 1, 3, 2).reshape(g * 512, n)


def gelu(v):
    return 0.5 * v * (1.0 + np.tanh(np.sqrt(2.0 / np.pi) * (v + 0.044715 * v**3)))


T, S, P, P2, K, H, N = 2048, 1024, 512, 256, 1024, 1024, 512

def setup_inputs():
    n = np.random.standard_normal
    s = mx_kscale(K)[:, None]
    u = mx_kscale(H)[:, None]
    tab_words, tab_scales = pack_weight(n((K, T)) * s, "e4m3")
    w2_words, w2_scales = pack_weight(n((H, N)) / np.sqrt(H) / u, "e2m1")
    return {
        "tab_words": tab_words, "tab_scales": tab_scales,
        "offs": striped(np.random.permutation(T)[:S]),
        "pos1": striped(np.random.permutation(S)[:P]),
        "pos2": striped(np.random.permutation(S)[:P]),
        "pos3": striped(np.random.permutation(P)[:P2]),
        "pos4": striped(np.random.permutation(P)[:P2]),
        "w1": (n((K, H)) / np.sqrt(K) / s).astype(np.float32),
        "w2_words": w2_words, "w2_scales": w2_scales,
        "w3": (n((H, N)) / np.sqrt(H) / u).astype(np.float32),
        "gz": (np.exp(0.3 * n(H)) * u[:, 0]).astype(np.float32),
        "gt": (np.exp(0.3 * n(H)) * u[:, 0]).astype(np.float32),
        "gd": np.exp(0.3 * n(N)).astype(np.float32),
    }

def reference(tab_words, tab_scales, offs, pos1, pos2, pos3, pos4, w1, w2_words, w2_scales, w3, gz, gt, gd):
    v = unpack_weight(tab_words, tab_scales, "e4m3")[:, unstriped(offs)]
    h = mxq(f64(w1), 0, "e4m3").T @ v
    f = h[:, unstriped(pos1)] * h[:, unstriped(pos2)]
    z = f64(gz)[:, None] * f
    x = f64(gt)[:, None] * np.tanh(f)
    w2 = unpack_weight(w2_words, w2_scales, "e2m1")
    y = w2.T @ mxq(z, 0, "e4m3") + mxq(f64(w3), 0, "e4m3").T @ mxq(x, 0, "e4m3")
    return y[:, unstriped(pos3)] - f64(gd)[:, None] * y[:, unstriped(pos4)]

@@ -1,0 +1,297 @@
+from contextlib import ExitStack
+
+import concourse.mybir as mybir
+
+T, S, PAIRS, TRIADS, K, H, N = 2048, 1024, 512, 256, 1024, 1024, 512
+FLOPS = 2 * K * H * S + 2 * 2 * H * N * PAIRS
+
+F32 = mybir.dt.float32
+BF16 = mybir.dt.bfloat16
+I32 = mybir.dt.int32
+U32 = mybir.dt.uint32
+U16 = mybir.dt.uint16
+U8 = mybir.dt.uint8
+FP8X4 = mybir.dt.float8_e4m3fn_x4
+FP4X4 = mybir.dt.float4_e2m1fn_x4
+ALU = mybir.AluOpType
+ACT = mybir.ActivationFunctionType
+
+P = 128
+PACK = 4
+PASS = P * PACK
+BANK = 512
+
+
+def tile_list_friend_triad_scores_kernel(
+    tc, tab_words, tab_scales, offs, pos1, pos2, pos3, pos4, w1, w2_words, w2_scales, w3, gz, gt, gd, out
+):
+    nc = tc.nc
+    with ExitStack() as ctx:
+        lists = ctx.enter_context(tc.tile_pool(name="lists", bufs=1))
+        keep = ctx.enter_context(tc.tile_pool(name="keep", bufs=1))
+        ring = ctx.enter_context(tc.tile_pool(name="ring", bufs=2))
+        psum = ctx.enter_context(tc.psum_pool(name="psum", bufs=1))
+
+        def load_list(src, name):
+            t = lists.tile([P, src.shape[1]], U16, name=name)
+            nc.sync.dma_start(t[:], src)
+            return t
+
+        def mx_tiles(name):
+            codes = keep.tile([P, BANK], U32, name=name + "_codes", align_bytes=64)
+            scales = keep.tile([P, BANK], U8, name=name + "_scales", align_bytes=64)
+            return codes, scales
+
+        def quantize(mx, grouped, c0, c1):
+            nc.vector.quantize_mx(
+                out=mx[0][:, c0:c1].bitcast(FP8X4), scales=mx[1][:, c0:c1], in_=grouped[:, PACK * c0 : PACK * c1]
+            )
+
+        tab_sc = keep.tile([P, T], U8, name="tab_sc", align_bytes=64)
+        nc.gpsimd.memset(tab_sc[:].bitcast(I32), 0)
+        warm = keep.tile([P, 8], F32, name="warm")
+        nc.gpsimd.memset(warm[:], 0.0)
+        warm2 = keep.tile([P, 8], F32, name="warm2")
+        nc.scalar.activation(warm2[:], warm[:], ACT.Tanh)
+        w2_sc = keep.tile([P, 2, N], U8, name="w2_sc", align_bytes=64)
+        nc.gpsimd.memset(w2_sc[:].rearrange("p a c -> p (a c)").bitcast(I32), 0)
+
+        idx = load_list(offs, "idx")
+        for q in range(4):
+            nc.sync.dma_start(
+                tab_sc[32 * q : 32 * q + 8, :].bitcast(I32), tab_scales[:, 4 * q : 4 * q + 4, :].bitcast(I32)
+            )
+
+        def load_w(src, a, c0, c1, name):
+            raw = keep.tile([P, PACK, c1 - c0], F32, name=name)
+            nc.sync.dma_start(raw[:], src[PASS * a : PASS * (a + 1), c0:c1].rearrange("(p j) c -> p j c", j=PACK))
+            return raw
+
+        w1_raw = {}
+        tab_w = []
+        for a in range(2):
+            t = keep.tile([P, T], I32, name="tab_w%d" % a, align_bytes=64)
+            nc.sync.dma_start(t[:], tab_words[a].rearrange("p t i -> p (t i)").bitcast(I32))
+            tab_w.append(t)
+            if a == 0:
+                w1_raw[0, 0, 0] = load_w(w1, 0, 0, 256, "w1raw00a")
+                w1_raw[0, 0, 1] = load_w(w1, 0, 256, 512, "w1raw00b")
+        w1_raw[0, 1, 0] = load_w(w1, 1, 0, 256, "w1raw01a")
+        w1_raw[0, 1, 1] = load_w(w1, 1, 256, 512, "w1raw01b")
+        p1 = load_list(pos1, "p1")
+        p2 = load_list(pos2, "p2")
+        w1_raw[1, 0, 0] = load_w(w1, 0, 512, 1024, "w1raw10")
+        w1_raw[1, 1, 0] = load_w(w1, 1, 512, 1024, "w1raw11")
+        w2_w = keep.tile([P, 2, 2 * N], U8, name="w2_w", align_bytes=64)
+        nc.sync.dma_start(w2_w[:].bitcast(I32), w2_words.rearrange("a p c -> p a c").bitcast(I32))
+        for q in range(4):
+            nc.sync.dma_start(
+                w2_sc[32 * q : 32 * q + 4, :, :].bitcast(I32),
+                w2_scales[:, 4 * q : 4 * q + 4, :].rearrange("a r c -> r a c").bitcast(I32),
+            )
+        w3_raw = [load_w(w3, a, 0, N, "w3raw%d" % a) for a in range(2)]
+        p3 = load_list(pos3, "p3")
+        p4 = load_list(pos4, "p4")
+
+        gz_sb = keep.tile([P, 2, PACK], F32, name="gz_sb")
+        gt_sb = keep.tile([P, 2, PACK], F32, name="gt_sb")
+        gd_sb = keep.tile([P, N // P], F32, name="gd_sb")
+        nc.gpsimd.dma_start(gz_sb[:], gz.rearrange("(b p t) -> p b t", p=P, t=PACK))
+        nc.gpsimd.dma_start(gt_sb[:], gt.rearrange("(b p t) -> p b t", p=P, t=PACK))
+        with nc.allow_non_contiguous_dma(reason="one weight a partition"):
+            nc.gpsimd.dma_start(gd_sb[:], gd.rearrange("(n p) -> p n", p=P))
+        gd_wide = keep.tile([P, N // P, TRIADS], F32, name="gd_wide")
+
+        got_sc = keep.tile([P, S], U8, name="got_sc", align_bytes=64)
+        nc.vector.tensor_copy(got_sc[:], tab_sc[:].indirect(idx[:]))
+
+        def cast_w1(eng, grouped, raw, m0, m1):
+            dst = grouped[:].rearrange("p (t m j) -> p m j t", t=PACK, j=PACK)[:, m0:m1]
+            src = raw[:].rearrange("p j (m t) -> p m j t", t=PACK)
+            if eng == "v":
+                nc.vector.tensor_copy(dst, src)
+            else:
+                nc.scalar.copy(dst, src)
+
+        w1_bf = {}
+        w1_mx = {}
+        for b in range(2):
+            for a in range(2):
+                w1_bf[b, a] = keep.tile([P, PACK * BANK], BF16, name="w1bf%d%d" % (b, a), align_bytes=64)
+                w1_mx[b, a] = mx_tiles("w1_%d%d" % (b, a))
+
+        cast_w1("s", w1_bf[0, 0], w1_raw[0, 0, 0], 0, 64)
+        got_w = []
+        for a in range(2):
+            g = keep.tile([P, S], U32, name="got_w%d" % a, align_bytes=64)
+            nc.vector.tensor_copy(g[:], tab_w[a][:].bitcast(U32).indirect(idx[:]))
+            got_w.append(g)
+            if a == 0:
+                cast_w1("v", w1_bf[0, 0], w1_raw[0, 0, 1], 64, 128)
+                quantize(w1_mx[0, 0], w1_bf[0, 0], 0, 512)
+        nc.scalar.copy(gd_wide[:], gd_sb[:].unsqueeze(2).to_broadcast([P, N // P, TRIADS]))
+        cast_w1("s", w1_bf[0, 1], w1_raw[0, 1, 0], 0, 64)
+        cast_w1("v", w1_bf[0, 1], w1_raw[0, 1, 1], 64, 128)
+        quantize(w1_mx[0, 1], w1_bf[0, 1], 0, 128)
+        quantize(w1_mx[0, 1], w1_bf[0, 1], 128, 256)
+        quantize(w1_mx[0, 1], w1_bf[0, 1], 256, 512)
+
+        def stage1(b, t):
+            h = ring.tile([P, S], F32, name="h", bufs=4)
+            for half in range(2):
+                acc = psum.tile([P, BANK], F32, name="hacc", bufs=4)
+                cols = slice(BANK * half, BANK * (half + 1))
+                rows = slice(P * t, P * (t + 1))
+                for a in range(2):
+                    nc.tensor.matmul_mx(
+                        out=acc[:],
+                        lhsT=w1_mx[b, a][0][:, rows].bitcast(FP8X4),
+                        lhsT_scale=w1_mx[b, a][1][:, rows],
+                        rhs=got_w[a][:, cols].bitcast(FP8X4),
+                        rhs_scale=got_sc[4 * a : P, cols],
+                        start=(a == 0),
+                        stop=(a == 1),
+                    )
+                if (b, t, half) == (0, 0, 1):
+                    nc.vector.tensor_copy(h[:, cols], acc[:])
+                else:
+                    nc.scalar.copy(h[:, cols], acc[:])
+            return h
+
+        f4 = [keep.tile([P, PACK, PAIRS], F32, name="f4_%d" % b) for b in range(2)]
+        th4 = [keep.tile([P, PACK, PAIRS], F32, name="th4_%d" % b) for b in range(2)]
+
+        def pair(b, t, h):
+            left = ring.tile([P, PAIRS], F32, name="left")
+            for u in range(2):
+                nc.vector.tensor_copy(left[:, 256 * u : 256 * (u + 1)], h[:].indirect(p1[:, 16 * u : 16 * (u + 1)]))
+            for u in range(2):
+                cols = slice(256 * u, 256 * (u + 1))
+                nc.vector.tensor_tensor(
+                    f4[b][:, t, cols], h[:].indirect(p2[:, 16 * u : 16 * (u + 1)]), left[:, cols], ALU.mult
+                )
+
+        def tanh(b, t):
+            nc.scalar.activation(th4[b][:, t, :], f4[b][:, t, :], ACT.Tanh)
+
+        def weave_v(grouped, planes, gain, m0, m1):
+            nc.vector.tensor_tensor(
+                grouped[:, PACK * m0 : PACK * m1].rearrange("p (c i t) -> p c t i", i=2, t=PACK),
+                planes[:, :, m0:m1].rearrange("p t (c i) -> p c t i", i=2),
+                gain.unsqueeze(1).unsqueeze(3).to_broadcast([P, (m1 - m0) // 2, PACK, 2]),
+                ALU.mult,
+            )
+
+        def scale_s(scaled, planes, gain, t, m0, m1):
+            nc.scalar.activation(scaled[:, t, m0:m1], planes[:, t, m0:m1], ACT.Copy, scale=gain[:, t : t + 1])
+
+        def weave_s(grouped, scaled, m0, m1):
+            nc.scalar.copy(
+                grouped[:, PACK * m0 : PACK * m1].rearrange("p (c i t) -> p c t i", i=2, t=PACK),
+                scaled[:, :, m0:m1].rearrange("p t (c i) -> p c t i", i=2),
+            )
+
+        def cast_w3(grouped, raw, c0, c1):
+            nc.scalar.copy(
+                grouped[:, PACK * c0 : PACK * c1].rearrange("p (c i j) -> p c j i", i=2, j=PACK),
+                raw[:, :, c0:c1].rearrange("p j (c i) -> p c j i", i=2),
+            )
+
+        z_bf = [keep.tile([P, PACK * PAIRS], BF16, name="z_bf%d" % b, align_bytes=64) for b in range(2)]
+        z_scaled = keep.tile([P, PACK, PAIRS], BF16, name="z_scaled")
+        x_bf = [keep.tile([P, PACK * PAIRS], BF16, name="x_bf%d" % b, align_bytes=64) for b in range(2)]
+        z_mx = [mx_tiles("z%d" % b) for b in range(2)]
+        x_mx = [mx_tiles("x%d" % b) for b in range(2)]
+        w3_bf = [keep.tile([P, PACK * N], BF16, name="w3_bf%d" % b, align_bytes=64) for b in range(2)]
+        w3_mx = [mx_tiles("w3_%d" % b) for b in range(2)]
+        x_scaled = keep.tile([P, PACK, PAIRS], BF16, name="x_scaled")
+        y_acc = [psum.tile([P, PAIRS], F32, name="yacc%d" % n) for n in range(N // P)]
+
+        def z_pass(b, start):
+            for n in range(N // P):
+                nc.tensor.matmul_mx(
+                    out=y_acc[n][:],
+                    lhsT=w2_w[:, b, 2 * P * n : 2 * P * (n + 1)].bitcast(FP4X4),
+                    lhsT_scale=w2_sc[:, b, P * n : P * (n + 1)],
+                    rhs=z_mx[b][0][:].bitcast(FP8X4),
+                    rhs_scale=z_mx[b][1][:],
+                    start=start,
+                    stop=False,
+                )
+
+        def x_pass(b, stop, tiles):
+            for n in tiles:
+                nc.tensor.matmul_mx(
+                    out=y_acc[n][:],
+                    lhsT=w3_mx[b][0][:, P * n : P * (n + 1)].bitcast(FP8X4),
+                    lhsT_scale=w3_mx[b][1][:, P * n : P * (n + 1)],
+                    rhs=x_mx[b][0][:].bitcast(FP8X4),
+                    rhs_scale=x_mx[b][1][:],
+                    start=False,
+                    stop=stop,
+                )
+
+        ZS = 256
+        h0 = stage1(0, 0)
+        h1 = stage1(0, 1)
+        pair(0, 0, h0)
+        cast_w1("s", w1_bf[1, 0], w1_raw[1, 0, 0], 0, 128)
+        h2 = stage1(0, 2)
+        pair(0, 1, h1)
+        quantize(w1_mx[1, 0], w1_bf[1, 0], 0, 512)
+        cast_w1("s", w1_bf[1, 1], w1_raw[1, 1, 0], 0, 128)
+        h3 = stage1(0, 3)
+        pair(0, 2, h2)
+        quantize(w1_mx[1, 1], w1_bf[1, 1], 0, 512)
+        pair(0, 3, h3)
+        tanh(0, 0)
+        tanh(0, 1)
+        h4 = stage1(1, 0)
+        h5 = stage1(1, 1)
+        tanh(0, 2)
+        tanh(0, 3)
+        pair(1, 0, h4)
+        h6 = stage1(1, 2)
+        for t in range(PACK):
+            scale_s(x_scaled, th4[0], gt_sb[:, 0, :], t, 0, 512)
+        pair(1, 1, h5)
+        h7 = stage1(1, 3)
+        weave_s(x_bf[0], x_scaled, 0, 512)
+        for t in range(PACK):
+            scale_s(z_scaled, f4[0], gz_sb[:, 0, :], t, 0, ZS)
+        weave_s(z_bf[0], z_scaled, 0, ZS)
+        pair(1, 2, h6)
+        pair(1, 3, h7)
+        if ZS < 512:
+            weave_v(z_bf[0], f4[0], gz_sb[:, 0, :], ZS, 512)
+        for t in range(PACK):
+            tanh(1, t)
+        cast_w3(w3_bf[0], w3_raw[0], 0, 512)
+        weave_v(z_bf[1], f4[1], gz_sb[:, 1, :], 0, 512)
+        quantize(z_mx[0], z_bf[0], 0, 512)
+        z_pass(0, True)
+        quantize(x_mx[0], x_bf[0], 0, 512)
+        weave_v(x_bf[1], th4[1], gt_sb[:, 1, :], 0, 512)
+        quantize(z_mx[1], z_bf[1], 0, 512)
+        z_pass(1, False)
+        quantize(w3_mx[0], w3_bf[0], 0, 512)
+        x_pass(0, False, range(4))
+        cast_w3(w3_bf[1], w3_raw[1], 0, 128)
+        cast_w3(w3_bf[1], w3_raw[1], 128, 256)
+        cast_w3(w3_bf[1], w3_raw[1], 256, 512)
+        quantize(w3_mx[1], w3_bf[1], 0, 128)
+        quantize(x_mx[1], x_bf[1], 0, 512)
+        x_pass(1, True, [0])
+        quantize(w3_mx[1], w3_bf[1], 128, 256)
+        x_pass(1, True, [1])
+        quantize(w3_mx[1], w3_bf[1], 256, 512)
+        x_pass(1, True, [2, 3])
+
+        for n in range(N // P):
+            y = keep.tile([P, PAIRS], F32, name="y%d" % n)
+            nc.scalar.copy(y[:], y_acc[n][:])
+            other = ring.tile([P, TRIADS], F32, name="other")
+            nc.vector.tensor_tensor(other[:], y[:].indirect(p4[:]), gd_wide[:, n, :], ALU.mult)
+            res = keep.tile([P, TRIADS], F32, name="res%d" % n)
+            nc.vector.tensor_tensor(res[:], y[:].indirect(p3[:]), other[:], ALU.subtract)
+            nc.sync.dma_start(out[P * n : P * (n + 1), :], res[:])

@@ -57,10 +57,6 @@ def tile_list_friend_triad_scores_kernel(
         nc.gpsimd.memset(w2_sc[:].rearrange("p a c -> p (a c)").bitcast(I32), 0)
 
         idx = load_list(offs, "idx")
-        for q in range(4):
-            nc.sync.dma_start(
-                tab_sc[32 * q : 32 * q + 8, :].bitcast(I32), tab_scales[:, 4 * q : 4 * q + 4, :].bitcast(I32)
-            )
 
         def load_w(src, a, c0, c1, name):
             raw = keep.tile([P, PACK, c1 - c0], F32, name=name)
@@ -74,14 +70,24 @@ def tile_list_friend_triad_scores_kernel(
             nc.sync.dma_start(t[:], tab_words[a].rearrange("p t i -> p (t i)").bitcast(I32))
             tab_w.append(t)
             if a == 0:
-                w1_raw[0, 0, 0] = load_w(w1, 0, 0, 256, "w1raw00a")
-                w1_raw[0, 0, 1] = load_w(w1, 0, 256, 512, "w1raw00b")
+                for q in range(4):
+                    nc.sync.dma_start(
+                        tab_sc[32 * q : 32 * q + 8, :].bitcast(I32), tab_scales[:, 4 * q : 4 * q + 4, :].bitcast(I32)
+                    )
+                w1_raw[0, 0, 0] = load_w(w1, 0, 0, 512, "w1raw00")
         w1_raw[0, 1, 0] = load_w(w1, 1, 0, 256, "w1raw01a")
         w1_raw[0, 1, 1] = load_w(w1, 1, 256, 512, "w1raw01b")
         p1 = load_list(pos1, "p1")
         p2 = load_list(pos2, "p2")
         w1_raw[1, 0, 0] = load_w(w1, 0, 512, 1024, "w1raw10")
         w1_raw[1, 1, 0] = load_w(w1, 1, 512, 1024, "w1raw11")
+        gz_sb = keep.tile([P, 2, PACK], F32, name="gz_sb")
+        gt_sb = keep.tile([P, 2, PACK], F32, name="gt_sb")
+        gd_sb = keep.tile([P, N // P], F32, name="gd_sb")
+        nc.sync.dma_start(gz_sb[:], gz.rearrange("(b p t) -> p b t", p=P, t=PACK))
+        nc.sync.dma_start(gt_sb[:], gt.rearrange("(b p t) -> p b t", p=P, t=PACK))
+        with nc.allow_non_contiguous_dma(reason="one weight a partition"):
+            nc.sync.dma_start(gd_sb[:], gd.rearrange("(n p) -> p n", p=P))
         w2_w = keep.tile([P, 2, 2 * N], U8, name="w2_w", align_bytes=64)
         nc.sync.dma_start(w2_w[:].bitcast(I32), w2_words.rearrange("a p c -> p a c").bitcast(I32))
         for q in range(4):
@@ -93,17 +99,8 @@ def tile_list_friend_triad_scores_kernel(
         p3 = load_list(pos3, "p3")
         p4 = load_list(pos4, "p4")
 
-        gz_sb = keep.tile([P, 2, PACK], F32, name="gz_sb")
-        gt_sb = keep.tile([P, 2, PACK], F32, name="gt_sb")
-        gd_sb = keep.tile([P, N // P], F32, name="gd_sb")
-        nc.gpsimd.dma_start(gz_sb[:], gz.rearrange("(b p t) -> p b t", p=P, t=PACK))
-        nc.gpsimd.dma_start(gt_sb[:], gt.rearrange("(b p t) -> p b t", p=P, t=PACK))
-        with nc.allow_non_contiguous_dma(reason="one weight a partition"):
-            nc.gpsimd.dma_start(gd_sb[:], gd.rearrange("(n p) -> p n", p=P))
-        gd_wide = keep.tile([P, N // P, TRIADS], F32, name="gd_wide")
 
         got_sc = keep.tile([P, S], U8, name="got_sc", align_bytes=64)
-        nc.vector.tensor_copy(got_sc[:], tab_sc[:].indirect(idx[:]))
 
         def cast_w1(eng, grouped, raw, m0, m1):
             dst = grouped[:].rearrange("p (t m j) -> p m j t", t=PACK, j=PACK)[:, m0:m1]
@@ -120,18 +117,17 @@ def tile_list_friend_triad_scores_kernel(
                 w1_bf[b, a] = keep.tile([P, PACK * BANK], BF16, name="w1bf%d%d" % (b, a), align_bytes=64)
                 w1_mx[b, a] = mx_tiles("w1_%d%d" % (b, a))
 
-        cast_w1("s", w1_bf[0, 0], w1_raw[0, 0, 0], 0, 64)
+        cast_w1("s", w1_bf[0, 0], w1_raw[0, 0, 0], 0, 128)
         got_w = []
         for a in range(2):
             g = keep.tile([P, S], U32, name="got_w%d" % a, align_bytes=64)
             nc.vector.tensor_copy(g[:], tab_w[a][:].bitcast(U32).indirect(idx[:]))
             got_w.append(g)
             if a == 0:
-                cast_w1("v", w1_bf[0, 0], w1_raw[0, 0, 1], 64, 128)
+                nc.vector.tensor_copy(got_sc[:], tab_sc[:].indirect(idx[:]))
                 quantize(w1_mx[0, 0], w1_bf[0, 0], 0, 512)
-        nc.scalar.copy(gd_wide[:], gd_sb[:].unsqueeze(2).to_broadcast([P, N // P, TRIADS]))
         cast_w1("s", w1_bf[0, 1], w1_raw[0, 1, 0], 0, 64)
-        cast_w1("v", w1_bf[0, 1], w1_raw[0, 1, 1], 64, 128)
+        cast_w1("s", w1_bf[0, 1], w1_raw[0, 1, 1], 64, 128)
         quantize(w1_mx[0, 1], w1_bf[0, 1], 0, 128)
         quantize(w1_mx[0, 1], w1_bf[0, 1], 128, 256)
         quantize(w1_mx[0, 1], w1_bf[0, 1], 256, 512)
@@ -171,8 +167,8 @@ def tile_list_friend_triad_scores_kernel(
                     f4[b][:, t, cols], h[:].indirect(p2[:, 16 * u : 16 * (u + 1)]), left[:, cols], ALU.mult
                 )
 
-        def tanh(b, t):
-            nc.scalar.activation(th4[b][:, t, :], f4[b][:, t, :], ACT.Tanh)
+        def tanh(b, t0, t1):
+            nc.scalar.activation(th4[b][:, t0:t1, :], f4[b][:, t0:t1, :], ACT.Tanh)
 
         def weave_v(grouped, planes, gain, m0, m1):
             nc.vector.tensor_tensor(
@@ -191,19 +187,23 @@ def tile_list_friend_triad_scores_kernel(
                 scaled[:, :, m0:m1].rearrange("p t (c i) -> p c t i", i=2),
             )
 
-        def cast_w3(grouped, raw, c0, c1):
-            nc.scalar.copy(
-                grouped[:, PACK * c0 : PACK * c1].rearrange("p (c i j) -> p c j i", i=2, j=PACK),
-                raw[:, :, c0:c1].rearrange("p j (c i) -> p c j i", i=2),
-            )
+        def cast_w3(n0, n1):
+            for a in range(2):
+                nc.scalar.copy(
+                    w3_bf[:].rearrange("p (n a c i j) -> p n a c j i", a=2, c=P // 2, i=2, j=PACK)[:, n0:n1, a],
+                    w3_raw[a][:].rearrange("p j (n c i) -> p n c j i", c=P // 2, i=2)[:, n0:n1],
+                )
 
         z_bf = [keep.tile([P, PACK * PAIRS], BF16, name="z_bf%d" % b, align_bytes=64) for b in range(2)]
         z_scaled = keep.tile([P, PACK, PAIRS], BF16, name="z_scaled")
         x_bf = [keep.tile([P, PACK * PAIRS], BF16, name="x_bf%d" % b, align_bytes=64) for b in range(2)]
         z_mx = [mx_tiles("z%d" % b) for b in range(2)]
         x_mx = [mx_tiles("x%d" % b) for b in range(2)]
-        w3_bf = [keep.tile([P, PACK * N], BF16, name="w3_bf%d" % b, align_bytes=64) for b in range(2)]
-        w3_mx = [mx_tiles("w3_%d" % b) for b in range(2)]
+        w3_bf = keep.tile([P, 2 * PACK * N], BF16, name="w3_bf", align_bytes=64)
+        w3_mx = (
+            keep.tile([P, 2 * N], U32, name="w3_codes", align_bytes=64),
+            keep.tile([P, 2 * N], U8, name="w3_scales", align_bytes=64),
+        )
         x_scaled = keep.tile([P, PACK, PAIRS], BF16, name="x_scaled")
         y_acc = [psum.tile([P, PAIRS], F32, name="yacc%d" % n) for n in range(N // P)]
 
@@ -223,15 +223,15 @@ def tile_list_friend_triad_scores_kernel(
             for n in tiles:
                 nc.tensor.matmul_mx(
                     out=y_acc[n][:],
-                    lhsT=w3_mx[b][0][:, P * n : P * (n + 1)].bitcast(FP8X4),
-                    lhsT_scale=w3_mx[b][1][:, P * n : P * (n + 1)],
+                    lhsT=w3_mx[0][:, P * (2 * n + b) : P * (2 * n + b + 1)].bitcast(FP8X4),
+                    lhsT_scale=w3_mx[1][:, P * (2 * n + b) : P * (2 * n + b + 1)],
                     rhs=x_mx[b][0][:].bitcast(FP8X4),
                     rhs_scale=x_mx[b][1][:],
                     start=False,
                     stop=stop,
                 )
 
-        ZS = 256
+        ZS = 320
         h0 = stage1(0, 0)
         h1 = stage1(0, 1)
         pair(0, 0, h0)
@@ -244,12 +244,10 @@ def tile_list_friend_triad_scores_kernel(
         pair(0, 2, h2)
         quantize(w1_mx[1, 1], w1_bf[1, 1], 0, 512)
         pair(0, 3, h3)
-        tanh(0, 0)
-        tanh(0, 1)
+        tanh(0, 0, 2)
         h4 = stage1(1, 0)
         h5 = stage1(1, 1)
-        tanh(0, 2)
-        tanh(0, 3)
+        tanh(0, 2, 4)
         pair(1, 0, h4)
         h6 = stage1(1, 2)
         for t in range(PACK):
@@ -264,34 +262,45 @@ def tile_list_friend_triad_scores_kernel(
         pair(1, 3, h7)
         if ZS < 512:
             weave_v(z_bf[0], f4[0], gz_sb[:, 0, :], ZS, 512)
-        for t in range(PACK):
-            tanh(1, t)
-        cast_w3(w3_bf[0], w3_raw[0], 0, 512)
+        tanh(1, 0, 2)
+        tanh(1, 2, 4)
         weave_v(z_bf[1], f4[1], gz_sb[:, 1, :], 0, 512)
         quantize(z_mx[0], z_bf[0], 0, 512)
         z_pass(0, True)
         quantize(x_mx[0], x_bf[0], 0, 512)
+        cast_w3(0, 1)
         weave_v(x_bf[1], th4[1], gt_sb[:, 1, :], 0, 512)
         quantize(z_mx[1], z_bf[1], 0, 512)
         z_pass(1, False)
-        quantize(w3_mx[0], w3_bf[0], 0, 512)
-        x_pass(0, False, range(4))
-        cast_w3(w3_bf[1], w3_raw[1], 0, 128)
-        cast_w3(w3_bf[1], w3_raw[1], 128, 256)
-        cast_w3(w3_bf[1], w3_raw[1], 256, 512)
-        quantize(w3_mx[1], w3_bf[1], 0, 128)
+        cast_w3(1, 2)
+        cast_w3(2, 4)
+        quantize(w3_mx, w3_bf, 0, 256)
+        x_pass(0, False, [0])
         quantize(x_mx[1], x_bf[1], 0, 512)
         x_pass(1, True, [0])
-        quantize(w3_mx[1], w3_bf[1], 128, 256)
-        x_pass(1, True, [1])
-        quantize(w3_mx[1], w3_bf[1], 256, 512)
-        x_pass(1, True, [2, 3])
+        for n in range(1, 4):
+            quantize(w3_mx, w3_bf, 256 * n, 256 * (n + 1))
+            x_pass(0, False, [n])
+            x_pass(1, True, [n])
 
-        for n in range(N // P):
-            y = keep.tile([P, PAIRS], F32, name="y%d" % n)
-            nc.scalar.copy(y[:], y_acc[n][:])
-            other = ring.tile([P, TRIADS], F32, name="other")
-            nc.vector.tensor_tensor(other[:], y[:].indirect(p4[:]), gd_wide[:, n, :], ALU.mult)
+        y = {}
+        second = {}
+
+        def fetch(n):
+            y[n] = keep.tile([P, PAIRS], F32, name="y%d" % n)
+            nc.scalar.copy(y[n][:], y_acc[n][:])
+            second[n] = keep.tile([P, TRIADS], F32, name="second%d" % n)
+            nc.vector.tensor_copy(second[n][:], y[n][:].indirect(p4[:]))
+
+        def finish(n):
+            weighted = keep.tile([P, TRIADS], F32, name="weighted%d" % n)
+            nc.scalar.activation(weighted[:], second[n][:], ACT.Copy, scale=gd_sb[:, n : n + 1])
             res = keep.tile([P, TRIADS], F32, name="res%d" % n)
-            nc.vector.tensor_tensor(res[:], y[:].indirect(p3[:]), other[:], ALU.subtract)
+            nc.vector.tensor_tensor(res[:], y[n][:].indirect(p3[:]), weighted[:], ALU.subtract)
             nc.sync.dma_start(out[P * n : P * (n + 1), :], res[:])
+
+        fetch(0)
+        for n in range(1, N // P):
+            fetch(n)
+            finish(n - 1)
+        finish(N // P - 1)

@@ -49,12 +49,16 @@ def tile_list_friend_triad_scores_kernel(
 
         tab_sc = keep.tile([P, T], U8, name="tab_sc", align_bytes=64)
         nc.gpsimd.memset(tab_sc[:].bitcast(I32), 0)
+        for q in range(4):
+            nc.gpsimd.dma_start(
+                tab_sc[32 * q : 32 * q + 8, :].bitcast(I32), tab_scales[:, 4 * q : 4 * q + 4, :].bitcast(I32)
+            )
         warm = keep.tile([P, 8], F32, name="warm")
-        nc.gpsimd.memset(warm[:], 0.0)
+        nc.vector.memset(warm[:], 0.0)
         warm2 = keep.tile([P, 8], F32, name="warm2")
         nc.scalar.activation(warm2[:], warm[:], ACT.Tanh)
         w2_sc = keep.tile([P, 2, N], U8, name="w2_sc", align_bytes=64)
-        nc.gpsimd.memset(w2_sc[:].rearrange("p a c -> p (a c)").bitcast(I32), 0)
+        nc.vector.memset(w2_sc[:].rearrange("p a c -> p (a c)").bitcast(I32), 0)
 
         idx = load_list(offs, "idx")
 
@@ -70,13 +74,8 @@ def tile_list_friend_triad_scores_kernel(
             nc.sync.dma_start(t[:], tab_words[a].rearrange("p t i -> p (t i)").bitcast(I32))
             tab_w.append(t)
             if a == 0:
-                for q in range(4):
-                    nc.sync.dma_start(
-                        tab_sc[32 * q : 32 * q + 8, :].bitcast(I32), tab_scales[:, 4 * q : 4 * q + 4, :].bitcast(I32)
-                    )
                 w1_raw[0, 0, 0] = load_w(w1, 0, 0, 512, "w1raw00")
-        w1_raw[0, 1, 0] = load_w(w1, 1, 0, 256, "w1raw01a")
-        w1_raw[0, 1, 1] = load_w(w1, 1, 256, 512, "w1raw01b")
+        w1_raw[0, 1, 0] = load_w(w1, 1, 0, 512, "w1raw01")
         p1 = load_list(pos1, "p1")
         p2 = load_list(pos2, "p2")
         w1_raw[1, 0, 0] = load_w(w1, 0, 512, 1024, "w1raw10")
@@ -86,8 +85,7 @@ def tile_list_friend_triad_scores_kernel(
         gd_sb = keep.tile([P, N // P], F32, name="gd_sb")
         nc.sync.dma_start(gz_sb[:], gz.rearrange("(b p t) -> p b t", p=P, t=PACK))
         nc.sync.dma_start(gt_sb[:], gt.rearrange("(b p t) -> p b t", p=P, t=PACK))
-        with nc.allow_non_contiguous_dma(reason="one weight a partition"):
-            nc.sync.dma_start(gd_sb[:], gd.rearrange("(n p) -> p n", p=P))
+        w3_raw = [load_w(w3, a, 0, N, "w3raw%d" % a) for a in range(2)]
         w2_w = keep.tile([P, 2, 2 * N], U8, name="w2_w", align_bytes=64)
         nc.sync.dma_start(w2_w[:].bitcast(I32), w2_words.rearrange("a p c -> p a c").bitcast(I32))
         for q in range(4):
@@ -95,7 +93,8 @@ def tile_list_friend_triad_scores_kernel(
                 w2_sc[32 * q : 32 * q + 4, :, :].bitcast(I32),
                 w2_scales[:, 4 * q : 4 * q + 4, :].rearrange("a r c -> r a c").bitcast(I32),
             )
-        w3_raw = [load_w(w3, a, 0, N, "w3raw%d" % a) for a in range(2)]
+        with nc.allow_non_contiguous_dma(reason="one weight a partition"):
+            nc.sync.dma_start(gd_sb[:], gd.rearrange("(n p) -> p n", p=P))
         p3 = load_list(pos3, "p3")
         p4 = load_list(pos4, "p4")
 
@@ -104,7 +103,7 @@ def tile_list_friend_triad_scores_kernel(
 
         def cast_w1(eng, grouped, raw, m0, m1):
             dst = grouped[:].rearrange("p (t m j) -> p m j t", t=PACK, j=PACK)[:, m0:m1]
-            src = raw[:].rearrange("p j (m t) -> p m j t", t=PACK)
+            src = raw[:].rearrange("p j (m t) -> p m j t", t=PACK)[:, m0:m1]
             if eng == "v":
                 nc.vector.tensor_copy(dst, src)
             else:
@@ -126,8 +125,8 @@ def tile_list_friend_triad_scores_kernel(
             if a == 0:
                 nc.vector.tensor_copy(got_sc[:], tab_sc[:].indirect(idx[:]))
                 quantize(w1_mx[0, 0], w1_bf[0, 0], 0, 512)
-        cast_w1("s", w1_bf[0, 1], w1_raw[0, 1, 0], 0, 64)
-        cast_w1("s", w1_bf[0, 1], w1_raw[0, 1, 1], 64, 128)
+        cast_w1("s", w1_bf[0, 1], w1_raw[0, 1, 0], 0, 72)
+        cast_w1("v", w1_bf[0, 1], w1_raw[0, 1, 0], 72, 128)
         quantize(w1_mx[0, 1], w1_bf[0, 1], 0, 128)
         quantize(w1_mx[0, 1], w1_bf[0, 1], 128, 256)
         quantize(w1_mx[0, 1], w1_bf[0, 1], 256, 512)
@@ -183,8 +182,8 @@ def tile_list_friend_triad_scores_kernel(
 
         def weave_s(grouped, scaled, m0, m1):
             nc.scalar.copy(
-                grouped[:, PACK * m0 : PACK * m1].rearrange("p (c i t) -> p c t i", i=2, t=PACK),
-                scaled[:, :, m0:m1].rearrange("p t (c i) -> p c t i", i=2),
+                grouped[:, PACK * m0 : PACK * m1].rearrange("p (c i t) -> p c t i", i=4, t=PACK),
+                scaled[:, :, m0:m1].rearrange("p t (c i) -> p c t i", i=4),
             )
 
         def cast_w3(n0, n1):
@@ -231,7 +230,7 @@ def tile_list_friend_triad_scores_kernel(
                     stop=stop,
                 )
 
-        ZS = 320
+        ZS = 384
         h0 = stage1(0, 0)
         h1 = stage1(0, 1)
         pair(0, 0, h0)
@@ -245,6 +244,7 @@ def tile_list_friend_triad_scores_kernel(
         quantize(w1_mx[1, 1], w1_bf[1, 1], 0, 512)
         pair(0, 3, h3)
         tanh(0, 0, 2)
+        cast_w3(0, 1)
         h4 = stage1(1, 0)
         h5 = stage1(1, 1)
         tanh(0, 2, 4)
@@ -268,7 +268,6 @@ def tile_list_friend_triad_scores_kernel(
         quantize(z_mx[0], z_bf[0], 0, 512)
         z_pass(0, True)
         quantize(x_mx[0], x_bf[0], 0, 512)
-        cast_w3(0, 1)
         weave_v(x_bf[1], th4[1], gt_sb[:, 1, :], 0, 512)
         quantize(z_mx[1], z_bf[1], 0, 512)
         z_pass(1, False)

@@ -49,10 +49,6 @@ def tile_list_friend_triad_scores_kernel(
 
         tab_sc = keep.tile([P, T], U8, name="tab_sc", align_bytes=64)
         nc.gpsimd.memset(tab_sc[:].bitcast(I32), 0)
-        for q in range(4):
-            nc.gpsimd.dma_start(
-                tab_sc[32 * q : 32 * q + 8, :].bitcast(I32), tab_scales[:, 4 * q : 4 * q + 4, :].bitcast(I32)
-            )
         warm = keep.tile([P, 8], F32, name="warm")
         nc.vector.memset(warm[:], 0.0)
         warm2 = keep.tile([P, 8], F32, name="warm2")
@@ -74,6 +70,10 @@ def tile_list_friend_triad_scores_kernel(
             nc.sync.dma_start(t[:], tab_words[a].rearrange("p t i -> p (t i)").bitcast(I32))
             tab_w.append(t)
             if a == 0:
+                for q in range(4):
+                    nc.sync.dma_start(
+                        tab_sc[32 * q : 32 * q + 8, :].bitcast(I32), tab_scales[:, 4 * q : 4 * q + 4, :].bitcast(I32)
+                    )
                 w1_raw[0, 0, 0] = load_w(w1, 0, 0, 512, "w1raw00")
         w1_raw[0, 1, 0] = load_w(w1, 1, 0, 512, "w1raw01")
         p1 = load_list(pos1, "p1")
@@ -116,7 +116,7 @@ def tile_list_friend_triad_scores_kernel(
                 w1_bf[b, a] = keep.tile([P, PACK * BANK], BF16, name="w1bf%d%d" % (b, a), align_bytes=64)
                 w1_mx[b, a] = mx_tiles("w1_%d%d" % (b, a))
 
-        cast_w1("s", w1_bf[0, 0], w1_raw[0, 0, 0], 0, 128)
+        cast_w1("s", w1_bf[0, 0], w1_raw[0, 0, 0], 0, 80)
         got_w = []
         for a in range(2):
             g = keep.tile([P, S], U32, name="got_w%d" % a, align_bytes=64)
@@ -124,9 +124,10 @@ def tile_list_friend_triad_scores_kernel(
             got_w.append(g)
             if a == 0:
                 nc.vector.tensor_copy(got_sc[:], tab_sc[:].indirect(idx[:]))
+                cast_w1("v", w1_bf[0, 0], w1_raw[0, 0, 0], 80, 128)
                 quantize(w1_mx[0, 0], w1_bf[0, 0], 0, 512)
-        cast_w1("s", w1_bf[0, 1], w1_raw[0, 1, 0], 0, 72)
-        cast_w1("v", w1_bf[0, 1], w1_raw[0, 1, 0], 72, 128)
+        cast_w1("s", w1_bf[0, 1], w1_raw[0, 1, 0], 0, 44)
+        cast_w1("v", w1_bf[0, 1], w1_raw[0, 1, 0], 44, 128)
         quantize(w1_mx[0, 1], w1_bf[0, 1], 0, 128)
         quantize(w1_mx[0, 1], w1_bf[0, 1], 128, 256)
         quantize(w1_mx[0, 1], w1_bf[0, 1], 256, 512)
@@ -134,7 +135,7 @@ def tile_list_friend_triad_scores_kernel(
         def stage1(b, t):
             h = ring.tile([P, S], F32, name="h", bufs=4)
             for half in range(2):
-                acc = psum.tile([P, BANK], F32, name="hacc", bufs=4)
+                acc = psum.tile([P, BANK], F32, name="hacc", tag="bank", bufs=8)
                 cols = slice(BANK * half, BANK * (half + 1))
                 rows = slice(P * t, P * (t + 1))
                 for a in range(2):
@@ -204,7 +205,7 @@ def tile_list_friend_triad_scores_kernel(
             keep.tile([P, 2 * N], U8, name="w3_scales", align_bytes=64),
         )
         x_scaled = keep.tile([P, PACK, PAIRS], BF16, name="x_scaled")
-        y_acc = [psum.tile([P, PAIRS], F32, name="yacc%d" % n) for n in range(N // P)]
+        y_acc = []
 
         def z_pass(b, start):
             for n in range(N // P):
@@ -218,14 +219,14 @@ def tile_list_friend_triad_scores_kernel(
                     stop=False,
                 )
 
-        def x_pass(b, stop, tiles):
+        def x_pass(b, stop, tiles, m0=0, m1=PAIRS):
             for n in tiles:
                 nc.tensor.matmul_mx(
-                    out=y_acc[n][:],
+                    out=y_acc[n][:, m0:m1],
                     lhsT=w3_mx[0][:, P * (2 * n + b) : P * (2 * n + b + 1)].bitcast(FP8X4),
                     lhsT_scale=w3_mx[1][:, P * (2 * n + b) : P * (2 * n + b + 1)],
-                    rhs=x_mx[b][0][:].bitcast(FP8X4),
-                    rhs_scale=x_mx[b][1][:],
+                    rhs=x_mx[b][0][:, m0:m1].bitcast(FP8X4),
+                    rhs_scale=x_mx[b][1][:, m0:m1],
                     start=False,
                     stop=stop,
                 )
@@ -247,36 +248,40 @@ def tile_list_friend_triad_scores_kernel(
         cast_w3(0, 1)
         h4 = stage1(1, 0)
         h5 = stage1(1, 1)
-        tanh(0, 2, 4)
         pair(1, 0, h4)
-        h6 = stage1(1, 2)
-        for t in range(PACK):
-            scale_s(x_scaled, th4[0], gt_sb[:, 0, :], t, 0, 512)
-        pair(1, 1, h5)
-        h7 = stage1(1, 3)
-        weave_s(x_bf[0], x_scaled, 0, 512)
         for t in range(PACK):
             scale_s(z_scaled, f4[0], gz_sb[:, 0, :], t, 0, ZS)
+        h6 = stage1(1, 2)
+        pair(1, 1, h5)
         weave_s(z_bf[0], z_scaled, 0, ZS)
+        tanh(0, 2, 4)
+        h7 = stage1(1, 3)
+        for t in range(PACK):
+            scale_s(x_scaled, th4[0], gt_sb[:, 0, :], t, 0, 512)
         pair(1, 2, h6)
         pair(1, 3, h7)
         if ZS < 512:
             weave_v(z_bf[0], f4[0], gz_sb[:, 0, :], ZS, 512)
+        quantize(z_mx[0], z_bf[0], 0, 512)
+        y_acc.extend([psum.tile([P, PAIRS], F32, name="yacc%d" % n, tag="bank", bufs=8) for n in range(N // P)])
+        z_pass(0, True)
+        weave_s(x_bf[0], x_scaled, 0, 512)
         tanh(1, 0, 2)
         tanh(1, 2, 4)
         weave_v(z_bf[1], f4[1], gz_sb[:, 1, :], 0, 512)
-        quantize(z_mx[0], z_bf[0], 0, 512)
-        z_pass(0, True)
+        quantize(w3_mx, w3_bf, 0, 256)
         quantize(x_mx[0], x_bf[0], 0, 512)
-        weave_v(x_bf[1], th4[1], gt_sb[:, 1, :], 0, 512)
+        x_pass(0, False, [0])
         quantize(z_mx[1], z_bf[1], 0, 512)
         z_pass(1, False)
+        weave_v(x_bf[1], th4[1], gt_sb[:, 1, :], 0, 256)
+        weave_v(x_bf[1], th4[1], gt_sb[:, 1, :], 256, 512)
         cast_w3(1, 2)
         cast_w3(2, 4)
-        quantize(w3_mx, w3_bf, 0, 256)
-        x_pass(0, False, [0])
-        quantize(x_mx[1], x_bf[1], 0, 512)
-        x_pass(1, True, [0])
+        quantize(x_mx[1], x_bf[1], 0, 256)
+        x_pass(1, False, [0], 0, 256)
+        quantize(x_mx[1], x_bf[1], 256, 512)
+        x_pass(1, True, [0], 256, 512)
         for n in range(1, 4):
             quantize(w3_mx, w3_bf, 256 * n, 256 * (n + 1))
             x_pass(0, False, [n])

@@ -181,6 +181,15 @@ def tile_list_friend_triad_scores_kernel(
         def scale_s(scaled, planes, gain, t, m0, m1):
             nc.scalar.activation(scaled[:, t, m0:m1], planes[:, t, m0:m1], ACT.Copy, scale=gain[:, t : t + 1])
 
+        def scale_g(scaled, planes, gain, t):
+            nc.gpsimd.tensor_scalar(scaled[:, t, :], planes[:, t, :], gain[:, t : t + 1], 0.0, ALU.mult, ALU.add)
+
+        def weave_c(grouped, scaled, m0, m1):
+            nc.vector.tensor_copy(
+                grouped[:, PACK * m0 : PACK * m1].rearrange("p (c i t) -> p c t i", i=4, t=PACK),
+                scaled[:, :, m0:m1].rearrange("p t (c i) -> p c t i", i=4),
+            )
+
         def weave_s(grouped, scaled, m0, m1):
             nc.scalar.copy(
                 grouped[:, PACK * m0 : PACK * m1].rearrange("p (c i t) -> p c t i", i=4, t=PACK),
@@ -195,7 +204,7 @@ def tile_list_friend_triad_scores_kernel(
                 )
 
         z_bf = [keep.tile([P, PACK * PAIRS], BF16, name="z_bf%d" % b, align_bytes=64) for b in range(2)]
-        z_scaled = keep.tile([P, PACK, PAIRS], BF16, name="z_scaled")
+        z_scaled = [keep.tile([P, PACK, PAIRS], BF16, name="z_scaled%d" % b) for b in range(2)]
         x_bf = [keep.tile([P, PACK * PAIRS], BF16, name="x_bf%d" % b, align_bytes=64) for b in range(2)]
         z_mx = [mx_tiles("z%d" % b) for b in range(2)]
         x_mx = [mx_tiles("x%d" % b) for b in range(2)]
@@ -204,7 +213,7 @@ def tile_list_friend_triad_scores_kernel(
             keep.tile([P, 2 * N], U32, name="w3_codes", align_bytes=64),
             keep.tile([P, 2 * N], U8, name="w3_scales", align_bytes=64),
         )
-        x_scaled = keep.tile([P, PACK, PAIRS], BF16, name="x_scaled")
+        x_scaled = [keep.tile([P, PACK, PAIRS], BF16, name="x_scaled%d" % b) for b in range(2)]
         y_acc = []
 
         def z_pass(b, start):
@@ -231,57 +240,67 @@ def tile_list_friend_triad_scores_kernel(
                     stop=stop,
                 )
 
-        ZS = 384
+        def zs(b, t):
+            scale_g(z_scaled[b], f4[b], gz_sb[:, b, :], t)
+
+        def xs(b, t, m1):
+            scale_s(x_scaled[b], th4[b], gt_sb[:, b, :], t, 0, m1)
+
         h0 = stage1(0, 0)
         h1 = stage1(0, 1)
         pair(0, 0, h0)
+        zs(0, 0)
         cast_w1("s", w1_bf[1, 0], w1_raw[1, 0, 0], 0, 128)
         h2 = stage1(0, 2)
         pair(0, 1, h1)
+        zs(0, 1)
         quantize(w1_mx[1, 0], w1_bf[1, 0], 0, 512)
         cast_w1("s", w1_bf[1, 1], w1_raw[1, 1, 0], 0, 128)
         h3 = stage1(0, 3)
         pair(0, 2, h2)
+        zs(0, 2)
         quantize(w1_mx[1, 1], w1_bf[1, 1], 0, 512)
         pair(0, 3, h3)
+        zs(0, 3)
         tanh(0, 0, 2)
         cast_w3(0, 1)
         h4 = stage1(1, 0)
         h5 = stage1(1, 1)
         pair(1, 0, h4)
-        for t in range(PACK):
-            scale_s(z_scaled, f4[0], gz_sb[:, 0, :], t, 0, ZS)
+        zs(1, 0)
+        tanh(0, 2, 4)
         h6 = stage1(1, 2)
         pair(1, 1, h5)
-        weave_s(z_bf[0], z_scaled, 0, ZS)
-        tanh(0, 2, 4)
+        zs(1, 1)
+        weave_s(z_bf[0], z_scaled[0], 0, 512)
         h7 = stage1(1, 3)
         for t in range(PACK):
-            scale_s(x_scaled, th4[0], gt_sb[:, 0, :], t, 0, 512)
+            xs(0, t, 512)
         pair(1, 2, h6)
+        zs(1, 2)
         pair(1, 3, h7)
-        if ZS < 512:
-            weave_v(z_bf[0], f4[0], gz_sb[:, 0, :], ZS, 512)
         quantize(z_mx[0], z_bf[0], 0, 512)
         y_acc.extend([psum.tile([P, PAIRS], F32, name="yacc%d" % n, tag="bank", bufs=8) for n in range(N // P)])
         z_pass(0, True)
-        weave_s(x_bf[0], x_scaled, 0, 512)
         tanh(1, 0, 2)
+        weave_s(x_bf[0], x_scaled[0], 0, 384)
+        scale_s(z_scaled[1], f4[1], gz_sb[:, 1, :], 3, 0, 512)
         tanh(1, 2, 4)
-        weave_v(z_bf[1], f4[1], gz_sb[:, 1, :], 0, 512)
         quantize(w3_mx, w3_bf, 0, 256)
+        weave_c(x_bf[0], x_scaled[0], 384, 512)
+        weave_c(z_bf[1], z_scaled[1], 0, 512)
         quantize(x_mx[0], x_bf[0], 0, 512)
         x_pass(0, False, [0])
         quantize(z_mx[1], z_bf[1], 0, 512)
         z_pass(1, False)
-        weave_v(x_bf[1], th4[1], gt_sb[:, 1, :], 0, 256)
         weave_v(x_bf[1], th4[1], gt_sb[:, 1, :], 256, 512)
+        weave_v(x_bf[1], th4[1], gt_sb[:, 1, :], 0, 256)
         cast_w3(1, 2)
         cast_w3(2, 4)
-        quantize(x_mx[1], x_bf[1], 0, 256)
-        x_pass(1, False, [0], 0, 256)
         quantize(x_mx[1], x_bf[1], 256, 512)
-        x_pass(1, True, [0], 256, 512)
+        x_pass(1, False, [0], 256, 512)
+        quantize(x_mx[1], x_bf[1], 0, 256)
+        x_pass(1, True, [0], 0, 256)
         for n in range(1, 4):
             quantize(w3_mx, w3_bf, 256 * n, 256 * (n + 1))
             x_pass(0, False, [n])

@@ -30,6 +30,7 @@ def tile_list_friend_triad_scores_kernel(
         lists = ctx.enter_context(tc.tile_pool(name="lists", bufs=1))
         keep = ctx.enter_context(tc.tile_pool(name="keep", bufs=1))
         ring = ctx.enter_context(tc.tile_pool(name="ring", bufs=2))
+        shared = ctx.enter_context(tc.tile_pool(name="shared", bufs=1))
         psum = ctx.enter_context(tc.psum_pool(name="psum", bufs=1))
 
         def load_list(src, name):
@@ -58,8 +59,11 @@ def tile_list_friend_triad_scores_kernel(
 
         idx = load_list(offs, "idx")
 
-        def load_w(src, a, c0, c1, name):
-            raw = keep.tile([P, PACK, c1 - c0], F32, name=name)
+        def load_w(src, a, c0, c1, name, offset=None):
+            if offset is None:
+                raw = keep.tile([P, PACK, c1 - c0], F32, name=name)
+            else:
+                raw = shared.tile([P, PACK, c1 - c0], F32, name=name, offset=offset)
             nc.sync.dma_start(raw[:], src[PASS * a : PASS * (a + 1), c0:c1].rearrange("(p j) c -> p j c", j=PACK))
             return raw
 
@@ -74,12 +78,12 @@ def tile_list_friend_triad_scores_kernel(
                     nc.sync.dma_start(
                         tab_sc[32 * q : 32 * q + 8, :].bitcast(I32), tab_scales[:, 4 * q : 4 * q + 4, :].bitcast(I32)
                     )
-                w1_raw[0, 0, 0] = load_w(w1, 0, 0, 512, "w1raw00")
-        w1_raw[0, 1, 0] = load_w(w1, 1, 0, 512, "w1raw01")
+                w1_raw[0, 0] = load_w(w1, 0, 0, 512, "w1raw00")
+        w1_last = [load_w(w1, 1, 256 * u, 256 * (u + 1), "w1raw01_%d" % u) for u in range(2)]
         p1 = load_list(pos1, "p1")
         p2 = load_list(pos2, "p2")
-        w1_raw[1, 0, 0] = load_w(w1, 0, 512, 1024, "w1raw10")
-        w1_raw[1, 1, 0] = load_w(w1, 1, 512, 1024, "w1raw11")
+        w1_raw[1, 0] = load_w(w1, 0, 512, 1024, "w1raw10", 0)
+        w1_raw[1, 1] = load_w(w1, 1, 512, 1024, "w1raw11", 8192)
         gz_sb = keep.tile([P, 2, PACK], F32, name="gz_sb")
         gt_sb = keep.tile([P, 2, PACK], F32, name="gt_sb")
         gd_sb = keep.tile([P, N // P], F32, name="gd_sb")
@@ -98,12 +102,11 @@ def tile_list_friend_triad_scores_kernel(
         p3 = load_list(pos3, "p3")
         p4 = load_list(pos4, "p4")
 
-
         got_sc = keep.tile([P, S], U8, name="got_sc", align_bytes=64)
 
-        def cast_w1(eng, grouped, raw, m0, m1):
+        def cast_w1(eng, grouped, raw, m0, m1, first=0):
             dst = grouped[:].rearrange("p (t m j) -> p m j t", t=PACK, j=PACK)[:, m0:m1]
-            src = raw[:].rearrange("p j (m t) -> p m j t", t=PACK)[:, m0:m1]
+            src = raw[:].rearrange("p j (m t) -> p m j t", t=PACK)[:, m0 - first : m1 - first]
             if eng == "v":
                 nc.vector.tensor_copy(dst, src)
             else:
@@ -116,7 +119,7 @@ def tile_list_friend_triad_scores_kernel(
                 w1_bf[b, a] = keep.tile([P, PACK * BANK], BF16, name="w1bf%d%d" % (b, a), align_bytes=64)
                 w1_mx[b, a] = mx_tiles("w1_%d%d" % (b, a))
 
-        cast_w1("s", w1_bf[0, 0], w1_raw[0, 0, 0], 0, 80)
+        cast_w1("s", w1_bf[0, 0], w1_raw[0, 0], 0, 80)
         got_w = []
         for a in range(2):
             g = keep.tile([P, S], U32, name="got_w%d" % a, align_bytes=64)
@@ -124,16 +127,20 @@ def tile_list_friend_triad_scores_kernel(
             got_w.append(g)
             if a == 0:
                 nc.vector.tensor_copy(got_sc[:], tab_sc[:].indirect(idx[:]))
-                cast_w1("v", w1_bf[0, 0], w1_raw[0, 0, 0], 80, 128)
+                cast_w1("v", w1_bf[0, 0], w1_raw[0, 0], 80, 128)
                 quantize(w1_mx[0, 0], w1_bf[0, 0], 0, 512)
-        cast_w1("s", w1_bf[0, 1], w1_raw[0, 1, 0], 0, 44)
-        cast_w1("v", w1_bf[0, 1], w1_raw[0, 1, 0], 44, 128)
+        cast_w1("s", w1_bf[0, 1], w1_last[0], 0, 64)
+        cast_w1("s", w1_bf[0, 1], w1_last[1], 64, 88, 64)
+        cast_w1("v", w1_bf[0, 1], w1_last[1], 88, 128, 64)
         quantize(w1_mx[0, 1], w1_bf[0, 1], 0, 128)
         quantize(w1_mx[0, 1], w1_bf[0, 1], 128, 256)
         quantize(w1_mx[0, 1], w1_bf[0, 1], 256, 512)
 
         def stage1(b, t):
-            h = ring.tile([P, S], F32, name="h", bufs=4)
+            if b == 0 and t >= 2:
+                h = shared.tile([P, S], F32, name="h_shared%d" % t, offset=8192 * (t - 2))
+            else:
+                h = ring.tile([P, S], F32, name="h", bufs=4)
             for half in range(2):
                 acc = psum.tile([P, BANK], F32, name="hacc", tag="bank", bufs=8)
                 cols = slice(BANK * half, BANK * (half + 1))
@@ -155,7 +162,7 @@ def tile_list_friend_triad_scores_kernel(
             return h
 
         f4 = [keep.tile([P, PACK, PAIRS], F32, name="f4_%d" % b) for b in range(2)]
-        th4 = [keep.tile([P, PACK, PAIRS], F32, name="th4_%d" % b) for b in range(2)]
+        th = {(b, u): keep.tile([P, 2, PAIRS], F32, name="th%d%d" % (b, u)) for b, u in ((0, 1), (1, 0), (1, 1))}
 
         def pair(b, t, h):
             left = ring.tile([P, PAIRS], F32, name="left")
@@ -168,7 +175,10 @@ def tile_list_friend_triad_scores_kernel(
                 )
 
         def tanh(b, t0, t1):
-            nc.scalar.activation(th4[b][:, t0:t1, :], f4[b][:, t0:t1, :], ACT.Tanh)
+            if (b, t0) == (0, 0):
+                th[0, 0] = shared.tile([P, 2, PAIRS], F32, name="th00", offset=8192 + 4096)
+            u = t0 // 2
+            nc.scalar.activation(th[b, u][:, t0 - 2 * u : t1 - 2 * u, :], f4[b][:, t0:t1, :], ACT.Tanh)
 
         def weave_v(grouped, planes, gain, m0, m1):
             nc.vector.tensor_tensor(
@@ -204,7 +214,8 @@ def tile_list_friend_triad_scores_kernel(
                 )
 
         z_bf = [keep.tile([P, PACK * PAIRS], BF16, name="z_bf%d" % b, align_bytes=64) for b in range(2)]
-        z_scaled = [keep.tile([P, PACK, PAIRS], BF16, name="z_scaled%d" % b) for b in range(2)]
+        z_pairs = keep.tile([P, 2, PAIRS, 2], BF16, name="z_pairs")
+        z_scaled = keep.tile([P, PACK, PAIRS], BF16, name="z_scaled")
         x_bf = [keep.tile([P, PACK * PAIRS], BF16, name="x_bf%d" % b, align_bytes=64) for b in range(2)]
         z_mx = [mx_tiles("z%d" % b) for b in range(2)]
         x_mx = [mx_tiles("x%d" % b) for b in range(2)]
@@ -241,21 +252,41 @@ def tile_list_friend_triad_scores_kernel(
                 )
 
         def zs(b, t):
-            scale_g(z_scaled[b], f4[b], gz_sb[:, b, :], t)
+            dst = z_pairs[:, t // 2, :, t % 2] if b == 0 else z_scaled[:, t, :]
+            nc.gpsimd.tensor_scalar(dst, f4[b][:, t, :], gz_sb[:, b, t : t + 1], 0.0, ALU.mult, ALU.add)
 
         def xs(b, t, m1):
-            scale_s(x_scaled[b], th4[b], gt_sb[:, b, :], t, 0, m1)
+            nc.scalar.activation(
+                x_scaled[b][:, t, 0:m1], th[b, t // 2][:, t % 2, 0:m1], ACT.Copy, scale=gt_sb[:, b, t : t + 1]
+            )
+
+        def zs_v(b, t, m0, m1):
+            nc.vector.tensor_scalar(z_scaled[:, t, m0:m1], f4[b][:, t, m0:m1], gz_sb[:, b, t : t + 1], None, ALU.mult)
+
+        def weave_words(eng, grouped, pairs):
+            word = I32 if eng == "v" else U32
+            dst = grouped[:].bitcast(word).rearrange("p (m u) -> p m u", u=2)
+            src = pairs[:].rearrange("p u m e -> p u (m e)").bitcast(word).rearrange("p u m -> p m u")
+            if eng == "v":
+                nc.vector.tensor_copy(dst, src)
+            else:
+                nc.scalar.copy(dst, src)
+
+        gd_wide = keep.tile([P, N // P, TRIADS], F32, name="gd_wide")
+
+        def spread_gd(n0, n1):
+            nc.scalar.copy(gd_wide[:, n0:n1, :], gd_sb[:, n0:n1].unsqueeze(2).to_broadcast([P, n1 - n0, TRIADS]))
 
         h0 = stage1(0, 0)
         h1 = stage1(0, 1)
         pair(0, 0, h0)
         zs(0, 0)
-        cast_w1("s", w1_bf[1, 0], w1_raw[1, 0, 0], 0, 128)
+        cast_w1("s", w1_bf[1, 0], w1_raw[1, 0], 0, 128)
         h2 = stage1(0, 2)
         pair(0, 1, h1)
         zs(0, 1)
         quantize(w1_mx[1, 0], w1_bf[1, 0], 0, 512)
-        cast_w1("s", w1_bf[1, 1], w1_raw[1, 1, 0], 0, 128)
+        cast_w1("s", w1_bf[1, 1], w1_raw[1, 1], 0, 128)
         h3 = stage1(0, 3)
         pair(0, 2, h2)
         zs(0, 2)
@@ -263,67 +294,85 @@ def tile_list_friend_triad_scores_kernel(
         pair(0, 3, h3)
         zs(0, 3)
         tanh(0, 0, 2)
-        cast_w3(0, 1)
         h4 = stage1(1, 0)
-        h5 = stage1(1, 1)
         pair(1, 0, h4)
         zs(1, 0)
-        tanh(0, 2, 4)
-        h6 = stage1(1, 2)
+        h5 = stage1(1, 1)
         pair(1, 1, h5)
         zs(1, 1)
-        weave_s(z_bf[0], z_scaled[0], 0, 512)
-        h7 = stage1(1, 3)
-        for t in range(PACK):
-            xs(0, t, 512)
+        xs(0, 0, 512)
+        xs(0, 1, 512)
+        h6 = stage1(1, 2)
         pair(1, 2, h6)
         zs(1, 2)
-        pair(1, 3, h7)
-        quantize(z_mx[0], z_bf[0], 0, 512)
-        y_acc.extend([psum.tile([P, PAIRS], F32, name="yacc%d" % n, tag="bank", bufs=8) for n in range(N // P)])
-        z_pass(0, True)
-        tanh(1, 0, 2)
-        weave_s(x_bf[0], x_scaled[0], 0, 384)
-        scale_s(z_scaled[1], f4[1], gz_sb[:, 1, :], 3, 0, 512)
-        tanh(1, 2, 4)
+        cast_w3(0, 1)
         quantize(w3_mx, w3_bf, 0, 256)
-        weave_c(x_bf[0], x_scaled[0], 384, 512)
-        weave_c(z_bf[1], z_scaled[1], 0, 512)
-        quantize(x_mx[0], x_bf[0], 0, 512)
+        h7 = stage1(1, 3)
+        pair(1, 3, h7)
+        tanh(0, 2, 4)
+        weave_words("s", z_bf[0], z_pairs)
+        tanh(1, 0, 1)
+        xs(0, 2, 512)
+        xs(0, 3, 512)
+        tanh(1, 1, 2)
+        xs(1, 0, 512)
+        tanh(1, 2, 3)
+        xs(1, 1, 512)
+        tanh(1, 3, 4)
+        xs(1, 2, 512)
+        xs(1, 3, 512)
+        y_acc.extend([psum.tile([P, PAIRS], F32, name="yacc%d" % n, tag="bank", bufs=8) for n in range(N // P)])
+        halves = ((0, 256), (256, 512))
+        for m0, m1 in halves:
+            zs_v(1, 3, m0, m1)
+        for m0, m1 in halves:
+            weave_c(z_bf[1], z_scaled, m0, m1)
+        for m0, m1 in halves:
+            quantize(z_mx[1], z_bf[1], m0, m1)
+        z_pass(1, True)
+        quantize(z_mx[0], z_bf[0], 0, 512)
+        z_pass(0, False)
+        for m0, m1 in halves:
+            weave_c(x_bf[0], x_scaled[0], m0, m1)
+        for m0, m1 in halves:
+            quantize(x_mx[0], x_bf[0], m0, m1)
         x_pass(0, False, [0])
-        quantize(z_mx[1], z_bf[1], 0, 512)
-        z_pass(1, False)
-        weave_v(x_bf[1], th4[1], gt_sb[:, 1, :], 256, 512)
-        weave_v(x_bf[1], th4[1], gt_sb[:, 1, :], 0, 256)
-        cast_w3(1, 2)
-        cast_w3(2, 4)
-        quantize(x_mx[1], x_bf[1], 256, 512)
-        x_pass(1, False, [0], 256, 512)
+        for m0, m1 in halves:
+            weave_c(x_bf[1], x_scaled[1], m0, m1)
         quantize(x_mx[1], x_bf[1], 0, 256)
-        x_pass(1, True, [0], 0, 256)
-        for n in range(1, 4):
+        x_pass(1, False, [0], 0, 256)
+        quantize(x_mx[1], x_bf[1], 256, 512)
+        x_pass(1, True, [0], 256, 512)
+        spread_gd(0, 2)
+
+        def weights(n):
+            cast_w3(n, n + 1)
             quantize(w3_mx, w3_bf, 256 * n, 256 * (n + 1))
             x_pass(0, False, [n])
             x_pass(1, True, [n])
 
-        y = {}
-        second = {}
-
-        def fetch(n):
-            y[n] = keep.tile([P, PAIRS], F32, name="y%d" % n)
-            nc.scalar.copy(y[n][:], y_acc[n][:])
-            second[n] = keep.tile([P, TRIADS], F32, name="second%d" % n)
-            nc.vector.tensor_copy(second[n][:], y[n][:].indirect(p4[:]))
-
-        def finish(n):
-            weighted = keep.tile([P, TRIADS], F32, name="weighted%d" % n)
-            nc.scalar.activation(weighted[:], second[n][:], ACT.Copy, scale=gd_sb[:, n : n + 1])
+        def scores(n):
+            y = keep.tile([P, PAIRS], F32, name="y%d" % n)
+            nc.scalar.copy(y[:], y_acc[n][:])
+            second = keep.tile([P, TRIADS], F32, name="second%d" % n)
             res = keep.tile([P, TRIADS], F32, name="res%d" % n)
-            nc.vector.tensor_tensor(res[:], y[n][:].indirect(p3[:]), weighted[:], ALU.subtract)
+            for u in range(2):
+                cols = slice(128 * u, 128 * (u + 1))
+                nc.vector.tensor_tensor(
+                    second[:, cols], y[:].indirect(p4[:, 8 * u : 8 * (u + 1)]), gd_wide[:, n, cols], ALU.mult
+                )
+            for u in range(2):
+                cols = slice(128 * u, 128 * (u + 1))
+                nc.vector.tensor_tensor(
+                    res[:, cols], y[:].indirect(p3[:, 8 * u : 8 * (u + 1)]), second[:, cols], ALU.subtract
+                )
             nc.sync.dma_start(out[P * n : P * (n + 1), :], res[:])
 
-        fetch(0)
-        for n in range(1, N // P):
-            fetch(n)
-            finish(n - 1)
-        finish(N // P - 1)
+        weights(1)
+        weights(2)
+        weights(3)
+        scores(0)
+        spread_gd(2, 4)
+        scores(1)
+        scores(2)
+        scores(3)

@@ -83,12 +83,12 @@ def tile_list_friend_triad_scores_kernel(
         p1 = load_list(pos1, "p1")
         p2 = load_list(pos2, "p2")
         w1_raw[1, 0] = load_w(w1, 0, 512, 1024, "w1raw10", 0)
-        w1_raw[1, 1] = load_w(w1, 1, 512, 1024, "w1raw11", 8192)
         gz_sb = keep.tile([P, 2, PACK], F32, name="gz_sb")
         gt_sb = keep.tile([P, 2, PACK], F32, name="gt_sb")
         gd_sb = keep.tile([P, N // P], F32, name="gd_sb")
         nc.sync.dma_start(gz_sb[:], gz.rearrange("(b p t) -> p b t", p=P, t=PACK))
         nc.sync.dma_start(gt_sb[:], gt.rearrange("(b p t) -> p b t", p=P, t=PACK))
+        w1_raw[1, 1] = load_w(w1, 1, 512, 1024, "w1raw11", 8192)
         w3_raw = [load_w(w3, a, 0, N, "w3raw%d" % a) for a in range(2)]
         w2_w = keep.tile([P, 2, 2 * N], U8, name="w2_w", align_bytes=64)
         nc.sync.dma_start(w2_w[:].bitcast(I32), w2_words.rearrange("a p c -> p a c").bitcast(I32))
@@ -114,12 +114,26 @@ def tile_list_friend_triad_scores_kernel(
 
         w1_bf = {}
         w1_mx = {}
-        for b in range(2):
-            for a in range(2):
-                w1_bf[b, a] = keep.tile([P, PACK * BANK], BF16, name="w1bf%d%d" % (b, a), align_bytes=64)
-                w1_mx[b, a] = mx_tiles("w1_%d%d" % (b, a))
+        for a in range(2):
+            w1_bf[1, a] = keep.tile([P, PACK * BANK], BF16, name="w1bf1%d" % a, align_bytes=64)
+            w1_mx[1, a] = mx_tiles("w1_1%d" % a)
+        first_bf = keep.tile([P, 2 * PACK * BANK], BF16, name="first_bf", align_bytes=64)
+        first_mx = (
+            keep.tile([P, 2 * BANK], U32, name="first_codes", align_bytes=64),
+            keep.tile([P, 2 * BANK], U8, name="first_scales", align_bytes=64),
+        )
 
-        cast_w1("s", w1_bf[0, 0], w1_raw[0, 0], 0, 80)
+        def cast_first(eng, u, a, raw, m0, m1, first=0):
+            section = first_bf[:, 1024 * (2 * u + a) : 1024 * (2 * u + a + 1)]
+            dst = section.rearrange("p (e m j) -> p m j e", e=2, j=PACK)[:, m0:m1]
+            src = raw[:].rearrange("p j (m t) -> p m j t", t=PACK)[:, m0 - first : m1 - first, :, 2 * u : 2 * u + 2]
+            if eng == "v":
+                nc.vector.tensor_copy(dst, src)
+            else:
+                nc.scalar.copy(dst, src)
+
+        cast_first("s", 0, 0, w1_raw[0, 0], 0, 128)
+        cast_first("s", 1, 0, w1_raw[0, 0], 0, 128)
         got_w = []
         for a in range(2):
             g = keep.tile([P, S], U32, name="got_w%d" % a, align_bytes=64)
@@ -127,35 +141,42 @@ def tile_list_friend_triad_scores_kernel(
             got_w.append(g)
             if a == 0:
                 nc.vector.tensor_copy(got_sc[:], tab_sc[:].indirect(idx[:]))
-                cast_w1("v", w1_bf[0, 0], w1_raw[0, 0], 80, 128)
-                quantize(w1_mx[0, 0], w1_bf[0, 0], 0, 512)
-        cast_w1("s", w1_bf[0, 1], w1_last[0], 0, 64)
-        cast_w1("s", w1_bf[0, 1], w1_last[1], 64, 88, 64)
-        cast_w1("v", w1_bf[0, 1], w1_last[1], 88, 128, 64)
-        quantize(w1_mx[0, 1], w1_bf[0, 1], 0, 128)
-        quantize(w1_mx[0, 1], w1_bf[0, 1], 128, 256)
-        quantize(w1_mx[0, 1], w1_bf[0, 1], 256, 512)
+                quantize(first_mx, first_bf, 0, 256)
+        cast_first("s", 0, 1, w1_last[0], 0, 64)
+        cast_first("s", 1, 1, w1_last[0], 0, 64)
+        cast_first("v", 0, 1, w1_last[1], 64, 128, 64)
+        cast_first("s", 1, 1, w1_last[1], 64, 128, 64)
+        quantize(first_mx, first_bf, 256, 384)
+        quantize(first_mx, first_bf, 384, 512)
+        quantize(first_mx, first_bf, 512, 1024)
+
+        def stationary(b, t, a):
+            if b == 0:
+                c0 = 256 * (2 * (t // 2) + a) + P * (t % 2)
+                return first_mx[0][:, c0 : c0 + P], first_mx[1][:, c0 : c0 + P]
+            return w1_mx[b, a][0][:, P * t : P * (t + 1)], w1_mx[b, a][1][:, P * t : P * (t + 1)]
 
         def stage1(b, t):
             if b == 0 and t >= 2:
                 h = shared.tile([P, S], F32, name="h_shared%d" % t, offset=8192 * (t - 2))
             else:
                 h = ring.tile([P, S], F32, name="h", bufs=4)
-            for half in range(2):
-                acc = psum.tile([P, BANK], F32, name="hacc", tag="bank", bufs=8)
-                cols = slice(BANK * half, BANK * (half + 1))
-                rows = slice(P * t, P * (t + 1))
+            width = 256 if (b, t) == (0, 0) else BANK
+            for part in range(S // width):
+                acc = psum.tile([P, width], F32, name="hacc", tag="bank", bufs=8)
+                cols = slice(width * part, width * (part + 1))
                 for a in range(2):
+                    codes, scales = stationary(b, t, a)
                     nc.tensor.matmul_mx(
                         out=acc[:],
-                        lhsT=w1_mx[b, a][0][:, rows].bitcast(FP8X4),
-                        lhsT_scale=w1_mx[b, a][1][:, rows],
+                        lhsT=codes.bitcast(FP8X4),
+                        lhsT_scale=scales,
                         rhs=got_w[a][:, cols].bitcast(FP8X4),
                         rhs_scale=got_sc[4 * a : P, cols],
                         start=(a == 0),
                         stop=(a == 1),
                     )
-                if (b, t, half) == (0, 0, 1):
+                if (b, t) == (0, 0) and part % 2 == 1:
                     nc.vector.tensor_copy(h[:, cols], acc[:])
                 else:
                     nc.scalar.copy(h[:, cols], acc[:])
@@ -272,10 +293,6 @@ def tile_list_friend_triad_scores_kernel(
             else:
                 nc.scalar.copy(dst, src)
 
-        gd_wide = keep.tile([P, N // P, TRIADS], F32, name="gd_wide")
-
-        def spread_gd(n0, n1):
-            nc.scalar.copy(gd_wide[:, n0:n1, :], gd_sb[:, n0:n1].unsqueeze(2).to_broadcast([P, n1 - n0, TRIADS]))
 
         h0 = stage1(0, 0)
         h1 = stage1(0, 1)
@@ -286,7 +303,8 @@ def tile_list_friend_triad_scores_kernel(
         pair(0, 1, h1)
         zs(0, 1)
         quantize(w1_mx[1, 0], w1_bf[1, 0], 0, 512)
-        cast_w1("s", w1_bf[1, 1], w1_raw[1, 1], 0, 128)
+        cast_w1("s", w1_bf[1, 1], w1_raw[1, 1], 0, 48)
+        cast_w1("s", w1_bf[1, 1], w1_raw[1, 1], 48, 128)
         h3 = stage1(0, 3)
         pair(0, 2, h2)
         zs(0, 2)
@@ -305,23 +323,25 @@ def tile_list_friend_triad_scores_kernel(
         h6 = stage1(1, 2)
         pair(1, 2, h6)
         zs(1, 2)
-        cast_w3(0, 1)
-        quantize(w3_mx, w3_bf, 0, 256)
+        weave_words("s", z_bf[0], z_pairs)
+        quantize(z_mx[0], z_bf[0], 0, 512)
         h7 = stage1(1, 3)
+        y_acc.extend([psum.tile([P, PAIRS], F32, name="yacc%d" % n, tag="bank", bufs=8) for n in range(N // P)])
+        z_pass(0, True)
         pair(1, 3, h7)
         tanh(0, 2, 4)
-        weave_words("s", z_bf[0], z_pairs)
+        cast_w3(0, 1)
         tanh(1, 0, 1)
         xs(0, 2, 512)
         xs(0, 3, 512)
         tanh(1, 1, 2)
+        weave_s(x_bf[0], x_scaled[0], 0, 256)
         xs(1, 0, 512)
         tanh(1, 2, 3)
         xs(1, 1, 512)
         tanh(1, 3, 4)
         xs(1, 2, 512)
         xs(1, 3, 512)
-        y_acc.extend([psum.tile([P, PAIRS], F32, name="yacc%d" % n, tag="bank", bufs=8) for n in range(N // P)])
         halves = ((0, 256), (256, 512))
         for m0, m1 in halves:
             zs_v(1, 3, m0, m1)
@@ -329,13 +349,10 @@ def tile_list_friend_triad_scores_kernel(
             weave_c(z_bf[1], z_scaled, m0, m1)
         for m0, m1 in halves:
             quantize(z_mx[1], z_bf[1], m0, m1)
-        z_pass(1, True)
-        quantize(z_mx[0], z_bf[0], 0, 512)
-        z_pass(0, False)
-        for m0, m1 in halves:
-            weave_c(x_bf[0], x_scaled[0], m0, m1)
-        for m0, m1 in halves:
-            quantize(x_mx[0], x_bf[0], m0, m1)
+        z_pass(1, False)
+        weave_c(x_bf[0], x_scaled[0], 256, 512)
+        quantize(w3_mx, w3_bf, 0, 256)
+        quantize(x_mx[0], x_bf[0], 0, 512)
         x_pass(0, False, [0])
         for m0, m1 in halves:
             weave_c(x_bf[1], x_scaled[1], m0, m1)
@@ -343,7 +360,6 @@ def tile_list_friend_triad_scores_kernel(
         x_pass(1, False, [0], 0, 256)
         quantize(x_mx[1], x_bf[1], 256, 512)
         x_pass(1, True, [0], 256, 512)
-        spread_gd(0, 2)
 
         def weights(n):
             cast_w3(n, n + 1)
@@ -351,28 +367,30 @@ def tile_list_friend_triad_scores_kernel(
             x_pass(0, False, [n])
             x_pass(1, True, [n])
 
-        def scores(n):
-            y = keep.tile([P, PAIRS], F32, name="y%d" % n)
-            nc.scalar.copy(y[:], y_acc[n][:])
-            second = keep.tile([P, TRIADS], F32, name="second%d" % n)
+        y = {}
+        second = {}
+
+        def fetch(n):
+            y[n] = keep.tile([P, PAIRS], F32, name="y%d" % n)
+            nc.scalar.copy(y[n][:], y_acc[n][:])
+            second[n] = keep.tile([P, TRIADS], F32, name="second%d" % n)
+            nc.vector.tensor_copy(second[n][:], y[n][:].indirect(p4[:]))
+
+        def finish(n):
+            weighted = keep.tile([P, TRIADS], F32, name="weighted%d" % n)
+            nc.scalar.activation(weighted[:], second[n][:], ACT.Copy, scale=gd_sb[:, n : n + 1])
             res = keep.tile([P, TRIADS], F32, name="res%d" % n)
-            for u in range(2):
-                cols = slice(128 * u, 128 * (u + 1))
-                nc.vector.tensor_tensor(
-                    second[:, cols], y[:].indirect(p4[:, 8 * u : 8 * (u + 1)]), gd_wide[:, n, cols], ALU.mult
-                )
-            for u in range(2):
-                cols = slice(128 * u, 128 * (u + 1))
-                nc.vector.tensor_tensor(
-                    res[:, cols], y[:].indirect(p3[:, 8 * u : 8 * (u + 1)]), second[:, cols], ALU.subtract
-                )
+            nc.vector.tensor_tensor(res[:], y[n][:].indirect(p3[:]), weighted[:], ALU.subtract)
             nc.sync.dma_start(out[P * n : P * (n + 1), :], res[:])
 
         weights(1)
         weights(2)
         weights(3)
-        scores(0)
-        spread_gd(2, 4)
-        scores(1)
-        scores(2)
-        scores(3)
+        fetch(0)
+        fetch(1)
+        finish(0)
+        fetch(2)
+        finish(1)
+        fetch(3)
+        finish(2)
+        finish(3)

@@ -182,24 +182,33 @@ def tile_list_friend_triad_scores_kernel(
                     nc.scalar.copy(h[:, cols], acc[:])
             return h
 
-        f4 = [keep.tile([P, PACK, PAIRS], F32, name="f4_%d" % b) for b in range(2)]
+        f_first = keep.tile([P, PACK, PAIRS], F32, name="f_first")
+        f = {(0, t): f_first[:, t, :] for t in range(PACK)}
         th = {(b, u): keep.tile([P, 2, PAIRS], F32, name="th%d%d" % (b, u)) for b, u in ((0, 1), (1, 0), (1, 1))}
 
+        f_done = []
+
         def pair(b, t, h):
-            left = ring.tile([P, PAIRS], F32, name="left")
+            left = shared.tile([P, PAIRS], F32, name="left%d%d" % (b, t), offset=16384 + 2048 * (len(f_done) % 2))
+            f_done.append((b, t))
+            if b == 1:
+                f[b, t] = keep.tile([P, PAIRS], F32, name="f_second", tag="f_second%d" % min(t, 2))[:]
             for u in range(2):
                 nc.vector.tensor_copy(left[:, 256 * u : 256 * (u + 1)], h[:].indirect(p1[:, 16 * u : 16 * (u + 1)]))
             for u in range(2):
                 cols = slice(256 * u, 256 * (u + 1))
                 nc.vector.tensor_tensor(
-                    f4[b][:, t, cols], h[:].indirect(p2[:, 16 * u : 16 * (u + 1)]), left[:, cols], ALU.mult
+                    f[b, t][:, cols], h[:].indirect(p2[:, 16 * u : 16 * (u + 1)]), left[:, cols], ALU.mult
                 )
 
         def tanh(b, t0, t1):
             if (b, t0) == (0, 0):
                 th[0, 0] = shared.tile([P, 2, PAIRS], F32, name="th00", offset=8192 + 4096)
             u = t0 // 2
-            nc.scalar.activation(th[b, u][:, t0 - 2 * u : t1 - 2 * u, :], f4[b][:, t0:t1, :], ACT.Tanh)
+            if b == 0:
+                nc.scalar.activation(th[b, u][:], f_first[:, t0:t1, :], ACT.Tanh)
+            else:
+                nc.scalar.activation(th[b, u][:, t0 % 2, :], f[b, t0], ACT.Tanh)
 
         def weave_v(grouped, planes, gain, m0, m1):
             nc.vector.tensor_tensor(
@@ -227,20 +236,28 @@ def tile_list_friend_triad_scores_kernel(
                 scaled[:, :, m0:m1].rearrange("p t (c i) -> p c t i", i=4),
             )
 
-        def cast_w3(n0, n1):
+        w3_bf = {}
+
+        def cast_w3(n, eng="s"):
+            if eng == "s":
+                w3_bf[n] = keep.tile([P, 2 * PACK * P], BF16, name="w3_bf%d" % n, align_bytes=64)
+            else:
+                w3_bf[n] = shared.tile([P, 2 * PACK * P], BF16, name="w3_bf%d" % n, align_bytes=64, offset=16384 + 2048)
             for a in range(2):
-                nc.scalar.copy(
-                    w3_bf[:].rearrange("p (n a c i j) -> p n a c j i", a=2, c=P // 2, i=2, j=PACK)[:, n0:n1, a],
-                    w3_raw[a][:].rearrange("p j (n c i) -> p n c j i", c=P // 2, i=2)[:, n0:n1],
+                (nc.scalar.copy if eng == "s" else nc.vector.tensor_copy)(
+                    w3_bf[n][:].rearrange("p (a c i j) -> p a c j i", a=2, i=2, j=PACK)[:, a],
+                    w3_raw[a][:].rearrange("p j (n c i) -> p n c j i", c=P // 2, i=2)[:, n],
                 )
 
+        def quantize_w3(n):
+            cols = slice(256 * n, 256 * (n + 1))
+            nc.vector.quantize_mx(out=w3_mx[0][:, cols].bitcast(FP8X4), scales=w3_mx[1][:, cols], in_=w3_bf[n][:])
+
         z_bf = [keep.tile([P, PACK * PAIRS], BF16, name="z_bf%d" % b, align_bytes=64) for b in range(2)]
-        z_pairs = keep.tile([P, 2, PAIRS, 2], BF16, name="z_pairs")
-        z_scaled = keep.tile([P, PACK, PAIRS], BF16, name="z_scaled")
+        z_pairs = [keep.tile([P, 2, PAIRS, 2], BF16, name="z_pairs%d" % b) for b in range(2)]
         x_bf = [keep.tile([P, PACK * PAIRS], BF16, name="x_bf%d" % b, align_bytes=64) for b in range(2)]
         z_mx = [mx_tiles("z%d" % b) for b in range(2)]
         x_mx = [mx_tiles("x%d" % b) for b in range(2)]
-        w3_bf = keep.tile([P, 2 * PACK * N], BF16, name="w3_bf", align_bytes=64)
         w3_mx = (
             keep.tile([P, 2 * N], U32, name="w3_codes", align_bytes=64),
             keep.tile([P, 2 * N], U8, name="w3_scales", align_bytes=64),
@@ -273,8 +290,8 @@ def tile_list_friend_triad_scores_kernel(
                 )
 
         def zs(b, t):
-            dst = z_pairs[:, t // 2, :, t % 2] if b == 0 else z_scaled[:, t, :]
-            nc.gpsimd.tensor_scalar(dst, f4[b][:, t, :], gz_sb[:, b, t : t + 1], 0.0, ALU.mult, ALU.add)
+            dst = z_pairs[b][:, t // 2, :, t % 2]
+            nc.gpsimd.tensor_scalar(dst, f[b, t], gz_sb[:, b, t : t + 1], 0.0, ALU.mult, ALU.add)
 
         def xs(b, t, m1):
             nc.scalar.activation(
@@ -282,12 +299,12 @@ def tile_list_friend_triad_scores_kernel(
             )
 
         def zs_v(b, t, m0, m1):
-            nc.vector.tensor_scalar(z_scaled[:, t, m0:m1], f4[b][:, t, m0:m1], gz_sb[:, b, t : t + 1], None, ALU.mult)
+            nc.vector.tensor_scalar(z_pairs[b][:, t // 2, m0:m1, t % 2], f[b, t][:, m0:m1], gz_sb[:, b, t : t + 1], None, ALU.mult)
 
-        def weave_words(eng, grouped, pairs):
+        def weave_words(eng, grouped, pairs, m0, m1):
             word = I32 if eng == "v" else U32
-            dst = grouped[:].bitcast(word).rearrange("p (m u) -> p m u", u=2)
-            src = pairs[:].rearrange("p u m e -> p u (m e)").bitcast(word).rearrange("p u m -> p m u")
+            dst = grouped[:].bitcast(word).rearrange("p (m u) -> p m u", u=2)[:, m0:m1]
+            src = pairs[:].rearrange("p u m e -> p u (m e)").bitcast(word).rearrange("p u m -> p m u")[:, m0:m1]
             if eng == "v":
                 nc.vector.tensor_copy(dst, src)
             else:
@@ -312,47 +329,48 @@ def tile_list_friend_triad_scores_kernel(
         pair(0, 3, h3)
         zs(0, 3)
         tanh(0, 0, 2)
-        h4 = stage1(1, 0)
-        pair(1, 0, h4)
+        h4 = stage1(1, 2)
+        pair(1, 2, h4)
+        zs(1, 2)
+        h5 = stage1(1, 0)
+        pair(1, 0, h5)
         zs(1, 0)
-        h5 = stage1(1, 1)
-        pair(1, 1, h5)
-        zs(1, 1)
         xs(0, 0, 512)
         xs(0, 1, 512)
-        h6 = stage1(1, 2)
-        pair(1, 2, h6)
-        zs(1, 2)
-        weave_words("s", z_bf[0], z_pairs)
+        h6 = stage1(1, 1)
+        pair(1, 1, h6)
+        zs(1, 1)
+        weave_words("s", z_bf[0], z_pairs[0], 0, 512)
         quantize(z_mx[0], z_bf[0], 0, 512)
+        tanh(1, 2, 3)
         h7 = stage1(1, 3)
         y_acc.extend([psum.tile([P, PAIRS], F32, name="yacc%d" % n, tag="bank", bufs=8) for n in range(N // P)])
         z_pass(0, True)
         pair(1, 3, h7)
         tanh(0, 2, 4)
-        cast_w3(0, 1)
-        tanh(1, 0, 1)
+        cast_w3(0)
         xs(0, 2, 512)
         xs(0, 3, 512)
-        tanh(1, 1, 2)
-        weave_s(x_bf[0], x_scaled[0], 0, 256)
-        xs(1, 0, 512)
-        tanh(1, 2, 3)
-        xs(1, 1, 512)
-        tanh(1, 3, 4)
+        tanh(1, 0, 1)
         xs(1, 2, 512)
+        tanh(1, 1, 2)
+        xs(1, 0, 512)
+        tanh(1, 3, 4)
+        xs(1, 1, 512)
         xs(1, 3, 512)
         halves = ((0, 256), (256, 512))
         for m0, m1 in halves:
             zs_v(1, 3, m0, m1)
         for m0, m1 in halves:
-            weave_c(z_bf[1], z_scaled, m0, m1)
+            weave_words("v", z_bf[1], z_pairs[1], m0, m1)
         for m0, m1 in halves:
             quantize(z_mx[1], z_bf[1], m0, m1)
         z_pass(1, False)
-        weave_c(x_bf[0], x_scaled[0], 256, 512)
-        quantize(w3_mx, w3_bf, 0, 256)
-        quantize(x_mx[0], x_bf[0], 0, 512)
+        quantize_w3(0)
+        for m0, m1 in halves:
+            weave_c(x_bf[0], x_scaled[0], m0, m1)
+        for m0, m1 in halves:
+            quantize(x_mx[0], x_bf[0], m0, m1)
         x_pass(0, False, [0])
         for m0, m1 in halves:
             weave_c(x_bf[1], x_scaled[1], m0, m1)
@@ -362,8 +380,8 @@ def tile_list_friend_triad_scores_kernel(
         x_pass(1, True, [0], 256, 512)
 
         def weights(n):
-            cast_w3(n, n + 1)
-            quantize(w3_mx, w3_bf, 256 * n, 256 * (n + 1))
+            cast_w3(n)
+            quantize_w3(n)
             x_pass(0, False, [n])
             x_pass(1, True, [n])
 

@@ -17,6 +17,7 @@ ALU = mybir.AluOpType
 ACT = mybir.ActivationFunctionType
 
 P = 128
+HALF = 64
 PACK = 4
 PASS = P * PACK
 BANK = 512
@@ -38,15 +39,24 @@ def tile_list_friend_triad_scores_kernel(
             nc.sync.dma_start(t[:], src)
             return t
 
-        def mx_tiles(name):
-            codes = keep.tile([P, BANK], U32, name=name + "_codes", align_bytes=64)
-            scales = keep.tile([P, BANK], U8, name=name + "_scales", align_bytes=64)
+        def mx_tiles(name, width, offset=None):
+            if offset is None:
+                codes = keep.tile([P, width], U32, name=name + "_codes", align_bytes=64)
+            else:
+                codes = shared.tile([P, width], U32, name=name + "_codes", align_bytes=64, offset=offset)
+            scales = keep.tile([P, width], U8, name=name + "_scales", align_bytes=64)
             return codes, scales
 
         def quantize(mx, grouped, c0, c1):
             nc.vector.quantize_mx(
                 out=mx[0][:, c0:c1].bitcast(FP8X4), scales=mx[1][:, c0:c1], in_=grouped[:, PACK * c0 : PACK * c1]
             )
+
+        def copy_on(eng, dst, src):
+            if eng == "v":
+                nc.vector.tensor_copy(dst, src)
+            else:
+                nc.scalar.copy(dst, src)
 
         tab_sc = keep.tile([P, T], U8, name="tab_sc", align_bytes=64)
         nc.gpsimd.memset(tab_sc[:].bitcast(I32), 0)
@@ -59,16 +69,27 @@ def tile_list_friend_triad_scores_kernel(
 
         idx = load_list(offs, "idx")
 
-        def load_w(src, a, c0, c1, name, offset=None):
-            if offset is None:
-                raw = keep.tile([P, PACK, c1 - c0], F32, name=name)
-            else:
-                raw = shared.tile([P, PACK, c1 - c0], F32, name=name, offset=offset)
+        def load_w(src, a, c0, c1, name, offset):
+            raw = shared.tile([P, PACK, c1 - c0], F32, name=name, offset=offset)
             nc.sync.dma_start(raw[:], src[PASS * a : PASS * (a + 1), c0:c1].rearrange("(p j) c -> p j c", j=PACK))
             return raw
 
-        w1_raw = {}
+        def load_gain(src, name):
+            mixed = keep.tile([P, 2, 2], F32, name=name + "_mixed")
+            for s in range(2):
+                nc.sync.dma_start(
+                    mixed[HALF * s : HALF * (s + 1)],
+                    src[0:PASS].rearrange("(u w t) -> w u t", u=2, t=PACK)[:, :, 2 * s : 2 * s + 2],
+                )
+            return mixed
+
+        def load_gain_plain(src, name):
+            plain = keep.tile([P, PACK], F32, name=name + "_plain")
+            nc.sync.dma_start(plain[:], src[PASS : 2 * PASS].rearrange("(p t) -> p t", t=PACK))
+            return plain
+
         tab_w = []
+        quarter_raw = {}
         for a in range(2):
             t = keep.tile([P, T], I32, name="tab_w%d" % a, align_bytes=64)
             nc.sync.dma_start(t[:], tab_words[a].rearrange("p t i -> p (t i)").bitcast(I32))
@@ -78,18 +99,18 @@ def tile_list_friend_triad_scores_kernel(
                     nc.sync.dma_start(
                         tab_sc[32 * q : 32 * q + 8, :].bitcast(I32), tab_scales[:, 4 * q : 4 * q + 4, :].bitcast(I32)
                     )
-                w1_raw[0, 0] = load_w(w1, 0, 0, 512, "w1raw00")
-        w1_last = [load_w(w1, 1, 256 * u, 256 * (u + 1), "w1raw01_%d" % u) for u in range(2)]
+                first_raw = load_w(w1, 0, 0, 512, "firstraw", 0)
+        quarter_raw[0] = load_w(w1, 1, 0, 256, "q0raw", 8192)
         p1 = load_list(pos1, "p1")
         p2 = load_list(pos2, "p2")
-        w1_raw[1, 0] = load_w(w1, 0, 512, 1024, "w1raw10", 0)
-        gz_sb = keep.tile([P, 2, PACK], F32, name="gz_sb")
-        gt_sb = keep.tile([P, 2, PACK], F32, name="gt_sb")
-        gd_sb = keep.tile([P, N // P], F32, name="gd_sb")
-        nc.sync.dma_start(gz_sb[:], gz.rearrange("(b p t) -> p b t", p=P, t=PACK))
-        nc.sync.dma_start(gt_sb[:], gt.rearrange("(b p t) -> p b t", p=P, t=PACK))
-        w1_raw[1, 1] = load_w(w1, 1, 512, 1024, "w1raw11", 8192)
-        w3_raw = [load_w(w3, a, 0, N, "w3raw%d" % a) for a in range(2)]
+        quarter_raw[1] = load_w(w1, 1, 256, 512, "q1raw", 12288)
+        gz_mixed = load_gain(gz, "gz")
+        half_raw = [load_w(w1, 0, 512, 1024, "halfraw0", 16384)]
+        gt_mixed = load_gain(gt, "gt")
+        half_raw.append(load_w(w1, 1, 512, 1024, "halfraw1", 24576))
+        gz_plain = load_gain_plain(gz, "gz")
+        gt_plain = load_gain_plain(gt, "gt")
+        w3_raw = [load_w(w3, a, 0, N, "w3raw%d" % a, 32768 + 8192 * a) for a in range(2)]
         w2_w = keep.tile([P, 2, 2 * N], U8, name="w2_w", align_bytes=64)
         nc.sync.dma_start(w2_w[:].bitcast(I32), w2_words.rearrange("a p c -> p a c").bitcast(I32))
         for q in range(4):
@@ -97,43 +118,70 @@ def tile_list_friend_triad_scores_kernel(
                 w2_sc[32 * q : 32 * q + 4, :, :].bitcast(I32),
                 w2_scales[:, 4 * q : 4 * q + 4, :].rearrange("a r c -> r a c").bitcast(I32),
             )
+        gd_sb = keep.tile([P, N // P], F32, name="gd_sb")
         with nc.allow_non_contiguous_dma(reason="one weight a partition"):
             nc.sync.dma_start(gd_sb[:], gd.rearrange("(n p) -> p n", p=P))
         p3 = load_list(pos3, "p3")
         p4 = load_list(pos4, "p4")
 
-        got_sc = keep.tile([P, S], U8, name="got_sc", align_bytes=64)
-
-        def cast_w1(eng, grouped, raw, m0, m1, first=0):
-            dst = grouped[:].rearrange("p (t m j) -> p m j t", t=PACK, j=PACK)[:, m0:m1]
-            src = raw[:].rearrange("p j (m t) -> p m j t", t=PACK)[:, m0 - first : m1 - first]
-            if eng == "v":
-                nc.vector.tensor_copy(dst, src)
-            else:
-                nc.scalar.copy(dst, src)
+        def slot(k):
+            return 49152 + int(2048 * k)
 
         w1_bf = {}
         w1_mx = {}
-        for a in range(2):
-            w1_bf[1, a] = keep.tile([P, PACK * BANK], BF16, name="w1bf1%d" % a, align_bytes=64)
-            w1_mx[1, a] = mx_tiles("w1_1%d" % a)
-        first_bf = keep.tile([P, 2 * PACK * BANK], BF16, name="first_bf", align_bytes=64)
-        first_mx = (
-            keep.tile([P, 2 * BANK], U32, name="first_codes", align_bytes=64),
-            keep.tile([P, 2 * BANK], U8, name="first_scales", align_bytes=64),
-        )
+        w1_width = {}
 
-        def cast_first(eng, u, a, raw, m0, m1, first=0):
-            section = first_bf[:, 1024 * (2 * u + a) : 1024 * (2 * u + a + 1)]
-            dst = section.rearrange("p (e m j) -> p m j e", e=2, j=PACK)[:, m0:m1]
-            src = raw[:].rearrange("p j (m t) -> p m j t", t=PACK)[:, m0 - first : m1 - first, :, 2 * u : 2 * u + 2]
-            if eng == "v":
-                nc.vector.tensor_copy(dst, src)
+        def w1_unit(key, width, bf_slot, codes_slot):
+            name = "w1_" + "".join(str(k) for k in key)
+            if bf_slot is None:
+                w1_bf[key] = keep.tile([P, PACK * width], BF16, name=name + "_bf", align_bytes=64)
             else:
-                nc.scalar.copy(dst, src)
+                w1_bf[key] = shared.tile([P, PACK * width], BF16, name=name + "_bf", align_bytes=64, offset=slot(bf_slot))
+            w1_mx[key] = mx_tiles(name, width, None if codes_slot is None else slot(codes_slot))
+            w1_width[key] = width
 
-        cast_first("s", 0, 0, w1_raw[0, 0], 0, 128)
-        cast_first("s", 1, 0, w1_raw[0, 0], 0, 128)
+        def cast_both(key, raw):
+            dst = w1_bf[key][:].rearrange("p (e s w j) -> p w j s e", e=2, s=2, j=PACK)
+            nc.scalar.copy(dst, raw.rearrange("p j (w s e) -> p w j s e", s=2, e=2))
+
+        def cast_pool(key, raw, e):
+            dst = w1_bf[key][:].rearrange("p (e s w j) -> p e w j s", e=2, s=2, j=PACK)[:, e]
+            src = raw.rearrange("p j (w s e) -> p w j s e", s=2, e=2)[:, :, :, :, e]
+            nc.gpsimd.tensor_scalar(dst, src, 1.0, 0.0, ALU.mult, ALU.add)
+
+        def cast_plain(key, raw):
+            dst = w1_bf[key][:].rearrange("p (t w j) -> p w j t", t=PACK, j=PACK)
+            nc.scalar.copy(dst, raw.rearrange("p j (w t) -> p w j t", t=PACK))
+
+        def cast_one(key, raw, e, w0, w1):
+            dst = w1_bf[key][:].rearrange("p (s w j) -> p w j s", s=2, j=PACK)[:, w0:w1]
+            nc.scalar.copy(dst, raw.rearrange("p j (w s e) -> p w j s e", s=2, e=2)[:, w0:w1, :, :, e])
+
+        def stationary(tile, a):
+            u, e = tile
+            if (u, a) == (0, 1):
+                key, c0 = (0, 1, e), 0
+            elif u < 2:
+                key, c0 = (u, a), P * e
+            elif a == 0:
+                key, c0 = (2, 0), P * e
+            else:
+                key, c0 = (2, 1, e % 2), P * (e // 2)
+            return w1_mx[key][0][:, c0 : c0 + P], w1_mx[key][1][:, c0 : c0 + P]
+
+        w1_unit((0, 0), 256, None, None)
+        w1_unit((0, 1, 0), P, 5, 0)
+        w1_unit((0, 1, 1), P, None, 10)
+        w1_unit((1, 0), 256, None, 5)
+        w1_unit((1, 1), 256, 0, None)
+        w1_unit((2, 0), 512, 10, None)
+        w1_unit((2, 1, 0), 256, 1, None)
+        w1_unit((2, 1, 1), 256, 8.5, None)
+
+        def quantize_w1(key):
+            quantize(w1_mx[key], w1_bf[key], 0, w1_width[key])
+
+        got_sc = keep.tile([P, S], U8, name="got_sc", align_bytes=64)
         got_w = []
         for a in range(2):
             g = keep.tile([P, S], U32, name="got_w%d" % a, align_bytes=64)
@@ -141,32 +189,20 @@ def tile_list_friend_triad_scores_kernel(
             got_w.append(g)
             if a == 0:
                 nc.vector.tensor_copy(got_sc[:], tab_sc[:].indirect(idx[:]))
-                quantize(first_mx, first_bf, 0, 256)
-        cast_first("s", 0, 1, w1_last[0], 0, 64)
-        cast_first("s", 1, 1, w1_last[0], 0, 64)
-        cast_first("v", 0, 1, w1_last[1], 64, 128, 64)
-        cast_first("s", 1, 1, w1_last[1], 64, 128, 64)
-        quantize(first_mx, first_bf, 256, 384)
-        quantize(first_mx, first_bf, 384, 512)
-        quantize(first_mx, first_bf, 512, 1024)
 
-        def stationary(b, t, a):
-            if b == 0:
-                c0 = 256 * (2 * (t // 2) + a) + P * (t % 2)
-                return first_mx[0][:, c0 : c0 + P], first_mx[1][:, c0 : c0 + P]
-            return w1_mx[b, a][0][:, P * t : P * (t + 1)], w1_mx[b, a][1][:, P * t : P * (t + 1)]
+        h_place = {(1, 0): 16384, (1, 1): 16384 + 4096, (2, 0): 24576, (2, 2): 24576 + 4096}
 
-        def stage1(b, t):
-            if b == 0 and t >= 2:
-                h = shared.tile([P, S], F32, name="h_shared%d" % t, offset=8192 * (t - 2))
+        def stage1(tile):
+            if tile in h_place:
+                h = shared.tile([P, S], F32, name="h%d%d" % tile, offset=h_place[tile])
             else:
                 h = ring.tile([P, S], F32, name="h", bufs=4)
-            width = 256 if (b, t) == (0, 0) else BANK
+            width = 256 if tile == (0, 0) else BANK
             for part in range(S // width):
                 acc = psum.tile([P, width], F32, name="hacc", tag="bank", bufs=8)
                 cols = slice(width * part, width * (part + 1))
                 for a in range(2):
-                    codes, scales = stationary(b, t, a)
+                    codes, scales = stationary(tile, a)
                     nc.tensor.matmul_mx(
                         out=acc[:],
                         lhsT=codes.bitcast(FP8X4),
@@ -176,75 +212,111 @@ def tile_list_friend_triad_scores_kernel(
                         start=(a == 0),
                         stop=(a == 1),
                     )
-                if (b, t) == (0, 0) and part % 2 == 1:
-                    nc.vector.tensor_copy(h[:, cols], acc[:])
-                else:
-                    nc.scalar.copy(h[:, cols], acc[:])
+                copy_on("v" if tile == (0, 0) and part % 2 == 1 else "s", h[:, cols], acc[:])
             return h
 
-        f_first = keep.tile([P, PACK, PAIRS], F32, name="f_first")
-        f = {(0, t): f_first[:, t, :] for t in range(PACK)}
-        th = {(b, u): keep.tile([P, 2, PAIRS], F32, name="th%d%d" % (b, u)) for b, u in ((0, 1), (1, 0), (1, 1))}
+        f = {}
+        th = {}
+        z_pairs = [keep.tile([P, 2, PAIRS, 2], BF16, name="z_pairs%d" % b) for b in range(2)]
+        x_planes = [keep.tile([P, PACK, PAIRS], BF16, name="x_planes%d" % b) for b in range(2)]
+        z_late = shared.tile([P, PAIRS, 2], BF16, name="z_late", offset=slot(3))
+        x_late = shared.tile([P, 2, PAIRS], BF16, name="x_late", offset=slot(4))
+        z_bf = {1: keep.tile([P, PACK * PAIRS], BF16, name="z_bf1", align_bytes=64)}
+        x_bf = [keep.tile([P, PACK * PAIRS], BF16, name="x_bf%d" % b, align_bytes=64) for b in range(2)]
+        z_mx = [mx_tiles("z%d" % b, PAIRS) for b in range(2)]
+        x_mx = [mx_tiles("x%d" % b, PAIRS) for b in range(2)]
+        w3_mx = mx_tiles("w3", 2 * N)
+        halves = ((0, 256), (256, 512))
 
-        f_done = []
+        def gain(mixed, plain, tile):
+            u, e = tile
+            return mixed[:, u, e : e + 1] if u < 2 else plain[:, e : e + 1]
 
-        def pair(b, t, h):
-            left = shared.tile([P, PAIRS], F32, name="left%d%d" % (b, t), offset=16384 + 2048 * (len(f_done) % 2))
-            f_done.append((b, t))
-            if b == 1:
-                f[b, t] = keep.tile([P, PAIRS], F32, name="f_second", tag="f_second%d" % min(t, 2))[:]
-            for u in range(2):
-                nc.vector.tensor_copy(left[:, 256 * u : 256 * (u + 1)], h[:].indirect(p1[:, 16 * u : 16 * (u + 1)]))
-            for u in range(2):
-                cols = slice(256 * u, 256 * (u + 1))
+        def z_place(tile):
+            u, e = tile
+            if u == 0:
+                return z_pairs[0][:, 0, :, e]
+            if u == 1:
+                return z_late[:, :, e]
+            return z_pairs[1][:, e // 2, :, e % 2]
+
+        def x_place(tile):
+            u, e = tile
+            if u == 0:
+                return x_planes[0][:, e, :]
+            if u == 1:
+                return x_late[:, e, :]
+            return x_planes[1][:, e, :]
+
+        left_slot = {(0, 1): 0.5, (1, 1): 1.5}
+
+        first_slot = {(0, 1): 0, (1, 1): 1, (2, 3): 6}
+
+        def pair(tile, h):
+            if tile in first_slot:
+                left = [shared.tile([P, 256], F32, name="first%d%d" % tile, offset=slot(first_slot[tile]))]
+            else:
+                left = [ring.tile([P, 256], F32, name="left_a", bufs=2)]
+            if tile in left_slot:
+                left.append(shared.tile([P, 256], F32, name="left%d%d" % tile, offset=slot(left_slot[tile])))
+            else:
+                left.append(ring.tile([P, 256], F32, name="left_b", bufs=2))
+            tag = "f%d%d" % (tile[0], min(tile[1], 2))
+            f[tile] = keep.tile([P, PAIRS], F32, name=tag, tag=tag)
+            for k in range(2):
+                nc.vector.tensor_copy(left[k][:], h[:].indirect(p1[:, 16 * k : 16 * (k + 1)]))
+            for k, (m0, m1) in enumerate(halves):
                 nc.vector.tensor_tensor(
-                    f[b, t][:, cols], h[:].indirect(p2[:, 16 * u : 16 * (u + 1)]), left[:, cols], ALU.mult
+                    f[tile][:, m0:m1], h[:].indirect(p2[:, 16 * k : 16 * (k + 1)]), left[k][:], ALU.mult
                 )
 
-        def tanh(b, t0, t1):
-            if (b, t0) == (0, 0):
-                th[0, 0] = shared.tile([P, 2, PAIRS], F32, name="th00", offset=8192 + 4096)
-            u = t0 // 2
-            if b == 0:
-                nc.scalar.activation(th[b, u][:], f_first[:, t0:t1, :], ACT.Tanh)
-            else:
-                nc.scalar.activation(th[b, u][:, t0 % 2, :], f[b, t0], ACT.Tanh)
+        def zs(tile):
+            nc.gpsimd.tensor_scalar(z_place(tile), f[tile][:], gain(gz_mixed, gz_plain, tile), 0.0, ALU.mult, ALU.add)
 
-        def weave_v(grouped, planes, gain, m0, m1):
-            nc.vector.tensor_tensor(
-                grouped[:, PACK * m0 : PACK * m1].rearrange("p (c i t) -> p c t i", i=2, t=PACK),
-                planes[:, :, m0:m1].rearrange("p t (c i) -> p c t i", i=2),
-                gain.unsqueeze(1).unsqueeze(3).to_broadcast([P, (m1 - m0) // 2, PACK, 2]),
-                ALU.mult,
+        def zs_v(tile, m0, m1):
+            nc.vector.tensor_scalar(
+                z_place(tile)[:, m0:m1], f[tile][:, m0:m1], gain(gz_mixed, gz_plain, tile), None, ALU.mult
             )
 
-        def scale_s(scaled, planes, gain, t, m0, m1):
-            nc.scalar.activation(scaled[:, t, m0:m1], planes[:, t, m0:m1], ACT.Copy, scale=gain[:, t : t + 1])
+        th_slot = {(0, 0): 0, (0, 1): 1, (1, 0): 0, (1, 1): 1, (2, 2): 0, (2, 0): 1, (2, 1): 0, (2, 3): 0}
 
-        def scale_g(scaled, planes, gain, t):
-            nc.gpsimd.tensor_scalar(scaled[:, t, :], planes[:, t, :], gain[:, t : t + 1], 0.0, ALU.mult, ALU.add)
+        def tanh(tile):
+            th[tile] = shared.tile([P, PAIRS], F32, name="th%d%d" % tile, offset=slot(8 + th_slot[tile]))
+            nc.scalar.activation(th[tile][:], f[tile][:], ACT.Tanh)
 
-        def weave_c(grouped, scaled, m0, m1):
+        def xs(tile):
+            nc.scalar.activation(x_place(tile), th[tile][:], ACT.Copy, scale=gain(gt_mixed, gt_plain, tile))
+
+        def move_early(rows):
+            nc.sync.dma_start(rows[0:HALF, 1], rows[HALF:P, 0])
+
+        def move_late(rows, late):
+            nc.sync.dma_start(rows[HALF:P, 1], late[HALF:P])
+            nc.sync.dma_start(rows[HALF:P, 0], late[0:HALF])
+
+        z_rows = z_pairs[0][:].rearrange("p s m e -> p s (m e)")
+        x_rows = x_planes[0][:].rearrange("p (s e) m -> p s (e m)", s=2)
+
+        def weave_planes(grouped, planes, m0, m1):
             nc.vector.tensor_copy(
                 grouped[:, PACK * m0 : PACK * m1].rearrange("p (c i t) -> p c t i", i=4, t=PACK),
-                scaled[:, :, m0:m1].rearrange("p t (c i) -> p c t i", i=4),
+                planes[:, :, m0:m1].rearrange("p t (c i) -> p c t i", i=4),
             )
 
-        def weave_s(grouped, scaled, m0, m1):
-            nc.scalar.copy(
-                grouped[:, PACK * m0 : PACK * m1].rearrange("p (c i t) -> p c t i", i=4, t=PACK),
-                scaled[:, :, m0:m1].rearrange("p t (c i) -> p c t i", i=4),
-            )
+        def weave_words(eng, grouped, pairs, m0, m1):
+            word = I32 if eng == "v" else U32
+            dst = grouped[:].bitcast(word).rearrange("p (c i u) -> p c u i", i=2, u=2)[:, m0 // 2 : m1 // 2]
+            src = pairs[:].rearrange("p u m e -> p u (m e)").bitcast(word).rearrange("p u (c i) -> p c u i", i=2)[:, m0 // 2 : m1 // 2]
+            copy_on(eng, dst, src)
 
         w3_bf = {}
 
-        def cast_w3(n, eng="s"):
-            if eng == "s":
-                w3_bf[n] = keep.tile([P, 2 * PACK * P], BF16, name="w3_bf%d" % n, align_bytes=64)
-            else:
-                w3_bf[n] = shared.tile([P, 2 * PACK * P], BF16, name="w3_bf%d" % n, align_bytes=64, offset=16384 + 2048)
+        def cast_w3(n, eng):
+            place = (slot(9), slot(3), slot(4), slot(8))[n]
+            w3_bf[n] = shared.tile([P, 2 * PACK * P], BF16, name="w3_bf%d" % n, align_bytes=64, offset=place)
             for a in range(2):
-                (nc.scalar.copy if eng == "s" else nc.vector.tensor_copy)(
+                copy_on(
+                    eng,
                     w3_bf[n][:].rearrange("p (a c i j) -> p a c j i", a=2, i=2, j=PACK)[:, a],
                     w3_raw[a][:].rearrange("p j (n c i) -> p n c j i", c=P // 2, i=2)[:, n],
                 )
@@ -253,162 +325,143 @@ def tile_list_friend_triad_scores_kernel(
             cols = slice(256 * n, 256 * (n + 1))
             nc.vector.quantize_mx(out=w3_mx[0][:, cols].bitcast(FP8X4), scales=w3_mx[1][:, cols], in_=w3_bf[n][:])
 
-        z_bf = [keep.tile([P, PACK * PAIRS], BF16, name="z_bf%d" % b, align_bytes=64) for b in range(2)]
-        z_pairs = [keep.tile([P, 2, PAIRS, 2], BF16, name="z_pairs%d" % b) for b in range(2)]
-        x_bf = [keep.tile([P, PACK * PAIRS], BF16, name="x_bf%d" % b, align_bytes=64) for b in range(2)]
-        z_mx = [mx_tiles("z%d" % b) for b in range(2)]
-        x_mx = [mx_tiles("x%d" % b) for b in range(2)]
-        w3_mx = (
-            keep.tile([P, 2 * N], U32, name="w3_codes", align_bytes=64),
-            keep.tile([P, 2 * N], U8, name="w3_scales", align_bytes=64),
-        )
-        x_scaled = [keep.tile([P, PACK, PAIRS], BF16, name="x_scaled%d" % b) for b in range(2)]
-        y_acc = []
+        y_acc = {}
+
+        def open_y():
+            for n in range(N // P):
+                for m0, m1 in halves if n == 0 else ((0, PAIRS),):
+                    y_acc[n, m0, m1] = psum.tile([P, m1 - m0], F32, name="yacc%d_%d" % (n, m0), tag="bank", bufs=8)
+
+        def y_pass(codes, scales, mx, n, start, stop, c0, c1):
+            for (tile, m0, m1), acc in y_acc.items():
+                if tile == n and c0 <= m0 and m1 <= c1:
+                    nc.tensor.matmul_mx(
+                        out=acc[:],
+                        lhsT=codes,
+                        lhsT_scale=scales,
+                        rhs=mx[0][:, m0:m1].bitcast(FP8X4),
+                        rhs_scale=mx[1][:, m0:m1],
+                        start=start,
+                        stop=stop,
+                    )
 
         def z_pass(b, start):
             for n in range(N // P):
-                nc.tensor.matmul_mx(
-                    out=y_acc[n][:],
-                    lhsT=w2_w[:, b, 2 * P * n : 2 * P * (n + 1)].bitcast(FP4X4),
-                    lhsT_scale=w2_sc[:, b, P * n : P * (n + 1)],
-                    rhs=z_mx[b][0][:].bitcast(FP8X4),
-                    rhs_scale=z_mx[b][1][:],
-                    start=start,
-                    stop=False,
-                )
+                codes = w2_w[:, b, 2 * P * n : 2 * P * (n + 1)].bitcast(FP4X4)
+                y_pass(codes, w2_sc[:, b, P * n : P * (n + 1)], z_mx[b], n, start, False, 0, PAIRS)
 
         def x_pass(b, stop, tiles, m0=0, m1=PAIRS):
             for n in tiles:
-                nc.tensor.matmul_mx(
-                    out=y_acc[n][:, m0:m1],
-                    lhsT=w3_mx[0][:, P * (2 * n + b) : P * (2 * n + b + 1)].bitcast(FP8X4),
-                    lhsT_scale=w3_mx[1][:, P * (2 * n + b) : P * (2 * n + b + 1)],
-                    rhs=x_mx[b][0][:, m0:m1].bitcast(FP8X4),
-                    rhs_scale=x_mx[b][1][:, m0:m1],
-                    start=False,
-                    stop=stop,
-                )
-
-        def zs(b, t):
-            dst = z_pairs[b][:, t // 2, :, t % 2]
-            nc.gpsimd.tensor_scalar(dst, f[b, t], gz_sb[:, b, t : t + 1], 0.0, ALU.mult, ALU.add)
-
-        def xs(b, t, m1):
-            nc.scalar.activation(
-                x_scaled[b][:, t, 0:m1], th[b, t // 2][:, t % 2, 0:m1], ACT.Copy, scale=gt_sb[:, b, t : t + 1]
-            )
-
-        def zs_v(b, t, m0, m1):
-            nc.vector.tensor_scalar(z_pairs[b][:, t // 2, m0:m1, t % 2], f[b, t][:, m0:m1], gz_sb[:, b, t : t + 1], None, ALU.mult)
-
-        def weave_words(eng, grouped, pairs, m0, m1):
-            word = I32 if eng == "v" else U32
-            dst = grouped[:].bitcast(word).rearrange("p (m u) -> p m u", u=2)[:, m0:m1]
-            src = pairs[:].rearrange("p u m e -> p u (m e)").bitcast(word).rearrange("p u m -> p m u")[:, m0:m1]
-            if eng == "v":
-                nc.vector.tensor_copy(dst, src)
-            else:
-                nc.scalar.copy(dst, src)
-
-
-        h0 = stage1(0, 0)
-        h1 = stage1(0, 1)
-        pair(0, 0, h0)
-        zs(0, 0)
-        cast_w1("s", w1_bf[1, 0], w1_raw[1, 0], 0, 128)
-        h2 = stage1(0, 2)
-        pair(0, 1, h1)
-        zs(0, 1)
-        quantize(w1_mx[1, 0], w1_bf[1, 0], 0, 512)
-        cast_w1("s", w1_bf[1, 1], w1_raw[1, 1], 0, 48)
-        cast_w1("s", w1_bf[1, 1], w1_raw[1, 1], 48, 128)
-        h3 = stage1(0, 3)
-        pair(0, 2, h2)
-        zs(0, 2)
-        quantize(w1_mx[1, 1], w1_bf[1, 1], 0, 512)
-        pair(0, 3, h3)
-        zs(0, 3)
-        tanh(0, 0, 2)
-        h4 = stage1(1, 2)
-        pair(1, 2, h4)
-        zs(1, 2)
-        h5 = stage1(1, 0)
-        pair(1, 0, h5)
-        zs(1, 0)
-        xs(0, 0, 512)
-        xs(0, 1, 512)
-        h6 = stage1(1, 1)
-        pair(1, 1, h6)
-        zs(1, 1)
-        weave_words("s", z_bf[0], z_pairs[0], 0, 512)
-        quantize(z_mx[0], z_bf[0], 0, 512)
-        tanh(1, 2, 3)
-        h7 = stage1(1, 3)
-        y_acc.extend([psum.tile([P, PAIRS], F32, name="yacc%d" % n, tag="bank", bufs=8) for n in range(N // P)])
-        z_pass(0, True)
-        pair(1, 3, h7)
-        tanh(0, 2, 4)
-        cast_w3(0)
-        xs(0, 2, 512)
-        xs(0, 3, 512)
-        tanh(1, 0, 1)
-        xs(1, 2, 512)
-        tanh(1, 1, 2)
-        xs(1, 0, 512)
-        tanh(1, 3, 4)
-        xs(1, 1, 512)
-        xs(1, 3, 512)
-        halves = ((0, 256), (256, 512))
-        for m0, m1 in halves:
-            zs_v(1, 3, m0, m1)
-        for m0, m1 in halves:
-            weave_words("v", z_bf[1], z_pairs[1], m0, m1)
-        for m0, m1 in halves:
-            quantize(z_mx[1], z_bf[1], m0, m1)
-        z_pass(1, False)
-        quantize_w3(0)
-        for m0, m1 in halves:
-            weave_c(x_bf[0], x_scaled[0], m0, m1)
-        for m0, m1 in halves:
-            quantize(x_mx[0], x_bf[0], m0, m1)
-        x_pass(0, False, [0])
-        for m0, m1 in halves:
-            weave_c(x_bf[1], x_scaled[1], m0, m1)
-        quantize(x_mx[1], x_bf[1], 0, 256)
-        x_pass(1, False, [0], 0, 256)
-        quantize(x_mx[1], x_bf[1], 256, 512)
-        x_pass(1, True, [0], 256, 512)
-
-        def weights(n):
-            cast_w3(n)
-            quantize_w3(n)
-            x_pass(0, False, [n])
-            x_pass(1, True, [n])
+                cols = slice(P * (2 * n + b), P * (2 * n + b + 1))
+                y_pass(w3_mx[0][:, cols].bitcast(FP8X4), w3_mx[1][:, cols], x_mx[b], n, False, stop, m0, m1)
 
         y = {}
         second = {}
 
         def fetch(n):
-            y[n] = keep.tile([P, PAIRS], F32, name="y%d" % n)
-            nc.scalar.copy(y[n][:], y_acc[n][:])
-            second[n] = keep.tile([P, TRIADS], F32, name="second%d" % n)
+            y[n] = shared.tile([P, PAIRS], F32, name="y%d" % n, offset=2048 * n)
+            for (tile, m0, m1), acc in y_acc.items():
+                if tile == n:
+                    nc.scalar.copy(y[n][:, m0:m1], acc[:])
+            second[n] = shared.tile([P, TRIADS], F32, name="second%d" % n, offset=8192 + 1024 * n)
             nc.vector.tensor_copy(second[n][:], y[n][:].indirect(p4[:]))
 
         def finish(n):
-            weighted = keep.tile([P, TRIADS], F32, name="weighted%d" % n)
+            weighted = shared.tile([P, TRIADS], F32, name="weighted%d" % n, offset=32768 + 1024 * n)
             nc.scalar.activation(weighted[:], second[n][:], ACT.Copy, scale=gd_sb[:, n : n + 1])
-            res = keep.tile([P, TRIADS], F32, name="res%d" % n)
+            res = shared.tile([P, TRIADS], F32, name="res%d" % n, offset=40960 + 1024 * n)
             nc.vector.tensor_tensor(res[:], y[n][:].indirect(p3[:]), weighted[:], ALU.subtract)
             nc.sync.dma_start(out[P * n : P * (n + 1), :], res[:])
 
-        weights(1)
-        weights(2)
-        weights(3)
+        def tile_pairs(tile):
+            pair(tile, stage1(tile))
+            if tile != (2, 3):
+                zs(tile)
+
+        def x_of(tile):
+            tanh(tile)
+            xs(tile)
+
+        cast_both((0, 0), first_raw[:, :, 0:256])
+        quantize_w1((0, 0))
+        cast_both((1, 0), first_raw[:, :, 256:512])
+        cast_one((0, 1, 0), quarter_raw[0][:], 0, 0, HALF)
+        quantize_w1((0, 1, 0))
+        quantize_w1((1, 0))
+        cast_one((0, 1, 1), quarter_raw[0][:], 1, 0, HALF)
+        quantize_w1((0, 1, 1))
+        tile_pairs((0, 0))
+        h_next = stage1((0, 1))
+        cast_pool((1, 1), quarter_raw[1][:], 0)
+        cast_pool((1, 1), quarter_raw[1][:], 1)
+        quantize_w1((1, 1))
+        pair((0, 1), h_next)
+        zs((0, 1))
+        cast_plain((2, 0), half_raw[0][:])
+        quantize_w1((2, 0))
+        cast_one((2, 1, 0), half_raw[1][:], 0, 0, 16)
+        tile_pairs((1, 0))
+        h_next = stage1((1, 1))
+        cast_one((2, 1, 0), half_raw[1][:], 0, 16, P)
+        quantize_w1((2, 1, 0))
+        pair((1, 1), h_next)
+        zs((1, 1))
+        cast_one((2, 1, 1), half_raw[1][:], 1, 0, P)
+        quantize_w1((2, 1, 1))
+        tile_pairs((2, 0))
+        move_early(z_rows)
+        move_late(z_rows, z_late[:].rearrange("p m e -> p (m e)"))
+        tile_pairs((2, 2))
+        x_of((0, 0))
+        x_of((0, 1))
+        move_early(x_rows)
+        x_of((1, 0))
+        tile_pairs((2, 1))
+        x_of((1, 1))
+        move_late(x_rows, x_late[:].rearrange("p e m -> p (e m)"))
+        h_last = stage1((2, 3))
+        x_of((2, 2))
+        pair((2, 3), h_last)
+        x_of((2, 0))
+        x_of((2, 1))
+        x_of((2, 3))
+        for n in range(4):
+            cast_w3(n, "s")
+        open_y()
+        z_bf[0] = shared.tile([P, PACK * PAIRS], BF16, name="z_bf0", align_bytes=64, offset=slot(6))
+        for m0, m1 in halves:
+            zs_v((2, 3), m0, m1)
+        for m0, m1 in halves:
+            weave_words("v", z_bf[1], z_pairs[1], m0, m1)
+        for m0, m1 in halves:
+            quantize(z_mx[1], z_bf[1], m0, m1)
+        z_pass(1, True)
+        for m0, m1 in halves:
+            weave_words("v", z_bf[0], z_pairs[0], m0, m1)
+        for m0, m1 in halves:
+            weave_planes(x_bf[0], x_planes[0], m0, m1)
+        quantize(z_mx[0], z_bf[0], 0, PAIRS)
+        z_pass(0, False)
+        quantize(x_mx[0], x_bf[0], 0, PAIRS)
+        quantize_w3(0)
+        quantize_w3(1)
+        x_pass(0, False, [0, 1])
+        for m0, m1 in halves:
+            weave_planes(x_bf[1], x_planes[1], m0, m1)
+        quantize(x_mx[1], x_bf[1], 0, 256)
+        x_pass(1, True, [0], 0, 256)
+        quantize(x_mx[1], x_bf[1], 256, 512)
+        x_pass(1, True, [0], 256, 512)
+        x_pass(1, True, [1])
+        for n in range(2, 4):
+            quantize_w3(n)
+            x_pass(0, False, [n])
+            x_pass(1, True, [n])
         fetch(0)
         fetch(1)
         finish(0)
         fetch(2)
-        finish(1)
         fetch(3)
+        finish(1)
         finish(2)
         finish(3)

@@ -170,13 +170,13 @@ def tile_list_friend_triad_scores_kernel(
             return w1_mx[key][0][:, c0 : c0 + P], w1_mx[key][1][:, c0 : c0 + P]
 
         w1_unit((0, 0), 256, None, None)
-        w1_unit((0, 1, 0), P, 5, 0)
+        w1_unit((0, 1, 0), P, 5, None)
         w1_unit((0, 1, 1), P, None, 10)
         w1_unit((1, 0), 256, None, 5)
-        w1_unit((1, 1), 256, 0, None)
+        w1_unit((1, 1), 256, 0, 1)
         w1_unit((2, 0), 512, 10, None)
         w1_unit((2, 1, 0), 256, 1, None)
-        w1_unit((2, 1, 1), 256, 8.5, None)
+        w1_unit((2, 1, 1), 256, 10.5, None)
 
         def quantize_w1(key):
             quantize(w1_mx[key], w1_bf[key], 0, w1_width[key])
@@ -190,7 +190,7 @@ def tile_list_friend_triad_scores_kernel(
             if a == 0:
                 nc.vector.tensor_copy(got_sc[:], tab_sc[:].indirect(idx[:]))
 
-        h_place = {(1, 0): 16384, (1, 1): 16384 + 4096, (2, 0): 24576, (2, 2): 24576 + 4096}
+        h_place = {(1, 0): 16384, (1, 1): 16384 + 4096, (2, 0): 24576, (2, 2): slot(10)}
 
         def stage1(tile):
             if tile in h_place:
@@ -212,7 +212,7 @@ def tile_list_friend_triad_scores_kernel(
                         start=(a == 0),
                         stop=(a == 1),
                     )
-                copy_on("v" if tile == (0, 0) and part % 2 == 1 else "s", h[:, cols], acc[:])
+                copy_on("v" if tile == (0, 0) and part > 0 else "s", h[:, cols], acc[:])
             return h
 
         f = {}
@@ -221,9 +221,9 @@ def tile_list_friend_triad_scores_kernel(
         x_planes = [keep.tile([P, PACK, PAIRS], BF16, name="x_planes%d" % b) for b in range(2)]
         z_late = shared.tile([P, PAIRS, 2], BF16, name="z_late", offset=slot(3))
         x_late = shared.tile([P, 2, PAIRS], BF16, name="x_late", offset=slot(4))
-        z_bf = {1: keep.tile([P, PACK * PAIRS], BF16, name="z_bf1", align_bytes=64)}
-        x_bf = [keep.tile([P, PACK * PAIRS], BF16, name="x_bf%d" % b, align_bytes=64) for b in range(2)]
-        z_mx = [mx_tiles("z%d" % b, PAIRS) for b in range(2)]
+        z_bf = [keep.tile([P, PACK * PAIRS], BF16, name="z_bf%d" % b, align_bytes=64) for b in range(2)]
+        x_bf = {1: keep.tile([P, PACK * PAIRS], BF16, name="x_bf1", align_bytes=64)}
+        z_mx = {1: mx_tiles("z1", PAIRS)}
         x_mx = [mx_tiles("x%d" % b, PAIRS) for b in range(2)]
         w3_mx = mx_tiles("w3", 2 * N)
         halves = ((0, 256), (256, 512))
@@ -248,7 +248,7 @@ def tile_list_friend_triad_scores_kernel(
                 return x_late[:, e, :]
             return x_planes[1][:, e, :]
 
-        left_slot = {(0, 1): 0.5, (1, 1): 1.5}
+        left_slot = {(0, 1): 0.5, (1, 1): 1.5, (2, 3): 8}
 
         first_slot = {(0, 1): 0, (1, 1): 1, (2, 3): 6}
 
@@ -280,8 +280,10 @@ def tile_list_friend_triad_scores_kernel(
 
         th_slot = {(0, 0): 0, (0, 1): 1, (1, 0): 0, (1, 1): 1, (2, 2): 0, (2, 0): 1, (2, 1): 0, (2, 3): 0}
 
+        th_place = (24576 + 4096, 24576 + 6144)
+
         def tanh(tile):
-            th[tile] = shared.tile([P, PAIRS], F32, name="th%d%d" % tile, offset=slot(8 + th_slot[tile]))
+            th[tile] = shared.tile([P, PAIRS], F32, name="th%d%d" % tile, offset=th_place[th_slot[tile]])
             nc.scalar.activation(th[tile][:], f[tile][:], ACT.Tanh)
 
         def xs(tile):
@@ -312,7 +314,7 @@ def tile_list_friend_triad_scores_kernel(
         w3_bf = {}
 
         def cast_w3(n, eng):
-            place = (slot(9), slot(3), slot(4), slot(8))[n]
+            place = (th_place[1], slot(3), slot(4), th_place[0])[n]
             w3_bf[n] = shared.tile([P, 2 * PACK * P], BF16, name="w3_bf%d" % n, align_bytes=64, offset=place)
             for a in range(2):
                 copy_on(
@@ -392,8 +394,7 @@ def tile_list_friend_triad_scores_kernel(
         quantize_w1((0, 1, 1))
         tile_pairs((0, 0))
         h_next = stage1((0, 1))
-        cast_pool((1, 1), quarter_raw[1][:], 0)
-        cast_pool((1, 1), quarter_raw[1][:], 1)
+        cast_both((1, 1), quarter_raw[1][:])
         quantize_w1((1, 1))
         pair((0, 1), h_next)
         zs((0, 1))
@@ -408,12 +409,14 @@ def tile_list_friend_triad_scores_kernel(
         zs((1, 1))
         cast_one((2, 1, 1), half_raw[1][:], 1, 0, P)
         quantize_w1((2, 1, 1))
+        tanh((0, 0))
         tile_pairs((2, 0))
         move_early(z_rows)
         move_late(z_rows, z_late[:].rearrange("p m e -> p (m e)"))
+        tanh((0, 1))
+        xs((0, 0))
         tile_pairs((2, 2))
-        x_of((0, 0))
-        x_of((0, 1))
+        xs((0, 1))
         move_early(x_rows)
         x_of((1, 0))
         tile_pairs((2, 1))
@@ -422,13 +425,15 @@ def tile_list_friend_triad_scores_kernel(
         h_last = stage1((2, 3))
         x_of((2, 2))
         pair((2, 3), h_last)
+        weave_words("s", z_bf[0], z_pairs[0], 0, PAIRS)
         x_of((2, 0))
         x_of((2, 1))
         x_of((2, 3))
         for n in range(4):
             cast_w3(n, "s")
         open_y()
-        z_bf[0] = shared.tile([P, PACK * PAIRS], BF16, name="z_bf0", align_bytes=64, offset=slot(6))
+        x_bf[0] = shared.tile([P, PACK * PAIRS], BF16, name="x_bf0", align_bytes=64, offset=slot(8))
+        z_mx[0] = mx_tiles("z0", PAIRS, slot(6))
         for m0, m1 in halves:
             zs_v((2, 3), m0, m1)
         for m0, m1 in halves:
@@ -436,8 +441,6 @@ def tile_list_friend_triad_scores_kernel(
         for m0, m1 in halves:
             quantize(z_mx[1], z_bf[1], m0, m1)
         z_pass(1, True)
-        for m0, m1 in halves:
-            weave_words("v", z_bf[0], z_pairs[0], m0, m1)
         for m0, m1 in halves:
             weave_planes(x_bf[0], x_planes[0], m0, m1)
         quantize(z_mx[0], z_bf[0], 0, PAIRS)

@@ -75,18 +75,9 @@ def tile_list_friend_triad_scores_kernel(
             return raw
 
         def load_gain(src, name):
-            mixed = keep.tile([P, 2, 2], F32, name=name + "_mixed")
-            for s in range(2):
-                nc.sync.dma_start(
-                    mixed[HALF * s : HALF * (s + 1)],
-                    src[0:PASS].rearrange("(u w t) -> w u t", u=2, t=PACK)[:, :, 2 * s : 2 * s + 2],
-                )
-            return mixed
-
-        def load_gain_plain(src, name):
-            plain = keep.tile([P, PACK], F32, name=name + "_plain")
-            nc.sync.dma_start(plain[:], src[PASS : 2 * PASS].rearrange("(p t) -> p t", t=PACK))
-            return plain
+            t = keep.tile([P, 2, PACK], F32, name=name)
+            nc.sync.dma_start(t[:], src.rearrange("(b p t) -> p b t", p=P, t=PACK))
+            return t
 
         tab_w = []
         quarter_raw = {}
@@ -101,15 +92,13 @@ def tile_list_friend_triad_scores_kernel(
                     )
                 first_raw = load_w(w1, 0, 0, 512, "firstraw", 0)
         quarter_raw[0] = load_w(w1, 1, 0, 256, "q0raw", 8192)
+        quarter_raw[1] = load_w(w1, 1, 256, 512, "q1raw", 12288)
         p1 = load_list(pos1, "p1")
         p2 = load_list(pos2, "p2")
-        quarter_raw[1] = load_w(w1, 1, 256, 512, "q1raw", 12288)
-        gz_mixed = load_gain(gz, "gz")
         half_raw = [load_w(w1, 0, 512, 1024, "halfraw0", 16384)]
-        gt_mixed = load_gain(gt, "gt")
+        gz_sb = load_gain(gz, "gz_sb")
+        gt_sb = load_gain(gt, "gt_sb")
         half_raw.append(load_w(w1, 1, 512, 1024, "halfraw1", 24576))
-        gz_plain = load_gain_plain(gz, "gz")
-        gt_plain = load_gain_plain(gt, "gt")
         w3_raw = [load_w(w3, a, 0, N, "w3raw%d" % a, 32768 + 8192 * a) for a in range(2)]
         w2_w = keep.tile([P, 2, 2 * N], U8, name="w2_w", align_bytes=64)
         nc.sync.dma_start(w2_w[:].bitcast(I32), w2_words.rearrange("a p c -> p a c").bitcast(I32))
@@ -140,43 +129,30 @@ def tile_list_friend_triad_scores_kernel(
             w1_mx[key] = mx_tiles(name, width, None if codes_slot is None else slot(codes_slot))
             w1_width[key] = width
 
-        def cast_both(key, raw):
-            dst = w1_bf[key][:].rearrange("p (e s w j) -> p w j s e", e=2, s=2, j=PACK)
-            nc.scalar.copy(dst, raw.rearrange("p j (w s e) -> p w j s e", s=2, e=2))
+        def cast_plain(key, raw, w0, w1):
+            dst = w1_bf[key][:].rearrange("p (t w j) -> p w j t", t=PACK, j=PACK)[:, w0:w1]
+            nc.scalar.copy(dst, raw.rearrange("p j (w t) -> p w j t", t=PACK)[:, w0:w1])
 
-        def cast_pool(key, raw, e):
-            dst = w1_bf[key][:].rearrange("p (e s w j) -> p e w j s", e=2, s=2, j=PACK)[:, e]
-            src = raw.rearrange("p j (w s e) -> p w j s e", s=2, e=2)[:, :, :, :, e]
-            nc.gpsimd.tensor_scalar(dst, src, 1.0, 0.0, ALU.mult, ALU.add)
-
-        def cast_plain(key, raw):
-            dst = w1_bf[key][:].rearrange("p (t w j) -> p w j t", t=PACK, j=PACK)
-            nc.scalar.copy(dst, raw.rearrange("p j (w t) -> p w j t", t=PACK))
-
-        def cast_one(key, raw, e, w0, w1):
-            dst = w1_bf[key][:].rearrange("p (s w j) -> p w j s", s=2, j=PACK)[:, w0:w1]
-            nc.scalar.copy(dst, raw.rearrange("p j (w s e) -> p w j s e", s=2, e=2)[:, w0:w1, :, :, e])
+        def cast_slots(eng, section, raw, e, w0, w1, first=0):
+            dst = section.rearrange("p (s w j) -> p w j s", s=2, j=PACK)[:, w0:w1]
+            src = raw.rearrange("p j (w s e) -> p w j s e", s=2, e=2)[:, w0 - first : w1 - first, :, :, e]
+            copy_on(eng, dst, src)
 
         def stationary(tile, a):
-            u, e = tile
-            if (u, a) == (0, 1):
-                key, c0 = (0, 1, e), 0
-            elif u < 2:
-                key, c0 = (u, a), P * e
-            elif a == 0:
-                key, c0 = (2, 0), P * e
+            b, t = tile
+            if b == 1:
+                key, c0 = (1, a), P * t
+            elif b == 0 and t % 2 == 1:
+                key, c0 = (0, "odd"), 256 * a + P * (t // 2)
             else:
-                key, c0 = (2, 1, e % 2), P * (e // 2)
+                key, c0 = (b, a, t % 2), P * (t // 2)
             return w1_mx[key][0][:, c0 : c0 + P], w1_mx[key][1][:, c0 : c0 + P]
 
-        w1_unit((0, 0), 256, None, None)
-        w1_unit((0, 1, 0), P, 5, None)
-        w1_unit((0, 1, 1), P, None, 10)
-        w1_unit((1, 0), 256, None, 5)
-        w1_unit((1, 1), 256, 0, 1)
-        w1_unit((2, 0), 512, 10, None)
-        w1_unit((2, 1, 0), 256, 1, None)
-        w1_unit((2, 1, 1), 256, 10.5, None)
+        w1_unit((0, 0, 0), 256, None, None)
+        w1_unit((0, 1, 0), 256, None, 10)
+        w1_unit((0, "odd"), 512, None, None)
+        w1_unit((1, 0), 512, 10, None)
+        w1_unit((1, 1), 512, None, None)
 
         def quantize_w1(key):
             quantize(w1_mx[key], w1_bf[key], 0, w1_width[key])
@@ -190,37 +166,45 @@ def tile_list_friend_triad_scores_kernel(
             if a == 0:
                 nc.vector.tensor_copy(got_sc[:], tab_sc[:].indirect(idx[:]))
 
-        h_place = {(1, 0): 16384, (1, 1): 16384 + 4096, (2, 0): 24576, (2, 2): slot(10)}
+        h_place = {(0, 1): 16384, (0, 3): 24576}
+
+        banks = {}
+
+        def h_pass(tile, a):
+            width = 256 if tile == (0, 0) else BANK
+            codes, scales = stationary(tile, a)
+            for part in range(S // width):
+                if a == 0:
+                    banks[tile, part] = psum.tile([P, width], F32, name="hacc", tag="bank", bufs=8)
+                cols = slice(width * part, width * (part + 1))
+                nc.tensor.matmul_mx(
+                    out=banks[tile, part][:],
+                    lhsT=codes.bitcast(FP8X4),
+                    lhsT_scale=scales,
+                    rhs=got_w[a][:, cols].bitcast(FP8X4),
+                    rhs_scale=got_sc[4 * a : P, cols],
+                    start=(a == 0),
+                    stop=(a == 1),
+                )
 
         def stage1(tile):
+            if (tile, 0) not in banks:
+                h_pass(tile, 0)
+            h_pass(tile, 1)
             if tile in h_place:
                 h = shared.tile([P, S], F32, name="h%d%d" % tile, offset=h_place[tile])
             else:
                 h = ring.tile([P, S], F32, name="h", bufs=4)
             width = 256 if tile == (0, 0) else BANK
             for part in range(S // width):
-                acc = psum.tile([P, width], F32, name="hacc", tag="bank", bufs=8)
                 cols = slice(width * part, width * (part + 1))
-                for a in range(2):
-                    codes, scales = stationary(tile, a)
-                    nc.tensor.matmul_mx(
-                        out=acc[:],
-                        lhsT=codes.bitcast(FP8X4),
-                        lhsT_scale=scales,
-                        rhs=got_w[a][:, cols].bitcast(FP8X4),
-                        rhs_scale=got_sc[4 * a : P, cols],
-                        start=(a == 0),
-                        stop=(a == 1),
-                    )
-                copy_on("v" if tile == (0, 0) and part > 0 else "s", h[:, cols], acc[:])
+                copy_on("v" if tile == (0, 0) and part % 2 == 1 else "s", h[:, cols], banks[tile, part][:])
             return h
 
         f = {}
         th = {}
         z_pairs = [keep.tile([P, 2, PAIRS, 2], BF16, name="z_pairs%d" % b) for b in range(2)]
         x_planes = [keep.tile([P, PACK, PAIRS], BF16, name="x_planes%d" % b) for b in range(2)]
-        z_late = shared.tile([P, PAIRS, 2], BF16, name="z_late", offset=slot(3))
-        x_late = shared.tile([P, 2, PAIRS], BF16, name="x_late", offset=slot(4))
         z_bf = [keep.tile([P, PACK * PAIRS], BF16, name="z_bf%d" % b, align_bytes=64) for b in range(2)]
         x_bf = {1: keep.tile([P, PACK * PAIRS], BF16, name="x_bf1", align_bytes=64)}
         z_mx = {1: mx_tiles("z1", PAIRS)}
@@ -228,29 +212,13 @@ def tile_list_friend_triad_scores_kernel(
         w3_mx = mx_tiles("w3", 2 * N)
         halves = ((0, 256), (256, 512))
 
-        def gain(mixed, plain, tile):
-            u, e = tile
-            return mixed[:, u, e : e + 1] if u < 2 else plain[:, e : e + 1]
-
         def z_place(tile):
-            u, e = tile
-            if u == 0:
-                return z_pairs[0][:, 0, :, e]
-            if u == 1:
-                return z_late[:, :, e]
-            return z_pairs[1][:, e // 2, :, e % 2]
+            b, t = tile
+            return z_pairs[b][:, t // 2, :, t % 2]
 
-        def x_place(tile):
-            u, e = tile
-            if u == 0:
-                return x_planes[0][:, e, :]
-            if u == 1:
-                return x_late[:, e, :]
-            return x_planes[1][:, e, :]
+        left_slot = {}
 
-        left_slot = {(0, 1): 0.5, (1, 1): 1.5, (2, 3): 8}
-
-        first_slot = {(0, 1): 0, (1, 1): 1, (2, 3): 6}
+        first_slot = {(1, 2): 6, (1, 1): 4, (1, 3): 8}
 
         def pair(tile, h):
             if tile in first_slot:
@@ -261,7 +229,7 @@ def tile_list_friend_triad_scores_kernel(
                 left.append(shared.tile([P, 256], F32, name="left%d%d" % tile, offset=slot(left_slot[tile])))
             else:
                 left.append(ring.tile([P, 256], F32, name="left_b", bufs=2))
-            tag = "f%d%d" % (tile[0], min(tile[1], 2))
+            tag = "f12" if tile == (1, 3) else "f%d%d" % tile
             f[tile] = keep.tile([P, PAIRS], F32, name=tag, tag=tag)
             for k in range(2):
                 nc.vector.tensor_copy(left[k][:], h[:].indirect(p1[:, 16 * k : 16 * (k + 1)]))
@@ -270,34 +238,26 @@ def tile_list_friend_triad_scores_kernel(
                     f[tile][:, m0:m1], h[:].indirect(p2[:, 16 * k : 16 * (k + 1)]), left[k][:], ALU.mult
                 )
 
+        def gain(gains, tile):
+            b, t = tile
+            return gains[:, b, t : t + 1]
+
         def zs(tile):
-            nc.gpsimd.tensor_scalar(z_place(tile), f[tile][:], gain(gz_mixed, gz_plain, tile), 0.0, ALU.mult, ALU.add)
+            nc.gpsimd.tensor_scalar(z_place(tile), f[tile][:], gain(gz_sb, tile), 0.0, ALU.mult, ALU.add)
 
-        def zs_v(tile, m0, m1):
-            nc.vector.tensor_scalar(
-                z_place(tile)[:, m0:m1], f[tile][:, m0:m1], gain(gz_mixed, gz_plain, tile), None, ALU.mult
-            )
+        def zs_last(tile):
+            nc.scalar.activation(z_place(tile), f[tile][:], ACT.Copy, scale=gain(gz_sb, tile))
 
-        th_slot = {(0, 0): 0, (0, 1): 1, (1, 0): 0, (1, 1): 1, (2, 2): 0, (2, 0): 1, (2, 1): 0, (2, 3): 0}
+        th_slot = {(0, 0): 0, (0, 2): 1, (0, 1): 0, (0, 3): 2, (1, 2): 1, (1, 0): 0, (1, 1): 1, (1, 3): 0}
 
-        th_place = (24576 + 4096, 24576 + 6144)
+        th_place = (24576 + 4096, 24576 + 6144, slot(6))
 
         def tanh(tile):
             th[tile] = shared.tile([P, PAIRS], F32, name="th%d%d" % tile, offset=th_place[th_slot[tile]])
             nc.scalar.activation(th[tile][:], f[tile][:], ACT.Tanh)
 
         def xs(tile):
-            nc.scalar.activation(x_place(tile), th[tile][:], ACT.Copy, scale=gain(gt_mixed, gt_plain, tile))
-
-        def move_early(rows):
-            nc.sync.dma_start(rows[0:HALF, 1], rows[HALF:P, 0])
-
-        def move_late(rows, late):
-            nc.sync.dma_start(rows[HALF:P, 1], late[HALF:P])
-            nc.sync.dma_start(rows[HALF:P, 0], late[0:HALF])
-
-        z_rows = z_pairs[0][:].rearrange("p s m e -> p s (m e)")
-        x_rows = x_planes[0][:].rearrange("p (s e) m -> p s (e m)", s=2)
+            nc.scalar.activation(x_planes[tile[0]][:, tile[1], :], th[tile][:], ACT.Copy, scale=gain(gt_sb, tile))
 
         def weave_planes(grouped, planes, m0, m1):
             nc.vector.tensor_copy(
@@ -314,7 +274,7 @@ def tile_list_friend_triad_scores_kernel(
         w3_bf = {}
 
         def cast_w3(n, eng):
-            place = (th_place[1], slot(3), slot(4), th_place[0])[n]
+            place = w3_place[n]
             w3_bf[n] = shared.tile([P, 2 * PACK * P], BF16, name="w3_bf%d" % n, align_bytes=64, offset=place)
             for a in range(2):
                 copy_on(
@@ -377,80 +337,79 @@ def tile_list_friend_triad_scores_kernel(
 
         def tile_pairs(tile):
             pair(tile, stage1(tile))
-            if tile != (2, 3):
+            if tile != (1, 3):
                 zs(tile)
 
         def x_of(tile):
             tanh(tile)
             xs(tile)
 
-        cast_both((0, 0), first_raw[:, :, 0:256])
-        quantize_w1((0, 0))
-        cast_both((1, 0), first_raw[:, :, 256:512])
-        cast_one((0, 1, 0), quarter_raw[0][:], 0, 0, HALF)
-        quantize_w1((0, 1, 0))
-        quantize_w1((1, 0))
-        cast_one((0, 1, 1), quarter_raw[0][:], 1, 0, HALF)
-        quantize_w1((0, 1, 1))
+        odd = w1_bf[0, "odd"]
+        cast_slots("s", w1_bf[0, 0, 0][:], first_raw[:], 0, 0, P)
+        quantize_w1((0, 0, 0))
+        h_pass((0, 0), 0)
+        h_pass((0, 2), 0)
+        cast_slots("s", odd[:, 0:1024], first_raw[:], 1, 0, P)
+        cast_slots("s", w1_bf[0, 1, 0][:], quarter_raw[0][:], 0, 0, HALF)
+        cast_slots("s", odd[:, 1024:2048], quarter_raw[0][:], 1, 0, HALF)
+        cast_slots("v", w1_bf[0, 1, 0][:], quarter_raw[1][:], 0, HALF, P, HALF)
+        cast_slots("s", odd[:, 1024:2048], quarter_raw[1][:], 1, HALF, P, HALF)
+        quantize(w1_mx[0, 1, 0], w1_bf[0, 1, 0], 0, P)
+        quantize(w1_mx[0, 1, 0], w1_bf[0, 1, 0], P, 256)
+        quantize_w1((0, "odd"))
         tile_pairs((0, 0))
-        h_next = stage1((0, 1))
-        cast_both((1, 1), quarter_raw[1][:])
+        tile_pairs((0, 2))
+        cast_plain((1, 0), half_raw[0][:], 0, P)
+        quantize_w1((1, 0))
+        cast_plain((1, 1), half_raw[1][:], 0, 16)
+        tile_pairs((0, 1))
+        cast_plain((1, 1), half_raw[1][:], 16, P)
         quantize_w1((1, 1))
-        pair((0, 1), h_next)
-        zs((0, 1))
-        cast_plain((2, 0), half_raw[0][:])
-        quantize_w1((2, 0))
-        cast_one((2, 1, 0), half_raw[1][:], 0, 0, 16)
-        tile_pairs((1, 0))
-        h_next = stage1((1, 1))
-        cast_one((2, 1, 0), half_raw[1][:], 0, 16, P)
-        quantize_w1((2, 1, 0))
-        pair((1, 1), h_next)
-        zs((1, 1))
-        cast_one((2, 1, 1), half_raw[1][:], 1, 0, P)
-        quantize_w1((2, 1, 1))
+        tile_pairs((0, 3))
         tanh((0, 0))
-        tile_pairs((2, 0))
-        move_early(z_rows)
-        move_late(z_rows, z_late[:].rearrange("p m e -> p (m e)"))
-        tanh((0, 1))
+        tanh((0, 2))
         xs((0, 0))
-        tile_pairs((2, 2))
-        xs((0, 1))
-        move_early(x_rows)
-        x_of((1, 0))
-        tile_pairs((2, 1))
-        x_of((1, 1))
-        move_late(x_rows, x_late[:].rearrange("p e m -> p (e m)"))
-        h_last = stage1((2, 3))
-        x_of((2, 2))
-        pair((2, 3), h_last)
+        tile_pairs((1, 0))
+        xs((0, 2))
+        tile_pairs((1, 2))
+        x_of((0, 1))
+        tile_pairs((1, 1))
         weave_words("s", z_bf[0], z_pairs[0], 0, PAIRS)
-        x_of((2, 0))
-        x_of((2, 1))
-        x_of((2, 3))
-        for n in range(4):
-            cast_w3(n, "s")
+        z_mx[0] = mx_tiles("z0", PAIRS, slot(4))
+        quantize(z_mx[0], z_bf[0], 0, PAIRS)
+        h_last = stage1((1, 3))
         open_y()
+        z_pass(0, True)
+        tanh((0, 3))
+        x_of((1, 2))
+        pair((1, 3), h_last)
+        xs((0, 3))
+        tanh((1, 0))
+        tanh((1, 1))
+        xs((1, 0))
+        xs((1, 1))
+        w3_place = (th_place[2], th_place[1], th_place[0], th_place[2])
+        cast_w3(0, "s")
+        zs_last((1, 3))
+        x_of((1, 3))
+        for n in range(1, 4):
+            cast_w3(n, "s")
         x_bf[0] = shared.tile([P, PACK * PAIRS], BF16, name="x_bf0", align_bytes=64, offset=slot(8))
-        z_mx[0] = mx_tiles("z0", PAIRS, slot(6))
         for m0, m1 in halves:
-            zs_v((2, 3), m0, m1)
+            weave_planes(x_bf[0], x_planes[0], m0, m1)
+        for m0, m1 in halves:
+            quantize(x_mx[0], x_bf[0], m0, m1)
+        quantize_w3(0)
+        x_pass(0, False, [0])
         for m0, m1 in halves:
             weave_words("v", z_bf[1], z_pairs[1], m0, m1)
         for m0, m1 in halves:
             quantize(z_mx[1], z_bf[1], m0, m1)
-        z_pass(1, True)
-        for m0, m1 in halves:
-            weave_planes(x_bf[0], x_planes[0], m0, m1)
-        quantize(z_mx[0], z_bf[0], 0, PAIRS)
-        z_pass(0, False)
-        quantize(x_mx[0], x_bf[0], 0, PAIRS)
-        quantize_w3(0)
-        quantize_w3(1)
-        x_pass(0, False, [0, 1])
+        z_pass(1, False)
         for m0, m1 in halves:
             weave_planes(x_bf[1], x_planes[1], m0, m1)
+        quantize_w3(1)
+        x_pass(0, False, [1])
         quantize(x_mx[1], x_bf[1], 0, 256)
         x_pass(1, True, [0], 0, 256)
         quantize(x_mx[1], x_bf[1], 256, 512)

@@ -242,8 +242,13 @@ def tile_list_friend_triad_scores_kernel(
             b, t = tile
             return gains[:, b, t : t + 1]
 
+        before_quantize = ((0, 2), (0, 1), (1, 1))
+
         def zs(tile):
-            nc.gpsimd.tensor_scalar(z_place(tile), f[tile][:], gain(gz_sb, tile), 0.0, ALU.mult, ALU.add)
+            for m0, m1 in ((0, PAIRS),) if tile in before_quantize else halves:
+                nc.gpsimd.tensor_scalar(
+                    z_place(tile)[:, m0:m1], f[tile][:, m0:m1], gain(gz_sb, tile), 0.0, ALU.mult, ALU.add
+                )
 
         def zs_last(tile):
             nc.scalar.activation(z_place(tile), f[tile][:], ACT.Copy, scale=gain(gz_sb, tile))

@@ -17,10 +17,26 @@ ALU = mybir.AluOpType
 ACT = mybir.ActivationFunctionType
 
 P = 128
-HALF = 64
 PACK = 4
 PASS = P * PACK
 BANK = 512
+BANKS = 8
+QUADRANT = 32
+GROUP = 16
+ALIGN = 64
+HALVES = ((0, PAIRS // 2), (PAIRS // 2, PAIRS))
+FIRST, LAST = (0, 0), (1, 3)
+
+KIB = 1024
+AT_W1_FIRST = 0
+AT_W1_QUARTER = (8 * KIB, 12 * KIB)
+AT_W1_HALF = (16 * KIB, 24 * KIB)
+AT_W3 = (32 * KIB, 40 * KIB)
+AT_Z_CODES = 56 * KIB
+AT_THIRD_TANH = 60 * KIB
+AT_X_WOVEN = 64 * KIB
+AT_W1_ROUNDED = 68 * KIB
+AT_TANH = (AT_W1_HALF[1] + 4 * KIB, AT_W1_HALF[1] + 6 * KIB, AT_THIRD_TANH)
 
 
 def tile_list_friend_triad_scores_kernel(
@@ -39,73 +55,69 @@ def tile_list_friend_triad_scores_kernel(
             nc.sync.dma_start(t[:], src)
             return t
 
-        def mx_tiles(name, width, offset=None):
-            if offset is None:
-                codes = keep.tile([P, width], U32, name=name + "_codes", align_bytes=64)
-            else:
-                codes = shared.tile([P, width], U32, name=name + "_codes", align_bytes=64, offset=offset)
-            scales = keep.tile([P, width], U8, name=name + "_scales", align_bytes=64)
-            return codes, scales
+        def operand_tile(name, width, dtype, at=None):
+            if at is None:
+                return keep.tile([P, width], dtype, name=name, align_bytes=ALIGN)
+            return shared.tile([P, width], dtype, name=name, align_bytes=ALIGN, offset=at)
+
+        def mx_tiles(name, width, at=None):
+            return operand_tile(name + "_codes", width, U32, at), operand_tile(name + "_scales", width, U8)
 
         def quantize(mx, grouped, c0, c1):
             nc.vector.quantize_mx(
                 out=mx[0][:, c0:c1].bitcast(FP8X4), scales=mx[1][:, c0:c1], in_=grouped[:, PACK * c0 : PACK * c1]
             )
 
-        def copy_on(eng, dst, src):
-            if eng == "v":
-                nc.vector.tensor_copy(dst, src)
-            else:
-                nc.scalar.copy(dst, src)
-
-        tab_sc = keep.tile([P, T], U8, name="tab_sc", align_bytes=64)
-        nc.gpsimd.memset(tab_sc[:].bitcast(I32), 0)
-        warm = keep.tile([P, 8], F32, name="warm")
-        nc.vector.memset(warm[:], 0.0)
-        warm2 = keep.tile([P, 8], F32, name="warm2")
-        nc.scalar.activation(warm2[:], warm[:], ACT.Tanh)
-        w2_sc = keep.tile([P, 2, N], U8, name="w2_sc", align_bytes=64)
+        tab_sc = operand_tile("tab_sc", T, U8)
+        nc.vector.memset(tab_sc[:].bitcast(I32), 0)
+        warm_in = keep.tile([P, 8], F32, name="warm_in")
+        nc.vector.memset(warm_in[:], 0.0)
+        warm_out = keep.tile([P, 8], F32, name="warm_out")
+        nc.scalar.activation(warm_out[:], warm_in[:], ACT.Tanh)
+        w2_sc = keep.tile([P, 2, N], U8, name="w2_sc", align_bytes=ALIGN)
         nc.vector.memset(w2_sc[:].rearrange("p a c -> p (a c)").bitcast(I32), 0)
 
-        idx = load_list(offs, "idx")
-
-        def load_w(src, a, c0, c1, name, offset):
-            raw = shared.tile([P, PACK, c1 - c0], F32, name=name, offset=offset)
+        def load_weights(src, a, c0, c1, name, at):
+            raw = shared.tile([P, PACK, c1 - c0], F32, name=name, offset=at)
             nc.sync.dma_start(raw[:], src[PASS * a : PASS * (a + 1), c0:c1].rearrange("(p j) c -> p j c", j=PACK))
             return raw
+
+        def load_table(a):
+            t = operand_tile("tab_w%d" % a, T, I32)
+            nc.sync.dma_start(t[:], tab_words[a].rearrange("p t i -> p (t i)").bitcast(I32))
+            return t
 
         def load_gain(src, name):
             t = keep.tile([P, 2, PACK], F32, name=name)
             nc.sync.dma_start(t[:], src.rearrange("(b p t) -> p b t", p=P, t=PACK))
             return t
 
-        tab_w = []
-        quarter_raw = {}
-        for a in range(2):
-            t = keep.tile([P, T], I32, name="tab_w%d" % a, align_bytes=64)
-            nc.sync.dma_start(t[:], tab_words[a].rearrange("p t i -> p (t i)").bitcast(I32))
-            tab_w.append(t)
-            if a == 0:
-                for q in range(4):
-                    nc.sync.dma_start(
-                        tab_sc[32 * q : 32 * q + 8, :].bitcast(I32), tab_scales[:, 4 * q : 4 * q + 4, :].bitcast(I32)
-                    )
-                first_raw = load_w(w1, 0, 0, 512, "firstraw", 0)
-        quarter_raw[0] = load_w(w1, 1, 0, 256, "q0raw", 8192)
-        quarter_raw[1] = load_w(w1, 1, 256, 512, "q1raw", 12288)
+        tab_w = [load_table(0)]
+        idx = load_list(offs, "idx")
         p1 = load_list(pos1, "p1")
+        for q in range(P // QUADRANT):
+            nc.sync.dma_start(
+                tab_sc[QUADRANT * q : QUADRANT * q + 2 * PACK, :].bitcast(I32),
+                tab_scales[:, PACK * q : PACK * (q + 1), :].bitcast(I32),
+            )
+        first_raw = load_weights(w1, 0, 0, PASS, "first_raw", AT_W1_FIRST)
+        tab_w.append(load_table(1))
+        quarter_raw = [
+            load_weights(w1, 1, PASS // 2 * u, PASS // 2 * (u + 1), "quarter_raw%d" % u, AT_W1_QUARTER[u])
+            for u in range(2)
+        ]
         p2 = load_list(pos2, "p2")
-        half_raw = [load_w(w1, 0, 512, 1024, "halfraw0", 16384)]
+        half_raw = [load_weights(w1, 0, PASS, H, "half_raw0", AT_W1_HALF[0])]
         gz_sb = load_gain(gz, "gz_sb")
         gt_sb = load_gain(gt, "gt_sb")
-        half_raw.append(load_w(w1, 1, 512, 1024, "halfraw1", 24576))
-        w3_raw = [load_w(w3, a, 0, N, "w3raw%d" % a, 32768 + 8192 * a) for a in range(2)]
-        w2_w = keep.tile([P, 2, 2 * N], U8, name="w2_w", align_bytes=64)
+        half_raw.append(load_weights(w1, 1, PASS, H, "half_raw1", AT_W1_HALF[1]))
+        w3_raw = [load_weights(w3, b, 0, N, "w3_raw%d" % b, AT_W3[b]) for b in range(2)]
+        w2_w = keep.tile([P, 2, 2 * N], U8, name="w2_w", align_bytes=ALIGN)
         nc.sync.dma_start(w2_w[:].bitcast(I32), w2_words.rearrange("a p c -> p a c").bitcast(I32))
-        for q in range(4):
+        for q in range(P // QUADRANT):
             nc.sync.dma_start(
-                w2_sc[32 * q : 32 * q + 4, :, :].bitcast(I32),
-                w2_scales[:, 4 * q : 4 * q + 4, :].rearrange("a r c -> r a c").bitcast(I32),
+                w2_sc[QUADRANT * q : QUADRANT * q + PACK, :, :].bitcast(I32),
+                w2_scales[:, PACK * q : PACK * (q + 1), :].rearrange("a r c -> r a c").bitcast(I32),
             )
         gd_sb = keep.tile([P, N // P], F32, name="gd_sb")
         with nc.allow_non_contiguous_dma(reason="one weight a partition"):
@@ -113,194 +125,182 @@ def tile_list_friend_triad_scores_kernel(
         p3 = load_list(pos3, "p3")
         p4 = load_list(pos4, "p4")
 
-        def slot(k):
-            return 49152 + int(2048 * k)
-
         w1_bf = {}
         w1_mx = {}
-        w1_width = {}
 
-        def w1_unit(key, width, bf_slot, codes_slot):
-            name = "w1_" + "".join(str(k) for k in key)
-            if bf_slot is None:
-                w1_bf[key] = keep.tile([P, PACK * width], BF16, name=name + "_bf", align_bytes=64)
-            else:
-                w1_bf[key] = shared.tile([P, PACK * width], BF16, name=name + "_bf", align_bytes=64, offset=slot(bf_slot))
-            w1_mx[key] = mx_tiles(name, width, None if codes_slot is None else slot(codes_slot))
-            w1_width[key] = width
+        def w1_unit(unit, stationaries, bf_at=None, codes_at=None):
+            w1_bf[unit] = operand_tile(unit + "_bf", PACK * P * stationaries, BF16, bf_at)
+            w1_mx[unit] = mx_tiles(unit, P * stationaries, codes_at)
 
-        def cast_plain(key, raw, w0, w1):
-            dst = w1_bf[key][:].rearrange("p (t w j) -> p w j t", t=PACK, j=PACK)[:, w0:w1]
-            nc.scalar.copy(dst, raw.rearrange("p j (w t) -> p w j t", t=PACK)[:, w0:w1])
+        w1_unit("even0", 2)
+        w1_unit("even1", 2, codes_at=AT_W1_ROUNDED)
+        w1_unit("odd", 4)
+        w1_unit("late0", 4, bf_at=AT_W1_ROUNDED)
+        w1_unit("late1", 4)
 
-        def cast_slots(eng, section, raw, e, w0, w1, first=0):
-            dst = section.rearrange("p (s w j) -> p w j s", s=2, j=PACK)[:, w0:w1]
-            src = raw.rearrange("p j (w s e) -> p w j s e", s=2, e=2)[:, w0 - first : w1 - first, :, :, e]
-            copy_on(eng, dst, src)
+        def round_two_slots(copy, section, raw, e, lo, hi, first=0):
+            dst = section.rearrange("p (s w j) -> p w j s", s=2, j=PACK)[:, lo:hi]
+            src = raw.rearrange("p j (w s e) -> p w j s e", s=2, e=2)[:, lo - first : hi - first, :, :, e]
+            copy(dst, src)
+
+        def round_four_slots(a, lo, hi):
+            dst = w1_bf["late%d" % a][:].rearrange("p (t w j) -> p w j t", t=PACK, j=PACK)[:, lo:hi]
+            nc.scalar.copy(dst, half_raw[a][:].rearrange("p j (w t) -> p w j t", t=PACK)[:, lo:hi])
+
+        def quantize_w1(unit, first, count):
+            quantize(w1_mx[unit], w1_bf[unit], P * first, P * (first + count))
 
         def stationary(tile, a):
             b, t = tile
             if b == 1:
-                key, c0 = (1, a), P * t
-            elif b == 0 and t % 2 == 1:
-                key, c0 = (0, "odd"), 256 * a + P * (t // 2)
+                unit, place = "late%d" % a, t
+            elif t % 2 == 1:
+                unit, place = "odd", 2 * a + t // 2
             else:
-                key, c0 = (b, a, t % 2), P * (t // 2)
-            return w1_mx[key][0][:, c0 : c0 + P], w1_mx[key][1][:, c0 : c0 + P]
+                unit, place = "even%d" % a, t // 2
+            cols = slice(P * place, P * (place + 1))
+            return w1_mx[unit][0][:, cols], w1_mx[unit][1][:, cols]
 
-        w1_unit((0, 0, 0), 256, None, None)
-        w1_unit((0, 1, 0), 256, None, 10)
-        w1_unit((0, "odd"), 512, None, None)
-        w1_unit((1, 0), 512, 10, None)
-        w1_unit((1, 1), 512, None, None)
-
-        def quantize_w1(key):
-            quantize(w1_mx[key], w1_bf[key], 0, w1_width[key])
-
-        got_sc = keep.tile([P, S], U8, name="got_sc", align_bytes=64)
+        got_sc = operand_tile("got_sc", S, U8)
         got_w = []
         for a in range(2):
-            g = keep.tile([P, S], U32, name="got_w%d" % a, align_bytes=64)
-            nc.vector.tensor_copy(g[:], tab_w[a][:].bitcast(U32).indirect(idx[:]))
-            got_w.append(g)
+            got_w.append(operand_tile("got_w%d" % a, S, U32))
+            nc.vector.tensor_copy(got_w[a][:], tab_w[a][:].bitcast(U32).indirect(idx[:]))
             if a == 0:
                 nc.vector.tensor_copy(got_sc[:], tab_sc[:].indirect(idx[:]))
 
-        h_place = {(0, 1): 16384, (0, 3): 24576}
+        h_banks = {}
 
-        banks = {}
+        def h_width(tile):
+            return BANK // 2 if tile == FIRST else BANK
 
         def h_pass(tile, a):
-            width = 256 if tile == (0, 0) else BANK
+            width = h_width(tile)
             codes, scales = stationary(tile, a)
             for part in range(S // width):
                 if a == 0:
-                    banks[tile, part] = psum.tile([P, width], F32, name="hacc", tag="bank", bufs=8)
+                    h_banks[tile, part] = psum.tile([P, width], F32, name="h_acc", tag="bank", bufs=BANKS)
                 cols = slice(width * part, width * (part + 1))
                 nc.tensor.matmul_mx(
-                    out=banks[tile, part][:],
+                    out=h_banks[tile, part][:],
                     lhsT=codes.bitcast(FP8X4),
                     lhsT_scale=scales,
                     rhs=got_w[a][:, cols].bitcast(FP8X4),
-                    rhs_scale=got_sc[4 * a : P, cols],
+                    rhs_scale=got_sc[PACK * a : P, cols],
                     start=(a == 0),
                     stop=(a == 1),
                 )
 
-        def stage1(tile):
-            if (tile, 0) not in banks:
+        h_at = {(0, 1): AT_W1_HALF[0], (0, 3): AT_W1_HALF[1]}
+
+        def h_tile(tile):
+            if (tile, 0) not in h_banks:
                 h_pass(tile, 0)
             h_pass(tile, 1)
-            if tile in h_place:
-                h = shared.tile([P, S], F32, name="h%d%d" % tile, offset=h_place[tile])
+            if tile in h_at:
+                h = shared.tile([P, S], F32, name="h%d%d" % tile, offset=h_at[tile])
             else:
                 h = ring.tile([P, S], F32, name="h", bufs=4)
-            width = 256 if tile == (0, 0) else BANK
+            width = h_width(tile)
             for part in range(S // width):
                 cols = slice(width * part, width * (part + 1))
-                copy_on("v" if tile == (0, 0) and part % 2 == 1 else "s", h[:, cols], banks[tile, part][:])
+                copy = nc.vector.tensor_copy if tile == FIRST and part % 2 == 1 else nc.scalar.copy
+                copy(h[:, cols], h_banks[tile, part][:])
             return h
 
         f = {}
         th = {}
         z_pairs = [keep.tile([P, 2, PAIRS, 2], BF16, name="z_pairs%d" % b) for b in range(2)]
         x_planes = [keep.tile([P, PACK, PAIRS], BF16, name="x_planes%d" % b) for b in range(2)]
-        z_bf = [keep.tile([P, PACK * PAIRS], BF16, name="z_bf%d" % b, align_bytes=64) for b in range(2)]
-        x_bf = {1: keep.tile([P, PACK * PAIRS], BF16, name="x_bf1", align_bytes=64)}
+        z_bf = [operand_tile("z_bf%d" % b, PACK * PAIRS, BF16) for b in range(2)]
+        x_bf = {1: operand_tile("x_bf1", PACK * PAIRS, BF16)}
         z_mx = {1: mx_tiles("z1", PAIRS)}
         x_mx = [mx_tiles("x%d" % b, PAIRS) for b in range(2)]
         w3_mx = mx_tiles("w3", 2 * N)
-        halves = ((0, 256), (256, 512))
 
-        def z_place(tile):
-            b, t = tile
-            return z_pairs[b][:, t // 2, :, t % 2]
+        factor_at = {(1, 2): AT_THIRD_TANH, (1, 1): AT_Z_CODES, (1, 3): AT_X_WOVEN}
 
-        left_slot = {}
-
-        first_slot = {(1, 2): 6, (1, 1): 4, (1, 3): 8}
-
-        def pair(tile, h):
-            if tile in first_slot:
-                left = [shared.tile([P, 256], F32, name="first%d%d" % tile, offset=slot(first_slot[tile]))]
+        def product(tile, h):
+            width = PAIRS // 2
+            if tile in factor_at:
+                left = [shared.tile([P, width], F32, name="factor%d%d" % tile, offset=factor_at[tile])]
             else:
-                left = [ring.tile([P, 256], F32, name="left_a", bufs=2)]
-            if tile in left_slot:
-                left.append(shared.tile([P, 256], F32, name="left%d%d" % tile, offset=slot(left_slot[tile])))
-            else:
-                left.append(ring.tile([P, 256], F32, name="left_b", bufs=2))
-            tag = "f12" if tile == (1, 3) else "f%d%d" % tile
+                left = [ring.tile([P, width], F32, name="left_a")]
+            left.append(ring.tile([P, width], F32, name="left_b"))
+            tag = "f%d%d" % ((1, 2) if tile == LAST else tile)
             f[tile] = keep.tile([P, PAIRS], F32, name=tag, tag=tag)
-            for k in range(2):
-                nc.vector.tensor_copy(left[k][:], h[:].indirect(p1[:, 16 * k : 16 * (k + 1)]))
-            for k, (m0, m1) in enumerate(halves):
+            for k, (m0, m1) in enumerate(HALVES):
+                nc.vector.tensor_copy(left[k][:], h[:].indirect(p1[:, m0 // GROUP : m1 // GROUP]))
+            for k, (m0, m1) in enumerate(HALVES):
                 nc.vector.tensor_tensor(
-                    f[tile][:, m0:m1], h[:].indirect(p2[:, 16 * k : 16 * (k + 1)]), left[k][:], ALU.mult
+                    f[tile][:, m0:m1], h[:].indirect(p2[:, m0 // GROUP : m1 // GROUP]), left[k][:], ALU.mult
                 )
 
         def gain(gains, tile):
             b, t = tile
             return gains[:, b, t : t + 1]
 
+        def z_place(tile):
+            b, t = tile
+            return z_pairs[b][:, t // 2, :, t % 2]
+
         before_quantize = ((0, 2), (0, 1), (1, 1))
 
-        def zs(tile):
-            for m0, m1 in ((0, PAIRS),) if tile in before_quantize else halves:
+        def z_gain(tile):
+            for m0, m1 in ((0, PAIRS),) if tile in before_quantize else HALVES:
                 nc.gpsimd.tensor_scalar(
                     z_place(tile)[:, m0:m1], f[tile][:, m0:m1], gain(gz_sb, tile), 0.0, ALU.mult, ALU.add
                 )
 
-        def zs_last(tile):
-            nc.scalar.activation(z_place(tile), f[tile][:], ACT.Copy, scale=gain(gz_sb, tile))
+        def tile_and_product(tile):
+            product(tile, h_tile(tile))
+            z_gain(tile)
 
-        th_slot = {(0, 0): 0, (0, 2): 1, (0, 1): 0, (0, 3): 2, (1, 2): 1, (1, 0): 0, (1, 1): 1, (1, 3): 0}
-
-        th_place = (24576 + 4096, 24576 + 6144, slot(6))
-
-        def tanh(tile):
-            th[tile] = shared.tile([P, PAIRS], F32, name="th%d%d" % tile, offset=th_place[th_slot[tile]])
+        def tanh(tile, place):
+            th[tile] = shared.tile([P, PAIRS], F32, name="th%d%d" % tile, offset=AT_TANH[place])
             nc.scalar.activation(th[tile][:], f[tile][:], ACT.Tanh)
 
-        def xs(tile):
-            nc.scalar.activation(x_planes[tile[0]][:, tile[1], :], th[tile][:], ACT.Copy, scale=gain(gt_sb, tile))
+        def x_gain(tile):
+            b, t = tile
+            nc.scalar.activation(x_planes[b][:, t, :], th[tile][:], ACT.Copy, scale=gain(gt_sb, tile))
 
-        def weave_planes(grouped, planes, m0, m1):
+        def weave_x(b, m0, m1):
+            run = 4
             nc.vector.tensor_copy(
-                grouped[:, PACK * m0 : PACK * m1].rearrange("p (c i t) -> p c t i", i=4, t=PACK),
-                planes[:, :, m0:m1].rearrange("p t (c i) -> p c t i", i=4),
+                x_bf[b][:, PACK * m0 : PACK * m1].rearrange("p (c i t) -> p c t i", i=run, t=PACK),
+                x_planes[b][:, :, m0:m1].rearrange("p t (c i) -> p c t i", i=run),
             )
 
-        def weave_words(eng, grouped, pairs, m0, m1):
-            word = I32 if eng == "v" else U32
-            dst = grouped[:].bitcast(word).rearrange("p (c i u) -> p c u i", i=2, u=2)[:, m0 // 2 : m1 // 2]
-            src = pairs[:].rearrange("p u m e -> p u (m e)").bitcast(word).rearrange("p u (c i) -> p c u i", i=2)[:, m0 // 2 : m1 // 2]
-            copy_on(eng, dst, src)
+        def weave_z(copy, word, b, m0, m1):
+            dst = z_bf[b][:].bitcast(word).rearrange("p (c i u) -> p c u i", i=2, u=2)
+            src = z_pairs[b][:].rearrange("p u m e -> p u (m e)").bitcast(word).rearrange("p u (c i) -> p c u i", i=2)
+            copy(dst[:, m0 // 2 : m1 // 2], src[:, m0 // 2 : m1 // 2])
 
         w3_bf = {}
 
-        def cast_w3(n, eng):
-            place = w3_place[n]
-            w3_bf[n] = shared.tile([P, 2 * PACK * P], BF16, name="w3_bf%d" % n, align_bytes=64, offset=place)
-            for a in range(2):
-                copy_on(
-                    eng,
-                    w3_bf[n][:].rearrange("p (a c i j) -> p a c j i", a=2, i=2, j=PACK)[:, a],
-                    w3_raw[a][:].rearrange("p j (n c i) -> p n c j i", c=P // 2, i=2)[:, n],
+        def round_w3(n, place):
+            w3_bf[n] = operand_tile("w3_bf%d" % n, 2 * PACK * P, BF16, AT_TANH[place])
+            for b in range(2):
+                nc.scalar.copy(
+                    w3_bf[n][:].rearrange("p (b c i j) -> p b c j i", b=2, i=2, j=PACK)[:, b],
+                    w3_raw[b][:].rearrange("p j (n c i) -> p n c j i", c=P // 2, i=2)[:, n],
                 )
 
         def quantize_w3(n):
-            cols = slice(256 * n, 256 * (n + 1))
+            cols = slice(2 * P * n, 2 * P * (n + 1))
             nc.vector.quantize_mx(out=w3_mx[0][:, cols].bitcast(FP8X4), scales=w3_mx[1][:, cols], in_=w3_bf[n][:])
 
-        y_acc = {}
+        y_banks = {}
 
         def open_y():
             for n in range(N // P):
-                for m0, m1 in halves if n == 0 else ((0, PAIRS),):
-                    y_acc[n, m0, m1] = psum.tile([P, m1 - m0], F32, name="yacc%d_%d" % (n, m0), tag="bank", bufs=8)
+                for m0, m1 in HALVES if n == 0 else ((0, PAIRS),):
+                    y_banks[n, m0, m1] = psum.tile(
+                        [P, m1 - m0], F32, name="y_acc%d_%d" % (n, m0), tag="bank", bufs=BANKS
+                    )
 
         def y_pass(codes, scales, mx, n, start, stop, c0, c1):
-            for (tile, m0, m1), acc in y_acc.items():
+            for (tile, m0, m1), acc in y_banks.items():
                 if tile == n and c0 <= m0 and m1 <= c1:
                     nc.tensor.matmul_mx(
                         out=acc[:],
@@ -312,123 +312,119 @@ def tile_list_friend_triad_scores_kernel(
                         stop=stop,
                     )
 
-        def z_pass(b, start):
+        def z_pass(b):
             for n in range(N // P):
                 codes = w2_w[:, b, 2 * P * n : 2 * P * (n + 1)].bitcast(FP4X4)
-                y_pass(codes, w2_sc[:, b, P * n : P * (n + 1)], z_mx[b], n, start, False, 0, PAIRS)
+                y_pass(codes, w2_sc[:, b, P * n : P * (n + 1)], z_mx[b], n, b == 0, False, 0, PAIRS)
 
-        def x_pass(b, stop, tiles, m0=0, m1=PAIRS):
-            for n in tiles:
-                cols = slice(P * (2 * n + b), P * (2 * n + b + 1))
-                y_pass(w3_mx[0][:, cols].bitcast(FP8X4), w3_mx[1][:, cols], x_mx[b], n, False, stop, m0, m1)
+        def x_pass(b, n, m0=0, m1=PAIRS):
+            cols = slice(P * (2 * n + b), P * (2 * n + b + 1))
+            y_pass(w3_mx[0][:, cols].bitcast(FP8X4), w3_mx[1][:, cols], x_mx[b], n, False, b == 1, m0, m1)
 
         y = {}
         second = {}
 
-        def fetch(n):
-            y[n] = shared.tile([P, PAIRS], F32, name="y%d" % n, offset=2048 * n)
-            for (tile, m0, m1), acc in y_acc.items():
+        def look_up_second(n):
+            y[n] = shared.tile([P, PAIRS], F32, name="y%d" % n, offset=AT_W1_FIRST + 2 * KIB * n)
+            for (tile, m0, m1), acc in y_banks.items():
                 if tile == n:
                     nc.scalar.copy(y[n][:, m0:m1], acc[:])
-            second[n] = shared.tile([P, TRIADS], F32, name="second%d" % n, offset=8192 + 1024 * n)
+            second[n] = shared.tile([P, TRIADS], F32, name="second%d" % n, offset=AT_W1_QUARTER[0] + KIB * n)
             nc.vector.tensor_copy(second[n][:], y[n][:].indirect(p4[:]))
 
         def finish(n):
-            weighted = shared.tile([P, TRIADS], F32, name="weighted%d" % n, offset=32768 + 1024 * n)
+            weighted = shared.tile([P, TRIADS], F32, name="weighted%d" % n, offset=AT_W3[0] + KIB * n)
             nc.scalar.activation(weighted[:], second[n][:], ACT.Copy, scale=gd_sb[:, n : n + 1])
-            res = shared.tile([P, TRIADS], F32, name="res%d" % n, offset=40960 + 1024 * n)
+            res = shared.tile([P, TRIADS], F32, name="res%d" % n, offset=AT_W3[1] + KIB * n)
             nc.vector.tensor_tensor(res[:], y[n][:].indirect(p3[:]), weighted[:], ALU.subtract)
             nc.sync.dma_start(out[P * n : P * (n + 1), :], res[:])
 
-        def tile_pairs(tile):
-            pair(tile, stage1(tile))
-            if tile != (1, 3):
-                zs(tile)
-
-        def x_of(tile):
-            tanh(tile)
-            xs(tile)
-
-        odd = w1_bf[0, "odd"]
-        cast_slots("s", w1_bf[0, 0, 0][:], first_raw[:], 0, 0, P)
-        quantize_w1((0, 0, 0))
+        section = 2 * PACK * P
+        odd0, odd1 = w1_bf["odd"][:, 0:section], w1_bf["odd"][:, section : 2 * section]
+        round_two_slots(nc.scalar.copy, w1_bf["even0"][:], first_raw[:], 0, 0, P)
+        quantize_w1("even0", 0, 2)
         h_pass((0, 0), 0)
         h_pass((0, 2), 0)
-        cast_slots("s", odd[:, 0:1024], first_raw[:], 1, 0, P)
-        cast_slots("s", w1_bf[0, 1, 0][:], quarter_raw[0][:], 0, 0, HALF)
-        cast_slots("s", odd[:, 1024:2048], quarter_raw[0][:], 1, 0, HALF)
-        cast_slots("v", w1_bf[0, 1, 0][:], quarter_raw[1][:], 0, HALF, P, HALF)
-        cast_slots("s", odd[:, 1024:2048], quarter_raw[1][:], 1, HALF, P, HALF)
-        quantize(w1_mx[0, 1, 0], w1_bf[0, 1, 0], 0, P)
-        quantize(w1_mx[0, 1, 0], w1_bf[0, 1, 0], P, 256)
-        quantize_w1((0, "odd"))
-        tile_pairs((0, 0))
-        tile_pairs((0, 2))
-        cast_plain((1, 0), half_raw[0][:], 0, P)
-        quantize_w1((1, 0))
-        cast_plain((1, 1), half_raw[1][:], 0, 16)
-        tile_pairs((0, 1))
-        cast_plain((1, 1), half_raw[1][:], 16, P)
-        quantize_w1((1, 1))
-        tile_pairs((0, 3))
-        tanh((0, 0))
-        tanh((0, 2))
-        xs((0, 0))
-        tile_pairs((1, 0))
-        xs((0, 2))
-        tile_pairs((1, 2))
-        x_of((0, 1))
-        tile_pairs((1, 1))
-        weave_words("s", z_bf[0], z_pairs[0], 0, PAIRS)
-        z_mx[0] = mx_tiles("z0", PAIRS, slot(4))
+        round_two_slots(nc.scalar.copy, odd0, first_raw[:], 1, 0, P)
+        round_two_slots(nc.scalar.copy, w1_bf["even1"][:], quarter_raw[0][:], 0, 0, P // 2)
+        round_two_slots(nc.scalar.copy, odd1, quarter_raw[0][:], 1, 0, P // 2)
+        round_two_slots(nc.vector.tensor_copy, w1_bf["even1"][:], quarter_raw[1][:], 0, P // 2, P, P // 2)
+        round_two_slots(nc.scalar.copy, odd1, quarter_raw[1][:], 1, P // 2, P, P // 2)
+        quantize_w1("even1", 0, 1)
+        quantize_w1("even1", 1, 1)
+        quantize_w1("odd", 0, 4)
+        tile_and_product((0, 0))
+        tile_and_product((0, 2))
+
+        short = 16
+        round_four_slots(0, 0, P)
+        quantize_w1("late0", 0, 4)
+        round_four_slots(1, 0, short)
+        tile_and_product((0, 1))
+        round_four_slots(1, short, P)
+        quantize_w1("late1", 0, 4)
+        tile_and_product((0, 3))
+
+        tanh((0, 0), 0)
+        tanh((0, 2), 1)
+        x_gain((0, 0))
+        tile_and_product((1, 0))
+        x_gain((0, 2))
+        tile_and_product((1, 2))
+        tanh((0, 1), 0)
+        x_gain((0, 1))
+        tile_and_product((1, 1))
+        weave_z(nc.scalar.copy, U32, 0, 0, PAIRS)
+        z_mx[0] = mx_tiles("z0", PAIRS, AT_Z_CODES)
         quantize(z_mx[0], z_bf[0], 0, PAIRS)
-        h_last = stage1((1, 3))
+        h_last = h_tile(LAST)
         open_y()
-        z_pass(0, True)
-        tanh((0, 3))
-        x_of((1, 2))
-        pair((1, 3), h_last)
-        xs((0, 3))
-        tanh((1, 0))
-        tanh((1, 1))
-        xs((1, 0))
-        xs((1, 1))
-        w3_place = (th_place[2], th_place[1], th_place[0], th_place[2])
-        cast_w3(0, "s")
-        zs_last((1, 3))
-        x_of((1, 3))
-        for n in range(1, 4):
-            cast_w3(n, "s")
-        x_bf[0] = shared.tile([P, PACK * PAIRS], BF16, name="x_bf0", align_bytes=64, offset=slot(8))
-        for m0, m1 in halves:
-            weave_planes(x_bf[0], x_planes[0], m0, m1)
-        for m0, m1 in halves:
+        z_pass(0)
+        tanh((0, 3), 2)
+        tanh((1, 2), 1)
+        x_gain((1, 2))
+        product(LAST, h_last)
+        x_gain((0, 3))
+        tanh((1, 0), 0)
+        tanh((1, 1), 1)
+        x_gain((1, 0))
+        x_gain((1, 1))
+        round_w3(0, 2)
+        nc.scalar.activation(z_place(LAST), f[LAST][:], ACT.Copy, scale=gain(gz_sb, LAST))
+        tanh(LAST, 0)
+        x_gain(LAST)
+        for n, place in ((1, 1), (2, 0), (3, 2)):
+            round_w3(n, place)
+
+        x_bf[0] = operand_tile("x_bf0", PACK * PAIRS, BF16, AT_X_WOVEN)
+        for m0, m1 in HALVES:
+            weave_x(0, m0, m1)
+        for m0, m1 in HALVES:
             quantize(x_mx[0], x_bf[0], m0, m1)
         quantize_w3(0)
-        x_pass(0, False, [0])
-        for m0, m1 in halves:
-            weave_words("v", z_bf[1], z_pairs[1], m0, m1)
-        for m0, m1 in halves:
+        x_pass(0, 0)
+        for m0, m1 in HALVES:
+            weave_z(nc.vector.tensor_copy, I32, 1, m0, m1)
+        for m0, m1 in HALVES:
             quantize(z_mx[1], z_bf[1], m0, m1)
-        z_pass(1, False)
-        for m0, m1 in halves:
-            weave_planes(x_bf[1], x_planes[1], m0, m1)
+        z_pass(1)
+        for m0, m1 in HALVES:
+            weave_x(1, m0, m1)
         quantize_w3(1)
-        x_pass(0, False, [1])
-        quantize(x_mx[1], x_bf[1], 0, 256)
-        x_pass(1, True, [0], 0, 256)
-        quantize(x_mx[1], x_bf[1], 256, 512)
-        x_pass(1, True, [0], 256, 512)
-        x_pass(1, True, [1])
-        for n in range(2, 4):
+        x_pass(0, 1)
+        for m0, m1 in HALVES:
+            quantize(x_mx[1], x_bf[1], m0, m1)
+            x_pass(1, 0, m0, m1)
+        x_pass(1, 1)
+        for n in range(2, N // P):
             quantize_w3(n)
-            x_pass(0, False, [n])
-            x_pass(1, True, [n])
-        fetch(0)
-        fetch(1)
+            x_pass(0, n)
+            x_pass(1, n)
+
+        look_up_second(0)
+        look_up_second(1)
         finish(0)
-        fetch(2)
-        fetch(3)
-        finish(1)
-        finish(2)
-        finish(3)
+        look_up_second(2)
+        look_up_second(3)
+        for n in range(1, N // P):
+            finish(n)

@@ -312,6 +312,24 @@ def tile_list_friend_triad_scores_kernel(
                         stop=stop,
                     )
 
+        def first_z_half(k, at):
+            m0, m1 = HALVES[k]
+            mx = mx_tiles("z0_%d" % k, m1 - m0, at)
+            quantize(mx, z_bf[0][:, PACK * m0 : PACK * m1], 0, m1 - m0)
+            if k == 0:
+                open_y()
+            for (n, c0, c1), acc in y_banks.items():
+                if c0 <= m0 and m1 <= c1:
+                    nc.tensor.matmul_mx(
+                        out=acc[:, m0 - c0 : m1 - c0],
+                        lhsT=w2_w[:, 0, 2 * P * n : 2 * P * (n + 1)].bitcast(FP4X4),
+                        lhsT_scale=w2_sc[:, 0, P * n : P * (n + 1)],
+                        rhs=mx[0][:].bitcast(FP8X4),
+                        rhs_scale=mx[1][:],
+                        start=(m0 == c0),
+                        stop=False,
+                    )
+
         def z_pass(b):
             for n in range(N // P):
                 codes = w2_w[:, b, 2 * P * n : 2 * P * (n + 1)].bitcast(FP4X4)
@@ -336,8 +354,11 @@ def tile_list_friend_triad_scores_kernel(
             weighted = shared.tile([P, TRIADS], F32, name="weighted%d" % n, offset=AT_W3[0] + KIB * n)
             nc.scalar.activation(weighted[:], second[n][:], ACT.Copy, scale=gd_sb[:, n : n + 1])
             res = shared.tile([P, TRIADS], F32, name="res%d" % n, offset=AT_W3[1] + KIB * n)
-            nc.vector.tensor_tensor(res[:], y[n][:].indirect(p3[:]), weighted[:], ALU.subtract)
-            nc.sync.dma_start(out[P * n : P * (n + 1), :], res[:])
+            cuts = (0, 3 * TRIADS // 4, TRIADS) if n == N // P - 1 else (0, TRIADS)
+            for q0, q1 in zip(cuts, cuts[1:]):
+                picked = y[n][:].indirect(p3[:, q0 // GROUP : q1 // GROUP])
+                nc.vector.tensor_tensor(res[:, q0:q1], picked, weighted[:, q0:q1], ALU.subtract)
+                nc.sync.dma_start(out[P * n : P * (n + 1), q0:q1], res[:, q0:q1])
 
         section = 2 * PACK * P
         odd0, odd1 = w1_bf["odd"][:, 0:section], w1_bf["odd"][:, section : 2 * section]
@@ -375,11 +396,8 @@ def tile_list_friend_triad_scores_kernel(
         x_gain((0, 1))
         tile_and_product((1, 1))
         weave_z(nc.scalar.copy, U32, 0, 0, PAIRS)
-        z_mx[0] = mx_tiles("z0", PAIRS, AT_Z_CODES)
-        quantize(z_mx[0], z_bf[0], 0, PAIRS)
         h_last = h_tile(LAST)
-        open_y()
-        z_pass(0)
+        first_z_half(0, AT_Z_CODES)
         tanh((0, 3), 2)
         tanh((1, 2), 1)
         x_gain((1, 2))
@@ -396,11 +414,12 @@ def tile_list_friend_triad_scores_kernel(
         for n, place in ((1, 1), (2, 0), (3, 2)):
             round_w3(n, place)
 
-        x_bf[0] = operand_tile("x_bf0", PACK * PAIRS, BF16, AT_X_WOVEN)
+        x_bf[0] = operand_tile("x_bf0", PACK * PAIRS, BF16, AT_X_WOVEN + ALIGN)
         for m0, m1 in HALVES:
             weave_x(0, m0, m1)
         for m0, m1 in HALVES:
             quantize(x_mx[0], x_bf[0], m0, m1)
+        first_z_half(1, AT_X_WOVEN - KIB + ALIGN)
         quantize_w3(0)
         x_pass(0, 0)
         for m0, m1 in HALVES:

@@ -36,6 +36,7 @@ AT_Z_CODES = 56 * KIB
 AT_THIRD_TANH = 60 * KIB
 AT_X_WOVEN = 64 * KIB
 AT_W1_ROUNDED = 68 * KIB
+AT_W3_CODES = 48 * KIB
 AT_TANH = (AT_W1_HALF[1] + 4 * KIB, AT_W1_HALF[1] + 6 * KIB, AT_THIRD_TANH)
 
 
@@ -143,9 +144,12 @@ def tile_list_friend_triad_scores_kernel(
             src = raw.rearrange("p j (w s e) -> p w j s e", s=2, e=2)[:, lo - first : hi - first, :, :, e]
             copy(dst, src)
 
-        def round_four_slots(a, lo, hi):
+        def round_four_slots(a, lo, hi, slots=PACK):
             dst = w1_bf["late%d" % a][:].rearrange("p (t w j) -> p w j t", t=PACK, j=PACK)[:, lo:hi]
-            nc.scalar.copy(dst, half_raw[a][:].rearrange("p j (w t) -> p w j t", t=PACK)[:, lo:hi])
+            src = half_raw[a][:].rearrange("p j (w t) -> p w j t", t=PACK)[:, lo:hi]
+            nc.scalar.copy(dst[:, :, :, 0:slots], src[:, :, :, 0:slots])
+            for t in range(slots, PACK):
+                nc.gpsimd.tensor_scalar(dst[:, :, :, t], src[:, :, :, t], 1.0, 0.0, ALU.mult, ALU.add)
 
         def quantize_w1(unit, first, count):
             quantize(w1_mx[unit], w1_bf[unit], P * first, P * (first + count))
@@ -216,7 +220,7 @@ def tile_list_friend_triad_scores_kernel(
         x_bf = {1: operand_tile("x_bf1", PACK * PAIRS, BF16)}
         z_mx = {1: mx_tiles("z1", PAIRS)}
         x_mx = [mx_tiles("x%d" % b, PAIRS) for b in range(2)]
-        w3_mx = mx_tiles("w3", 2 * N)
+        w3_mx = {}
 
         factor_at = {(1, 2): AT_THIRD_TANH, (1, 1): AT_Z_CODES, (1, 3): AT_X_WOVEN}
 
@@ -287,14 +291,14 @@ def tile_list_friend_triad_scores_kernel(
                 )
 
         def quantize_w3(n):
-            cols = slice(2 * P * n, 2 * P * (n + 1))
-            nc.vector.quantize_mx(out=w3_mx[0][:, cols].bitcast(FP8X4), scales=w3_mx[1][:, cols], in_=w3_bf[n][:])
+            w3_mx[n] = mx_tiles("w3_%d" % n, 2 * P, AT_W3_CODES + KIB * n)
+            quantize(w3_mx[n], w3_bf[n], 0, 2 * P)
 
         y_banks = {}
 
         def open_y():
             for n in range(N // P):
-                for m0, m1 in HALVES if n == 0 else ((0, PAIRS),):
+                for m0, m1 in HALVES if n % 2 == 0 else ((0, PAIRS),):
                     y_banks[n, m0, m1] = psum.tile(
                         [P, m1 - m0], F32, name="y_acc%d_%d" % (n, m0), tag="bank", bufs=BANKS
                     )
@@ -336,8 +340,8 @@ def tile_list_friend_triad_scores_kernel(
                 y_pass(codes, w2_sc[:, b, P * n : P * (n + 1)], z_mx[b], n, b == 0, False, 0, PAIRS)
 
         def x_pass(b, n, m0=0, m1=PAIRS):
-            cols = slice(P * (2 * n + b), P * (2 * n + b + 1))
-            y_pass(w3_mx[0][:, cols].bitcast(FP8X4), w3_mx[1][:, cols], x_mx[b], n, False, b == 1, m0, m1)
+            cols = slice(P * b, P * (b + 1))
+            y_pass(w3_mx[n][0][:, cols].bitcast(FP8X4), w3_mx[n][1][:, cols], x_mx[b], n, False, b == 1, m0, m1)
 
         y = {}
         second = {}
@@ -350,8 +354,10 @@ def tile_list_friend_triad_scores_kernel(
             second[n] = shared.tile([P, TRIADS], F32, name="second%d" % n, offset=AT_W1_QUARTER[0] + KIB * n)
             nc.vector.tensor_copy(second[n][:], y[n][:].indirect(p4[:]))
 
+        weighted_at = (AT_W3_CODES + 2 * KIB, AT_W3_CODES + 3 * KIB, AT_W3[0], AT_W3[0] + KIB)
+
         def finish(n):
-            weighted = shared.tile([P, TRIADS], F32, name="weighted%d" % n, offset=AT_W3[0] + KIB * n)
+            weighted = shared.tile([P, TRIADS], F32, name="weighted%d" % n, offset=weighted_at[n])
             nc.scalar.activation(weighted[:], second[n][:], ACT.Copy, scale=gd_sb[:, n : n + 1])
             res = shared.tile([P, TRIADS], F32, name="res%d" % n, offset=AT_W3[1] + KIB * n)
             cuts = (0, 3 * TRIADS // 4, TRIADS) if n == N // P - 1 else (0, TRIADS)
@@ -374,11 +380,13 @@ def tile_list_friend_triad_scores_kernel(
         quantize_w1("even1", 0, 1)
         quantize_w1("even1", 1, 1)
         quantize_w1("odd", 0, 4)
-        tile_and_product((0, 0))
-        tile_and_product((0, 2))
+        h_first = [h_tile((0, 0)), h_tile((0, 2))]
+        round_four_slots(0, 0, P, PACK - 1)
+        for tile, h in zip(((0, 0), (0, 2)), h_first):
+            product(tile, h)
+            z_gain(tile)
 
         short = 16
-        round_four_slots(0, 0, P)
         quantize_w1("late0", 0, 4)
         round_four_slots(1, 0, short)
         tile_and_product((0, 1))
@@ -389,8 +397,8 @@ def tile_list_friend_triad_scores_kernel(
         tanh((0, 0), 0)
         tanh((0, 2), 1)
         x_gain((0, 0))
-        tile_and_product((1, 0))
         x_gain((0, 2))
+        tile_and_product((1, 0))
         tile_and_product((1, 2))
         tanh((0, 1), 0)
         x_gain((0, 1))
@@ -442,8 +450,8 @@ def tile_list_friend_triad_scores_kernel(
 
         look_up_second(0)
         look_up_second(1)
-        finish(0)
         look_up_second(2)
+        finish(0)
         look_up_second(3)
         for n in range(1, N // P):
             finish(n)

from contextlib import ExitStack

import concourse.mybir as mybir

T, S, PAIRS, TRIADS, K, H, N = 2048, 1024, 512, 256, 1024, 1024, 512
FLOPS = 2 * K * H * S + 2 * 2 * H * N * PAIRS

F32 = mybir.dt.float32
BF16 = mybir.dt.bfloat16
I32 = mybir.dt.int32
U32 = mybir.dt.uint32
U16 = mybir.dt.uint16
U8 = mybir.dt.uint8
FP8X4 = mybir.dt.float8_e4m3fn_x4
FP4X4 = mybir.dt.float4_e2m1fn_x4
ALU = mybir.AluOpType
ACT = mybir.ActivationFunctionType

P = 128
PACK = 4
PASS = P * PACK
BANK = 512
BANKS = 8
QUADRANT = 32
GROUP = 16
ALIGN = 64
HALVES = ((0, PAIRS // 2), (PAIRS // 2, PAIRS))
FIRST, LAST = (0, 0), (1, 3)

KIB = 1024
AT_W1_FIRST = 0
AT_W1_QUARTER = (8 * KIB, 12 * KIB)
AT_W1_HALF = (16 * KIB, 24 * KIB)
AT_W3 = (32 * KIB, 40 * KIB)
AT_Z_CODES = 56 * KIB
AT_THIRD_TANH = 60 * KIB
AT_X_WOVEN = 64 * KIB
AT_W1_ROUNDED = 68 * KIB
AT_W3_CODES = 48 * KIB
AT_TANH = (AT_W1_HALF[1] + 4 * KIB, AT_W1_HALF[1] + 6 * KIB, AT_THIRD_TANH)


def tile_list_friend_triad_scores_kernel(
    tc, tab_words, tab_scales, offs, pos1, pos2, pos3, pos4, w1, w2_words, w2_scales, w3, gz, gt, gd, out
):
    nc = tc.nc
    with ExitStack() as ctx:
        lists = ctx.enter_context(tc.tile_pool(name="lists", bufs=1))
        keep = ctx.enter_context(tc.tile_pool(name="keep", bufs=1))
        ring = ctx.enter_context(tc.tile_pool(name="ring", bufs=2))
        shared = ctx.enter_context(tc.tile_pool(name="shared", bufs=1))
        psum = ctx.enter_context(tc.psum_pool(name="psum", bufs=1))

        def load_list(src, name):
            t = lists.tile([P, src.shape[1]], U16, name=name)
            nc.sync.dma_start(t[:], src)
            return t

        def operand_tile(name, width, dtype, at=None):
            if at is None:
                return keep.tile([P, width], dtype, name=name, align_bytes=ALIGN)
            return shared.tile([P, width], dtype, name=name, align_bytes=ALIGN, offset=at)

        def mx_tiles(name, width, at=None):
            return operand_tile(name + "_codes", width, U32, at), operand_tile(name + "_scales", width, U8)

        def quantize(mx, grouped, c0, c1):
            nc.vector.quantize_mx(
                out=mx[0][:, c0:c1].bitcast(FP8X4), scales=mx[1][:, c0:c1], in_=grouped[:, PACK * c0 : PACK * c1]
            )

        tab_sc = operand_tile("tab_sc", T, U8)
        nc.vector.memset(tab_sc[:].bitcast(I32), 0)
        warm_in = keep.tile([P, 8], F32, name="warm_in")
        nc.vector.memset(warm_in[:], 0.0)
        warm_out = keep.tile([P, 8], F32, name="warm_out")
        nc.scalar.activation(warm_out[:], warm_in[:], ACT.Tanh)
        w2_sc = keep.tile([P, 2, N], U8, name="w2_sc", align_bytes=ALIGN)
        nc.vector.memset(w2_sc[:].rearrange("p a c -> p (a c)").bitcast(I32), 0)

        def load_weights(src, a, c0, c1, name, at):
            raw = shared.tile([P, PACK, c1 - c0], F32, name=name, offset=at)
            nc.sync.dma_start(raw[:], src[PASS * a : PASS * (a + 1), c0:c1].rearrange("(p j) c -> p j c", j=PACK))
            return raw

        def load_table(a):
            t = operand_tile("tab_w%d" % a, T, I32)
            nc.sync.dma_start(t[:], tab_words[a].rearrange("p t i -> p (t i)").bitcast(I32))
            return t

        def load_gain(src, name):
            t = keep.tile([P, 2, PACK], F32, name=name)
            nc.sync.dma_start(t[:], src.rearrange("(b p t) -> p b t", p=P, t=PACK))
            return t

        tab_w = [load_table(0)]
        idx = load_list(offs, "idx")
        p1 = load_list(pos1, "p1")
        for q in range(P // QUADRANT):
            nc.sync.dma_start(
                tab_sc[QUADRANT * q : QUADRANT * q + 2 * PACK, :].bitcast(I32),
                tab_scales[:, PACK * q : PACK * (q + 1), :].bitcast(I32),
            )
        first_raw = load_weights(w1, 0, 0, PASS, "first_raw", AT_W1_FIRST)
        tab_w.append(load_table(1))
        quarter_raw = [
            load_weights(w1, 1, PASS // 2 * u, PASS // 2 * (u + 1), "quarter_raw%d" % u, AT_W1_QUARTER[u])
            for u in range(2)
        ]
        p2 = load_list(pos2, "p2")
        half_raw = [load_weights(w1, 0, PASS, H, "half_raw0", AT_W1_HALF[0])]
        gz_sb = load_gain(gz, "gz_sb")
        gt_sb = load_gain(gt, "gt_sb")
        half_raw.append(load_weights(w1, 1, PASS, H, "half_raw1", AT_W1_HALF[1]))
        w3_raw = [load_weights(w3, b, 0, N, "w3_raw%d" % b, AT_W3[b]) for b in range(2)]
        w2_w = keep.tile([P, 2, 2 * N], U8, name="w2_w", align_bytes=ALIGN)
        nc.sync.dma_start(w2_w[:].bitcast(I32), w2_words.rearrange("a p c -> p a c").bitcast(I32))
        for q in range(P // QUADRANT):
            nc.sync.dma_start(
                w2_sc[QUADRANT * q : QUADRANT * q + PACK, :, :].bitcast(I32),
                w2_scales[:, PACK * q : PACK * (q + 1), :].rearrange("a r c -> r a c").bitcast(I32),
            )
        gd_sb = keep.tile([P, N // P], F32, name="gd_sb")
        with nc.allow_non_contiguous_dma(reason="one weight a partition"):
            nc.sync.dma_start(gd_sb[:], gd.rearrange("(n p) -> p n", p=P))
        p3 = load_list(pos3, "p3")
        p4 = load_list(pos4, "p4")

        w1_bf = {}
        w1_mx = {}

        def w1_unit(unit, stationaries, bf_at=None, codes_at=None):
            w1_bf[unit] = operand_tile(unit + "_bf", PACK * P * stationaries, BF16, bf_at)
            w1_mx[unit] = mx_tiles(unit, P * stationaries, codes_at)

        w1_unit("even0", 2)
        w1_unit("even1", 2, codes_at=AT_W1_ROUNDED)
        w1_unit("odd", 4)
        w1_unit("late0", 4, bf_at=AT_W1_ROUNDED)
        w1_unit("late1", 4)

        def round_two_slots(copy, section, raw, e, lo, hi, first=0):
            dst = section.rearrange("p (s w j) -> p w j s", s=2, j=PACK)[:, lo:hi]
            src = raw.rearrange("p j (w s e) -> p w j s e", s=2, e=2)[:, lo - first : hi - first, :, :, e]
            copy(dst, src)

        def round_four_slots(a, lo, hi, slots=PACK):
            dst = w1_bf["late%d" % a][:].rearrange("p (t w j) -> p w j t", t=PACK, j=PACK)[:, lo:hi]
            src = half_raw[a][:].rearrange("p j (w t) -> p w j t", t=PACK)[:, lo:hi]
            nc.scalar.copy(dst[:, :, :, 0:slots], src[:, :, :, 0:slots])
            for t in range(slots, PACK):
                nc.gpsimd.tensor_scalar(dst[:, :, :, t], src[:, :, :, t], 1.0, 0.0, ALU.mult, ALU.add)

        def quantize_w1(unit, first, count):
            quantize(w1_mx[unit], w1_bf[unit], P * first, P * (first + count))

        def stationary(tile, a):
            b, t = tile
            if b == 1:
                unit, place = "late%d" % a, t
            elif t % 2 == 1:
                unit, place = "odd", 2 * a + t // 2
            else:
                unit, place = "even%d" % a, t // 2
            cols = slice(P * place, P * (place + 1))
            return w1_mx[unit][0][:, cols], w1_mx[unit][1][:, cols]

        got_sc = operand_tile("got_sc", S, U8)
        got_w = []
        for a in range(2):
            got_w.append(operand_tile("got_w%d" % a, S, U32))
            nc.vector.tensor_copy(got_w[a][:], tab_w[a][:].bitcast(U32).indirect(idx[:]))
            if a == 0:
                nc.vector.tensor_copy(got_sc[:], tab_sc[:].indirect(idx[:]))

        h_banks = {}

        def h_width(tile):
            return BANK // 2 if tile == FIRST else BANK

        def h_pass(tile, a):
            width = h_width(tile)
            codes, scales = stationary(tile, a)
            for part in range(S // width):
                if a == 0:
                    h_banks[tile, part] = psum.tile([P, width], F32, name="h_acc", tag="bank", bufs=BANKS)
                cols = slice(width * part, width * (part + 1))
                nc.tensor.matmul_mx(
                    out=h_banks[tile, part][:],
                    lhsT=codes.bitcast(FP8X4),
                    lhsT_scale=scales,
                    rhs=got_w[a][:, cols].bitcast(FP8X4),
                    rhs_scale=got_sc[PACK * a : P, cols],
                    start=(a == 0),
                    stop=(a == 1),
                )

        h_at = {(0, 1): AT_W1_HALF[0], (0, 3): AT_W1_HALF[1]}

        def h_tile(tile):
            if (tile, 0) not in h_banks:
                h_pass(tile, 0)
            h_pass(tile, 1)
            if tile in h_at:
                h = shared.tile([P, S], F32, name="h%d%d" % tile, offset=h_at[tile])
            else:
                h = ring.tile([P, S], F32, name="h", bufs=4)
            width = h_width(tile)
            for part in range(S // width):
                cols = slice(width * part, width * (part + 1))
                copy = nc.vector.tensor_copy if tile == FIRST and part % 2 == 1 else nc.scalar.copy
                copy(h[:, cols], h_banks[tile, part][:])
            return h

        f = {}
        th = {}
        z_pairs = [keep.tile([P, 2, PAIRS, 2], BF16, name="z_pairs%d" % b) for b in range(2)]
        x_planes = [keep.tile([P, PACK, PAIRS], BF16, name="x_planes%d" % b) for b in range(2)]
        z_bf = [operand_tile("z_bf%d" % b, PACK * PAIRS, BF16) for b in range(2)]
        x_bf = {1: operand_tile("x_bf1", PACK * PAIRS, BF16)}
        z_mx = {1: mx_tiles("z1", PAIRS)}
        x_mx = [mx_tiles("x%d" % b, PAIRS) for b in range(2)]
        w3_mx = {}

        factor_at = {(1, 2): AT_THIRD_TANH, (1, 1): AT_Z_CODES, (1, 3): AT_X_WOVEN}

        def product(tile, h):
            width = PAIRS // 2
            if tile in factor_at:
                left = [shared.tile([P, width], F32, name="factor%d%d" % tile, offset=factor_at[tile])]
            else:
                left = [ring.tile([P, width], F32, name="left_a")]
            left.append(ring.tile([P, width], F32, name="left_b"))
            tag = "f%d%d" % ((1, 2) if tile == LAST else tile)
            f[tile] = keep.tile([P, PAIRS], F32, name=tag, tag=tag)
            for k, (m0, m1) in enumerate(HALVES):
                nc.vector.tensor_copy(left[k][:], h[:].indirect(p1[:, m0 // GROUP : m1 // GROUP]))
            for k, (m0, m1) in enumerate(HALVES):
                nc.vector.tensor_tensor(
                    f[tile][:, m0:m1], h[:].indirect(p2[:, m0 // GROUP : m1 // GROUP]), left[k][:], ALU.mult
                )

        def gain(gains, tile):
            b, t = tile
            return gains[:, b, t : t + 1]

        def z_place(tile):
            b, t = tile
            return z_pairs[b][:, t // 2, :, t % 2]

        before_quantize = ((0, 2), (0, 1), (1, 1))

        def z_gain(tile):
            for m0, m1 in ((0, PAIRS),) if tile in before_quantize else HALVES:
                nc.gpsimd.tensor_scalar(
                    z_place(tile)[:, m0:m1], f[tile][:, m0:m1], gain(gz_sb, tile), 0.0, ALU.mult, ALU.add
                )

        def tile_and_product(tile):
            product(tile, h_tile(tile))
            z_gain(tile)

        def tanh(tile, place):
            th[tile] = shared.tile([P, PAIRS], F32, name="th%d%d" % tile, offset=AT_TANH[place])
            nc.scalar.activation(th[tile][:], f[tile][:], ACT.Tanh)

        def x_gain(tile):
            b, t = tile
            nc.scalar.activation(x_planes[b][:, t, :], th[tile][:], ACT.Copy, scale=gain(gt_sb, tile))

        def weave_x(b, m0, m1):
            run = 4
            nc.vector.tensor_copy(
                x_bf[b][:, PACK * m0 : PACK * m1].rearrange("p (c i t) -> p c t i", i=run, t=PACK),
                x_planes[b][:, :, m0:m1].rearrange("p t (c i) -> p c t i", i=run),
            )

        def weave_z(copy, word, b, m0, m1):
            dst = z_bf[b][:].bitcast(word).rearrange("p (c i u) -> p c u i", i=2, u=2)
            src = z_pairs[b][:].rearrange("p u m e -> p u (m e)").bitcast(word).rearrange("p u (c i) -> p c u i", i=2)
            copy(dst[:, m0 // 2 : m1 // 2], src[:, m0 // 2 : m1 // 2])

        w3_bf = {}

        def round_w3(n, place):
            w3_bf[n] = operand_tile("w3_bf%d" % n, 2 * PACK * P, BF16, AT_TANH[place])
            for b in range(2):
                nc.scalar.copy(
                    w3_bf[n][:].rearrange("p (b c i j) -> p b c j i", b=2, i=2, j=PACK)[:, b],
                    w3_raw[b][:].rearrange("p j (n c i) -> p n c j i", c=P // 2, i=2)[:, n],
                )

        def quantize_w3(n):
            w3_mx[n] = mx_tiles("w3_%d" % n, 2 * P, AT_W3_CODES + KIB * n)
            quantize(w3_mx[n], w3_bf[n], 0, 2 * P)

        y_banks = {}

        def open_y():
            for n in range(N // P):
                for m0, m1 in HALVES if n % 2 == 0 else ((0, PAIRS),):
                    y_banks[n, m0, m1] = psum.tile(
                        [P, m1 - m0], F32, name="y_acc%d_%d" % (n, m0), tag="bank", bufs=BANKS
                    )

        def y_pass(codes, scales, mx, n, start, stop, c0, c1):
            for (tile, m0, m1), acc in y_banks.items():
                if tile == n and c0 <= m0 and m1 <= c1:
                    nc.tensor.matmul_mx(
                        out=acc[:],
                        lhsT=codes,
                        lhsT_scale=scales,
                        rhs=mx[0][:, m0:m1].bitcast(FP8X4),
                        rhs_scale=mx[1][:, m0:m1],
                        start=start,
                        stop=stop,
                    )

        def first_z_half(k, at):
            m0, m1 = HALVES[k]
            mx = mx_tiles("z0_%d" % k, m1 - m0, at)
            quantize(mx, z_bf[0][:, PACK * m0 : PACK * m1], 0, m1 - m0)
            if k == 0:
                open_y()
            for (n, c0, c1), acc in y_banks.items():
                if c0 <= m0 and m1 <= c1:
                    nc.tensor.matmul_mx(
                        out=acc[:, m0 - c0 : m1 - c0],
                        lhsT=w2_w[:, 0, 2 * P * n : 2 * P * (n + 1)].bitcast(FP4X4),
                        lhsT_scale=w2_sc[:, 0, P * n : P * (n + 1)],
                        rhs=mx[0][:].bitcast(FP8X4),
                        rhs_scale=mx[1][:],
                        start=(m0 == c0),
                        stop=False,
                    )

        def z_pass(b):
            for n in range(N // P):
                codes = w2_w[:, b, 2 * P * n : 2 * P * (n + 1)].bitcast(FP4X4)
                y_pass(codes, w2_sc[:, b, P * n : P * (n + 1)], z_mx[b], n, b == 0, False, 0, PAIRS)

        def x_pass(b, n, m0=0, m1=PAIRS):
            cols = slice(P * b, P * (b + 1))
            y_pass(w3_mx[n][0][:, cols].bitcast(FP8X4), w3_mx[n][1][:, cols], x_mx[b], n, False, b == 1, m0, m1)

        y = {}
        second = {}

        def look_up_second(n):
            y[n] = shared.tile([P, PAIRS], F32, name="y%d" % n, offset=AT_W1_FIRST + 2 * KIB * n)
            for (tile, m0, m1), acc in y_banks.items():
                if tile == n:
                    nc.scalar.copy(y[n][:, m0:m1], acc[:])
            second[n] = shared.tile([P, TRIADS], F32, name="second%d" % n, offset=AT_W1_QUARTER[0] + KIB * n)
            nc.vector.tensor_copy(second[n][:], y[n][:].indirect(p4[:]))

        weighted_at = (AT_W3_CODES + 2 * KIB, AT_W3_CODES + 3 * KIB, AT_W3[0], AT_W3[0] + KIB)

        def finish(n):
            weighted = shared.tile([P, TRIADS], F32, name="weighted%d" % n, offset=weighted_at[n])
            nc.scalar.activation(weighted[:], second[n][:], ACT.Copy, scale=gd_sb[:, n : n + 1])
            res = shared.tile([P, TRIADS], F32, name="res%d" % n, offset=AT_W3[1] + KIB * n)
            cuts = (0, 3 * TRIADS // 4, TRIADS) if n == N // P - 1 else (0, TRIADS)
            for q0, q1 in zip(cuts, cuts[1:]):
                picked = y[n][:].indirect(p3[:, q0 // GROUP : q1 // GROUP])
                nc.vector.tensor_tensor(res[:, q0:q1], picked, weighted[:, q0:q1], ALU.subtract)
                nc.sync.dma_start(out[P * n : P * (n + 1), q0:q1], res[:, q0:q1])

        section = 2 * PACK * P
        odd0, odd1 = w1_bf["odd"][:, 0:section], w1_bf["odd"][:, section : 2 * section]
        round_two_slots(nc.scalar.copy, w1_bf["even0"][:], first_raw[:], 0, 0, P)
        quantize_w1("even0", 0, 2)
        h_pass((0, 0), 0)
        h_pass((0, 2), 0)
        round_two_slots(nc.scalar.copy, odd0, first_raw[:], 1, 0, P)
        round_two_slots(nc.scalar.copy, w1_bf["even1"][:], quarter_raw[0][:], 0, 0, P // 2)
        round_two_slots(nc.scalar.copy, odd1, quarter_raw[0][:], 1, 0, P // 2)
        round_two_slots(nc.vector.tensor_copy, w1_bf["even1"][:], quarter_raw[1][:], 0, P // 2, P, P // 2)
        round_two_slots(nc.scalar.copy, odd1, quarter_raw[1][:], 1, P // 2, P, P // 2)
        quantize_w1("even1", 0, 1)
        quantize_w1("even1", 1, 1)
        quantize_w1("odd", 0, 4)
        h_first = [h_tile((0, 0)), h_tile((0, 2))]
        round_four_slots(0, 0, P, PACK - 1)
        for tile, h in zip(((0, 0), (0, 2)), h_first):
            product(tile, h)
            z_gain(tile)

        short = 16
        quantize_w1("late0", 0, 4)
        round_four_slots(1, 0, short)
        tile_and_product((0, 1))
        round_four_slots(1, short, P)
        quantize_w1("late1", 0, 4)
        tile_and_product((0, 3))

        tanh((0, 0), 0)
        tanh((0, 2), 1)
        x_gain((0, 0))
        x_gain((0, 2))
        tile_and_product((1, 0))
        tile_and_product((1, 2))
        tanh((0, 1), 0)
        x_gain((0, 1))
        tile_and_product((1, 1))
        weave_z(nc.scalar.copy, U32, 0, 0, PAIRS)
        h_last = h_tile(LAST)
        first_z_half(0, AT_Z_CODES)
        tanh((0, 3), 2)
        tanh((1, 2), 1)
        x_gain((1, 2))
        product(LAST, h_last)
        x_gain((0, 3))
        tanh((1, 0), 0)
        tanh((1, 1), 1)
        x_gain((1, 0))
        x_gain((1, 1))
        round_w3(0, 2)
        nc.scalar.activation(z_place(LAST), f[LAST][:], ACT.Copy, scale=gain(gz_sb, LAST))
        tanh(LAST, 0)
        x_gain(LAST)
        for n, place in ((1, 1), (2, 0), (3, 2)):
            round_w3(n, place)

        x_bf[0] = operand_tile("x_bf0", PACK * PAIRS, BF16, AT_X_WOVEN + ALIGN)
        for m0, m1 in HALVES:
            weave_x(0, m0, m1)
        for m0, m1 in HALVES:
            quantize(x_mx[0], x_bf[0], m0, m1)
        first_z_half(1, AT_X_WOVEN - KIB + ALIGN)
        quantize_w3(0)
        x_pass(0, 0)
        for m0, m1 in HALVES:
            weave_z(nc.vector.tensor_copy, I32, 1, m0, m1)
        for m0, m1 in HALVES:
            quantize(z_mx[1], z_bf[1], m0, m1)
        z_pass(1)
        for m0, m1 in HALVES:
            weave_x(1, m0, m1)
        quantize_w3(1)
        x_pass(0, 1)
        for m0, m1 in HALVES:
            quantize(x_mx[1], x_bf[1], m0, m1)
            x_pass(1, 0, m0, m1)
        x_pass(1, 1)
        for n in range(2, N // P):
            quantize_w3(n)
            x_pass(0, n)
            x_pass(1, n)

        look_up_second(0)
        look_up_second(1)
        look_up_second(2)
        finish(0)
        look_up_second(3)
        for n in range(1, N // P):
            finish(n)
